import numpy as np
import ml_dtypes


def mxq(x, axis, fmt="e4m3"):
    dtype, down = {"e4m3": (ml_dtypes.float8_e4m3fn, 7), "e5m2": (ml_dtypes.float8_e5m2, 14)}[fmt]
    v = np.moveaxis(np.asarray(x, np.float32).astype(ml_dtypes.bfloat16).astype(np.float64), axis, -1)
    blocks = v.reshape(v.shape[:-1] + (-1, 32))
    amax = np.abs(blocks).max(-1, keepdims=True)
    byte = np.maximum(np.where(amax > 0, np.frexp(amax)[1] - 1 + 127, 0) - down, 1)
    scale = np.exp2(byte - 127.0)
    codes = (blocks / scale).astype(np.float32).astype(dtype).astype(np.float64)
    return np.moveaxis((codes * scale).reshape(v.shape), -1, axis)


WIDE = False


def mx_kscale(k):
    if not WIDE:
        return np.ones(k)
    levels = np.array([10, -10, 5, -5, 0])
    if k % 512:
        return np.exp2(np.random.permutation(np.resize(levels, k // 32))).repeat(32)
    a = np.empty((k // 512, 16))
    for p in range(k // 512):
        a[p, :8] = np.random.permutation(np.resize(levels, 8))
        for g in range(8):
            far = levels[np.abs(levels - a[p, g]) >= 10]
            a[p, g + 8] = far[np.random.randint(len(far))]
    return np.exp2(a.ravel()).repeat(32)


def f64(x):
    return np.asarray(x).astype(np.float64)


def striped(idx):
    return np.tile(idx.reshape(-1, 16).T, (8, 1)).astype(np.uint16)


def unstriped(offs):
    return offs[:16].T.reshape(-1).astype(np.int64)


E2M1 = np.array([0.0, 0.5, 1.0, 1.5, 2.0, 3.0, 4.0, 6.0, -0.0, -0.5, -1.0, -1.5, -2.0, -3.0, -4.0, -6.0])


def pack_weight(w, fmt):
    k, n = w.shape
    w = f64(np.asarray(w, np.float32).astype(ml_dtypes.bfloat16)).reshape(k // 32, 32, n)
    amax = np.abs(w).max(1)
    if fmt == "e4m3":
        byte = np.frexp(amax)[1] - 1 + 127 - 7
    else:
        mant, ex = np.frexp(amax / 6.0)
        byte = np.where(mant > 0.5, ex, ex - 1) + 127
    byte = np.clip(np.where(amax > 0, byte, 1), 1, 254)
    scaled = (w * np.exp2(127.0 - byte)[:, None, :]).reshape(k, n).astype(np.float32)
    by_word = np.ascontiguousarray(scaled.reshape(k // 512, 128, 4, n).transpose(0, 1, 3, 2))
    if fmt == "e4m3":
        words = by_word.astype(ml_dtypes.float8_e4m3fn).view(np.uint8)
    else:
        c = by_word.astype(ml_dtypes.float4_e2m1fn).view(np.uint8) & 0xF
        words = (c[..., 0::2] | (c[..., 1::2] << 4)).reshape(k // 512, 128, 2 * n)
    return np.ascontiguousarray(words), np.ascontiguousarray(byte.astype(np.uint8).reshape(k // 512, 16, n))


def unpack_weight(words, scales, fmt):
    g, _, n = scales.shape
    words = np.ascontiguousarray(words).reshape(g, 128, n, -1)
    if fmt == "e4m3":
        vals = words.view(ml_dtypes.float8_e4m3fn).astype(np.float64)
    else:
        nib = np.empty((g, 128, n, 4), np.uint8)
        nib[..., 0::2] = words & 0xF
        nib[..., 1::2] = words >> 4
        vals = E2M1[nib]
    vals = vals * np.repeat(np.exp2(scales.astype(np.float64) - 127.0), 8, axis=1)[..., None]
    return vals.transpose(0, 1, 3, 2).reshape(g * 512, n)


def gelu(v):
    return 0.5 * v * (1.0 + np.tanh(np.sqrt(2.0 / np.pi) * (v + 0.044715 * v**3)))


def bf(x):
    return np.asarray(x, np.float32).astype(ml_dtypes.bfloat16)


def planes(Y):
    n, m = Y.shape
    b = f64(bf(Y)).reshape(n // 32, 32, m)
    amax = np.abs(b).max(1)
    byte = np.clip(np.where(amax > 0, np.frexp(amax)[1] - 1 + 127 - 7, 1), 1, 254)
    codes = (b * np.exp2(127.0 - byte)[:, None, :]).reshape(n, m).astype(np.float32).astype(ml_dtypes.float8_e4m3fn).view(np.uint8)
    words = codes.reshape(n // 512, 128, 4, m).transpose(0, 1, 3, 2)
    return np.ascontiguousarray(words), np.ascontiguousarray(byte.astype(np.uint8).reshape(n // 512, 16, m))


K, H, N, T, S, T2, P = 1024, 512, 1024, 2048, 1024, 2048, 1024

def setup_inputs():
    n = np.random.standard_normal
    s = mx_kscale(K)[:, None]
    u = mx_kscale(H)[:, None]
    d = {}
    d["tab_words"], d["tab_scales"] = pack_weight(n((K, T)) * s, "e4m3")
    d["offs"] = striped(np.random.permutation(T)[:S])
    d["w1"] = (n((K, H)) / np.sqrt(K) / s * u.T).astype(np.float32)
    d["page0"] = (n((H, T2)) * u).astype(np.float32)
    d["wgs"] = np.exp(0.3 * n((128, S))).astype(np.float32)
    d["offs2"] = striped(np.random.permutation(T2)[:S])
    d["offs3"] = striped(np.random.permutation(T2)[:P])
    d["wg_words"], d["wg_scales"] = pack_weight(n((H, H)) / np.sqrt(H) / u, "e2m1")
    d["wc"] = (n((H, H)) / np.sqrt(H) / u).astype(np.float32)
    d["gain"] = (np.exp(0.3 * n(H)) * u[:, 0]).astype(np.float32)
    d["wo_words"], d["wo_scales"] = pack_weight(n((H, N)) / np.sqrt(H) / u * np.exp(0.8 * n(N)), "e4m3")
    return d

def reference(tab_words, tab_scales, offs, w1, page0, wgs, offs2, offs3,
              wg_words, wg_scales, wc, gain, wo_words, wo_scales):
    v = unpack_weight(tab_words, tab_scales, "e4m3")[:, unstriped(offs)]
    h = mxq(f64(w1), 0, "e4m3").T @ v
    page = f64(page0).copy()
    page[:, unstriped(offs2)] = np.tile(f64(wgs), (H // 128, 1)) * h
    x = page[:, unstriped(offs3)]
    xq = mxq(x, 0, "e4m3")
    wg = unpack_weight(wg_words, wg_scales, "e2m1")
    g = 1.0 / (1.0 + np.exp(-(wg.T @ xq)))
    c = np.tanh(mxq(f64(wc), 0, "e4m3").T @ xq) * f64(gain)[:, None]
    z = x + g * (c - x)
    wo = unpack_weight(wo_words, wo_scales, "e4m3")
    y = wo.T @ mxq(z, 0, "e4m3")
    words, scales = planes(y)
    return y, words, scales

@@ -1,0 +1,284 @@
+from contextlib import ExitStack
+
+import concourse.mybir as mybir
+
+K, H, N, T, S, T2, M = 1024, 512, 1024, 2048, 1024, 2048, 1024
+FLOPS = 2 * (K * H * S + 2 * H * H * M + H * N * M)
+
+F32 = mybir.dt.float32
+BF16 = mybir.dt.bfloat16
+I32 = mybir.dt.int32
+U32 = mybir.dt.uint32
+U16 = mybir.dt.uint16
+U8 = mybir.dt.uint8
+FP8X4 = mybir.dt.float8_e4m3fn_x4
+FP4X4 = mybir.dt.float4_e2m1fn_x4
+ALU = mybir.AluOpType
+ACT = mybir.ActivationFunctionType
+
+P = 128
+PACK = 4
+KP = P * PACK
+BANK = 512
+LIST = 16
+GATHER = 256
+CHUNKS = (256, 256, 256, 128, 128)
+
+
+def tile_list_household_profile_cells_kernel(
+    tc, tab_words, tab_scales, offs, w1, page0, wgs, offs2, offs3,
+    wg_words, wg_scales, wc, gain, wo_words, wo_scales, out_0, out_1, out_2,
+):
+    nc = tc.nc
+    passes = K // KP
+    groups = N // KP
+
+    with ExitStack() as ctx:
+        keep = ctx.enter_context(tc.tile_pool(name="keep", bufs=1))
+        ring = ctx.enter_context(tc.tile_pool(name="ring", bufs=2))
+        psum = ctx.enter_context(tc.psum_pool(name="psum", bufs=2))
+
+        def kept(shape, dtype, name):
+            return keep.tile(shape, dtype, name=name, align_bytes=64)
+
+        def big(shape, name):
+            return ring.tile(shape, F32, name=name, tag="big", bufs=4, align_bytes=64)
+
+        def entries(offsets, lo, hi):
+            return offsets[:, lo // LIST : hi // LIST]
+
+        idx = keep.tile([P, S // LIST], U16, name="idx")
+        idx2 = keep.tile([P, S // LIST], U16, name="idx2")
+        idx3 = keep.tile([P, M // LIST], U16, name="idx3")
+
+        tab_sc = kept([P, T], U8, "tab_sc")
+        nc.vector.memset(tab_sc[:].bitcast(I32), 0)
+        wg_sc_raw = kept([P, H], U8, "wg_sc_raw")
+        nc.vector.memset(wg_sc_raw[:].bitcast(I32), 0)
+        wo_sc_raw = kept([P, N], U8, "wo_sc_raw")
+        nc.vector.memset(wo_sc_raw[:].bitcast(I32), 0)
+        warm_in = kept([P, 1], F32, "warm_in")
+        warm_out = kept([P, 1], F32, "warm_out")
+        nc.vector.memset(warm_in[:], 0.0)
+        nc.scalar.activation(out=warm_out[:], in_=warm_in[:], func=ACT.Sigmoid)
+
+        nc.sync.dma_start(idx[:], offs)
+        w1_raw = []
+        for a in range(passes):
+            raw = big([P, PACK, H], "w1_raw%d" % a)
+            nc.sync.dma_start(out=raw[:], in_=w1[a * KP : (a + 1) * KP, :].rearrange("(p j) c -> p j c", j=PACK))
+            w1_raw.append(raw)
+            if a == 0:
+                for q in range(4):
+                    nc.sync.dma_start(
+                        out=tab_sc[32 * q : 32 * q + 4 * passes, :].bitcast(I32),
+                        in_=tab_scales[:, 4 * q : 4 * q + 4, :].bitcast(I32),
+                    )
+        tab_w = []
+        for a in range(passes):
+            words = kept([P, T], I32, "tab_w%d" % a)
+            nc.sync.dma_start(out=words[:], in_=tab_words[a].rearrange("p t i -> p (t i)").bitcast(I32))
+            tab_w.append(words)
+        page_rows = page0.rearrange("(p t) c -> p t c", t=PACK)
+        wgs_rows = wgs.rearrange("(i t) j -> i t j", t=PACK)
+        page, wgs_sb = [], {}
+
+        def load_page(t):
+            tile = kept([P, T2], F32, "page%d" % t)
+            nc.sync.dma_start(out=tile[:], in_=page_rows[:, t, :])
+            page.append(tile)
+
+        def load_wgs(t, lo, hi):
+            tile = kept([P, hi - lo], F32, "wgs%d_%d" % (t, lo))
+            for q in (0, 2, 1, 3):
+                nc.sync.dma_start(out=tile[32 * q : 32 * (q + 1), :], in_=wgs_rows[:, t, lo:hi])
+            wgs_sb[t, lo] = tile
+
+        cuts = [((0, BANK), (BANK, S))] + [((0, S),)] * (PACK - 1)
+        load_page(0)
+        nc.sync.dma_start(idx2[:], offs2)
+        for lo, hi in cuts[0]:
+            load_wgs(0, lo, hi)
+        nc.sync.dma_start(idx3[:], offs3)
+        load_page(1)
+        load_wgs(1, 0, S)
+        wc_raw = big([P, PACK, H], "wc_raw")
+        nc.sync.dma_start(out=wc_raw[:], in_=wc.rearrange("(p j) c -> p j c", j=PACK))
+        gain_sb = kept([P, PACK], F32, "gain_sb")
+        nc.sync.dma_start(out=gain_sb[:], in_=gain.rearrange("(p t) -> p t", t=PACK))
+        wg_raw = kept([P, 2 * H], U8, "wg_raw")
+        nc.sync.dma_start(out=wg_raw[:].bitcast(I32), in_=wg_words[0].bitcast(I32))
+
+        def load_scales(raw, scales):
+            for q in range(4):
+                nc.sync.dma_start(
+                    out=raw[32 * q : 32 * q + 4, :].bitcast(I32), in_=scales[0, 4 * q : 4 * q + 4, :].bitcast(I32)
+                )
+
+        load_scales(wg_sc_raw, wg_scales)
+        load_page(2)
+        load_wgs(2, 0, S)
+        load_page(3)
+        load_wgs(3, 0, S)
+        wo_raw = kept([P, N], I32, "wo_raw")
+        nc.sync.dma_start(out=wo_raw[:], in_=wo_words[0].rearrange("p n i -> p (n i)").bitcast(I32))
+        load_scales(wo_sc_raw, wo_scales)
+
+        def quantize_weight(raw, name):
+            dealt = ring.tile([P, PACK * H], BF16, name=name + "_bf", tag="dealt", align_bytes=64)
+            nc.scalar.copy(
+                out=dealt[:].rearrange("p (t m j) -> p m j t", t=PACK, j=PACK),
+                in_=raw[:].rearrange("p j (m t) -> p m j t", t=PACK),
+            )
+            codes = kept([P, H], U32, name + "_q")
+            scales = kept([P, H], U8, name + "_s")
+            nc.vector.quantize_mx(out=codes[:].bitcast(FP8X4), scales=scales[:], in_=dealt[:])
+            return codes, scales
+
+        v_sc = kept([P, S], U8, "v_sc")
+        nc.vector.tensor_copy(out=v_sc[:], in_=tab_sc[:].indirect(idx[:]))
+        w1_q = [quantize_weight(w1_raw[a], "w1_%d" % a) for a in range(passes)]
+        v_w = {}
+        for a in range(passes):
+            for lo in range(0, S, BANK):
+                tile = kept([P, BANK], U32, "v_w%d_%d" % (a, lo))
+                nc.vector.tensor_copy(out=tile[:], in_=tab_w[a][:].bitcast(U32).indirect(entries(idx, lo, lo + BANK)))
+                v_w[a, lo] = tile
+
+        x = kept([P, PACK, M], F32, "x")
+        starts = [sum(CHUNKS[:i]) for i in range(len(CHUNKS))]
+        x_bf = [kept([P, c, PACK], BF16, "x_bf%d" % i) for i, c in enumerate(CHUNKS)]
+
+        def round_planes(i, t0, t1):
+            lo, c = starts[i], CHUNKS[i]
+            nc.scalar.copy(
+                out=x_bf[i][:, :, t0:t1],
+                in_=x[:, t0:t1, lo : lo + c].rearrange("p t n -> p n t"),
+            )
+
+        for t in range(PACK):
+            cols = slice(t * P, (t + 1) * P)
+            for lo, hi in cuts[t]:
+                h = ring.tile([P, hi - lo], F32, name="h", tag="h", bufs=3, align_bytes=64)
+                for b in range(lo, hi, BANK):
+                    acc = psum.tile([P, BANK], F32, name="acc_h", tag="y", bufs=4)
+                    for a in range(passes):
+                        nc.tensor.matmul_mx(
+                            out=acc[:],
+                            lhsT=w1_q[a][0][:, cols].bitcast(FP8X4),
+                            lhsT_scale=w1_q[a][1][:, cols],
+                            rhs=v_w[a, b][:].bitcast(FP8X4),
+                            rhs_scale=v_sc[4 * a : P, b : b + BANK],
+                            start=(a == 0),
+                            stop=(a == passes - 1),
+                        )
+                    nc.scalar.copy(out=h[:, b - lo : b - lo + BANK], in_=acc[:])
+                nc.vector.tensor_tensor(
+                    out=page[t][:].indirect(entries(idx2, lo, hi)), in0=h[:], in1=wgs_sb[t, lo][:], op=ALU.mult
+                )
+            step = M if t < PACK - 1 else GATHER
+            for lo in range(0, M, step):
+                nc.vector.tensor_copy(out=x[:, t, lo : lo + step], in_=page[t][:].indirect(entries(idx3, lo, lo + step)))
+            if t == PACK - 2:
+                for i in range(len(CHUNKS)):
+                    round_planes(i, 0, PACK - 1)
+
+        wc_q, wc_s = quantize_weight(wc_raw, "wc")
+        wg_q = kept([P, 2 * H], U8, "wg_q")
+        nc.vector.tensor_copy(
+            out=wg_q[:].rearrange("p (t m b) -> p m t b", t=PACK, b=2),
+            in_=wg_raw[:].rearrange("p (m t b) -> p m t b", t=PACK, b=2),
+        )
+
+        def deal(raw, dtype, name):
+            dealt = kept([P, raw.shape[1]], dtype, name)
+            nc.vector.tensor_copy(
+                out=dealt[:].rearrange("p (g t m) -> p g m t", t=PACK, m=P),
+                in_=raw[:].rearrange("p (g m t) -> p g m t", t=PACK, m=P),
+            )
+            return dealt
+
+        wg_s = deal(wg_sc_raw, U8, "wg_s")
+        wo_q = deal(wo_raw, I32, "wo_q")
+        wo_s = deal(wo_sc_raw, U8, "wo_s")
+
+        y_sc = kept([P, groups, M], U8, "y_sc")
+        y_rows = out_0.rearrange("(g p t) m -> g p t m", p=P, t=PACK)
+        y_words = out_1.rearrange("g p m t -> p g (m t)").bitcast(I32)
+
+        def product(tag, bufs, count, c, lhs, rhs, rhs_scale):
+            per_bank = BANK // c
+            banks = []
+            for first in range(0, count, per_bank):
+                acc = psum.tile([P, BANK], F32, name="acc_" + tag, tag=tag, bufs=bufs)
+                for s in range(per_bank):
+                    codes, scales = lhs(first + s)
+                    nc.tensor.matmul_mx(
+                        out=acc[:, s * c : (s + 1) * c], lhsT=codes, lhsT_scale=scales,
+                        rhs=rhs, rhs_scale=rhs_scale, start=True, stop=True,
+                    )
+                banks.append(acc)
+            return banks
+
+        def gate_lhs(t):
+            return wg_q[:, 2 * t * P : 2 * (t + 1) * P].bitcast(FP4X4), wg_s[:, t * P : (t + 1) * P]
+
+        def cand_lhs(t):
+            return wc_q[:, t * P : (t + 1) * P].bitcast(FP8X4), wc_s[:, t * P : (t + 1) * P]
+
+        def out_lhs(s):
+            return wo_q[:, s * P : (s + 1) * P].bitcast(FP8X4), wo_s[:, s * P : (s + 1) * P]
+
+        for i, c in enumerate(CHUNKS):
+            lo = starts[i]
+            cols = slice(lo, lo + c)
+            round_planes(i, PACK - 1, PACK)
+            x_q = kept([P, c], U32, "x_q%d" % i)
+            x_s = kept([P, c], U8, "x_s%d" % i)
+            nc.vector.quantize_mx(out=x_q[:].bitcast(FP8X4), scales=x_s[:], in_=x_bf[i][:].rearrange("p n t -> p (n t)"))
+
+            cand = ring.tile([P, PACK * c], F32, name="cand", align_bytes=64)
+            for b, acc in enumerate(product("c", 2, PACK, c, cand_lhs, x_q[:].bitcast(FP8X4), x_s[:])):
+                nc.scalar.activation(out=cand[:, b * BANK : (b + 1) * BANK], in_=acc[:], func=ACT.Tanh)
+            gate = ring.tile([P, PACK * c], F32, name="gate", align_bytes=64)
+            for b, acc in enumerate(product("g", 2, PACK, c, gate_lhs, x_q[:].bitcast(FP8X4), x_s[:])):
+                nc.scalar.activation(out=gate[:, b * BANK : (b + 1) * BANK], in_=acc[:], func=ACT.Sigmoid)
+
+            for t in range(PACK):
+                part = cand[:, t * c : (t + 1) * c]
+                nc.vector.scalar_tensor_tensor(
+                    out=part, in0=part, scalar=gain_sb[:, t : t + 1], in1=x[:, t, cols], op0=ALU.mult, op1=ALU.subtract
+                )
+            nc.vector.tensor_tensor(out=cand[:], in0=cand[:], in1=gate[:], op=ALU.mult)
+            z_bf = ring.tile([P, PACK * c], BF16, name="z_bf", align_bytes=64)
+            nc.vector.tensor_tensor(
+                out=z_bf[:].rearrange("p (n i t) -> p n t i", i=4, t=PACK),
+                in0=cand[:].rearrange("p (t n i) -> p n t i", i=4, t=PACK),
+                in1=x[:, :, cols].rearrange("p t (n i) -> p n t i", i=4),
+                op=ALU.add,
+            )
+            z_q = ring.tile([P, c], U32, name="z_q", align_bytes=64)
+            z_s = ring.tile([P, c], U8, name="z_s", align_bytes=64)
+            nc.vector.quantize_mx(out=z_q[:].bitcast(FP8X4), scales=z_s[:], in_=z_bf[:])
+
+            y = big([P, groups * PACK * c], "y")
+            for b, acc in enumerate(product("y", 4, groups * PACK, c, out_lhs, z_q[:].bitcast(FP8X4), z_s[:])):
+                nc.scalar.copy(out=y[:, b * BANK : (b + 1) * BANK], in_=acc[:])
+            y_q = ring.tile([P, groups, c], I32, name="y_q", bufs=3, align_bytes=64)
+            for g in range(groups):
+                y_g = y[:, g * PACK * c : (g + 1) * PACK * c]
+                nc.sync.dma_start(out=y_rows[g][:, :, cols], in_=y_g.rearrange("p (t n) -> p t n", t=PACK))
+                y_bf = ring.tile([P, PACK * c], BF16, name="y_bf", bufs=3, align_bytes=64)
+                rounder = nc.scalar.copy if (g == 1 and i < 2) else nc.vector.tensor_copy
+                rounder(
+                    out=y_bf[:].rearrange("p (n i t) -> p n t i", i=4, t=PACK),
+                    in_=y_g.rearrange("p (t n i) -> p n t i", i=4, t=PACK),
+                )
+                nc.vector.quantize_mx(out=y_q[:, g, :].bitcast(FP8X4), scales=y_sc[:, g, cols], in_=y_bf[:])
+            nc.sync.dma_start(out=y_words[:, :, cols], in_=y_q[:])
+
+        for q in range(4):
+            nc.sync.dma_start(
+                out=out_2[:, 4 * q : 4 * q + 4, :].rearrange("g r m -> r g m").bitcast(I32),
+                in_=y_sc[32 * q : 32 * q + 4, :, :].bitcast(I32),
+            )

@@ -19,10 +19,13 @@ ACT = mybir.ActivationFunctionType
 P = 128
 PACK = 4
 KP = P * PACK
+QUAD = 32
 BANK = 512
 LIST = 16
-GATHER = 256
+LINE = 4
+FETCH = 256
 CHUNKS = (256, 256, 256, 128, 128)
+ROUND_ON_SCALAR = ((0, 0), (0, 1), (1, 0), (1, 1), (2, 0), (2, 1), (4, 0))
 
 
 def tile_list_household_profile_cells_kernel(
@@ -32,17 +35,15 @@ def tile_list_household_profile_cells_kernel(
     nc = tc.nc
     passes = K // KP
     groups = N // KP
+    blocks = H // P
 
     with ExitStack() as ctx:
         keep = ctx.enter_context(tc.tile_pool(name="keep", bufs=1))
         ring = ctx.enter_context(tc.tile_pool(name="ring", bufs=2))
         psum = ctx.enter_context(tc.psum_pool(name="psum", bufs=2))
 
-        def kept(shape, dtype, name):
-            return keep.tile(shape, dtype, name=name, align_bytes=64)
-
-        def big(shape, name):
-            return ring.tile(shape, F32, name=name, tag="big", bufs=4, align_bytes=64)
+        def kept(shape, dtype, name, tag=""):
+            return keep.tile(shape, dtype, name=name, tag=tag or name, align_bytes=64)
 
         def entries(offsets, lo, hi):
             return offsets[:, lo // LIST : hi // LIST]
@@ -51,93 +52,90 @@ def tile_list_household_profile_cells_kernel(
         idx2 = keep.tile([P, S // LIST], U16, name="idx2")
         idx3 = keep.tile([P, M // LIST], U16, name="idx3")
 
-        tab_sc = kept([P, T], U8, "tab_sc")
-        nc.vector.memset(tab_sc[:].bitcast(I32), 0)
-        wg_sc_raw = kept([P, H], U8, "wg_sc_raw")
-        nc.vector.memset(wg_sc_raw[:].bitcast(I32), 0)
-        wo_sc_raw = kept([P, N], U8, "wo_sc_raw")
-        nc.vector.memset(wo_sc_raw[:].bitcast(I32), 0)
+        def zeroed_plane(width, name):
+            plane = kept([P, width], U8, name)
+            nc.vector.memset(plane[:].bitcast(I32), 0)
+            return plane
+
+        def load_scales(plane, scales):
+            rows = 4 * scales.shape[0]
+            for q in range(P // QUAD):
+                nc.sync.dma_start(
+                    out=plane[QUAD * q : QUAD * q + rows, :].bitcast(I32),
+                    in_=scales[:, 4 * q : 4 * q + 4, :].bitcast(I32),
+                )
+
+        tab_sc = zeroed_plane(T, "tab_sc")
+        wg_sc_raw = zeroed_plane(H, "wg_sc_raw")
+        wo_sc_raw = zeroed_plane(N, "wo_sc_raw")
         warm_in = kept([P, 1], F32, "warm_in")
         warm_out = kept([P, 1], F32, "warm_out")
         nc.vector.memset(warm_in[:], 0.0)
         nc.scalar.activation(out=warm_out[:], in_=warm_in[:], func=ACT.Sigmoid)
 
-        nc.sync.dma_start(idx[:], offs)
         w1_raw = []
-        for a in range(passes):
-            raw = big([P, PACK, H], "w1_raw%d" % a)
-            nc.sync.dma_start(out=raw[:], in_=w1[a * KP : (a + 1) * KP, :].rearrange("(p j) c -> p j c", j=PACK))
+
+        def load_w1(b):
+            raw = kept([P, passes, PACK, P], F32, "w1_raw%d" % b)
+            for a in range(passes):
+                rows = w1[a * KP : (a + 1) * KP, b * P : (b + 1) * P]
+                nc.sync.dma_start(out=raw[:, a, :, :], in_=rows.rearrange("(p j) c -> p j c", j=PACK))
             w1_raw.append(raw)
-            if a == 0:
-                for q in range(4):
-                    nc.sync.dma_start(
-                        out=tab_sc[32 * q : 32 * q + 4 * passes, :].bitcast(I32),
-                        in_=tab_scales[:, 4 * q : 4 * q + 4, :].bitcast(I32),
-                    )
-        tab_w = []
-        for a in range(passes):
-            words = kept([P, T], I32, "tab_w%d" % a)
-            nc.sync.dma_start(out=words[:], in_=tab_words[a].rearrange("p t i -> p (t i)").bitcast(I32))
-            tab_w.append(words)
-        page_rows = page0.rearrange("(p t) c -> p t c", t=PACK)
-        wgs_rows = wgs.rearrange("(i t) j -> i t j", t=PACK)
-        page, wgs_sb = [], {}
 
-        def load_page(t):
-            tile = kept([P, T2], F32, "page%d" % t)
-            nc.sync.dma_start(out=tile[:], in_=page_rows[:, t, :])
-            page.append(tile)
+        def load_words(words, name):
+            tile = kept([P, words.shape[1]], I32, name)
+            nc.sync.dma_start(out=tile[:], in_=words.rearrange("p c i -> p (c i)").bitcast(I32))
+            return tile
 
-        def load_wgs(t, lo, hi):
-            tile = kept([P, hi - lo], F32, "wgs%d_%d" % (t, lo))
-            for q in (0, 2, 1, 3):
-                nc.sync.dma_start(out=tile[32 * q : 32 * (q + 1), :], in_=wgs_rows[:, t, lo:hi])
-            wgs_sb[t, lo] = tile
+        def load_rows(rows, name):
+            tile = kept([P, rows.shape[1]], F32, name)
+            nc.sync.dma_start(out=tile[:], in_=rows)
+            return tile
 
-        cuts = [((0, BANK), (BANK, S))] + [((0, S),)] * (PACK - 1)
-        load_page(0)
+        tab_w = [load_words(tab_words[0], "tab_w0")]
+        load_scales(tab_sc, tab_scales)
+        nc.sync.dma_start(idx[:], offs)
+        load_w1(0)
+        tab_w.append(load_words(tab_words[1], "tab_w1"))
+        page = [load_rows(page0[0:P, :], "page0")]
         nc.sync.dma_start(idx2[:], offs2)
-        for lo, hi in cuts[0]:
-            load_wgs(0, lo, hi)
+        wgs_sb = kept([P, S], F32, "wgs")
+        nc.sync.dma_start(out=wgs_sb[:, 0:BANK], in_=wgs[:, 0:BANK])
+        load_w1(1)
+        load_w1(2)
+        nc.sync.dma_start(out=wgs_sb[:, BANK:S], in_=wgs[:, BANK:S])
+        page.append(load_rows(page0[P : 2 * P, :], "page1"))
+        load_w1(3)
+        for b in range(2, blocks):
+            page.append(load_rows(page0[b * P : (b + 1) * P, :], "page%d" % b))
         nc.sync.dma_start(idx3[:], offs3)
-        load_page(1)
-        load_wgs(1, 0, S)
-        wc_raw = big([P, PACK, H], "wc_raw")
+        wc_raw = kept([P, PACK, H], F32, "wc_raw")
         nc.sync.dma_start(out=wc_raw[:], in_=wc.rearrange("(p j) c -> p j c", j=PACK))
-        gain_sb = kept([P, PACK], F32, "gain_sb")
-        nc.sync.dma_start(out=gain_sb[:], in_=gain.rearrange("(p t) -> p t", t=PACK))
         wg_raw = kept([P, 2 * H], U8, "wg_raw")
         nc.sync.dma_start(out=wg_raw[:].bitcast(I32), in_=wg_words[0].bitcast(I32))
-
-        def load_scales(raw, scales):
-            for q in range(4):
-                nc.sync.dma_start(
-                    out=raw[32 * q : 32 * q + 4, :].bitcast(I32), in_=scales[0, 4 * q : 4 * q + 4, :].bitcast(I32)
-                )
-
         load_scales(wg_sc_raw, wg_scales)
-        load_page(2)
-        load_wgs(2, 0, S)
-        load_page(3)
-        load_wgs(3, 0, S)
-        wo_raw = kept([P, N], I32, "wo_raw")
-        nc.sync.dma_start(out=wo_raw[:], in_=wo_words[0].rearrange("p n i -> p (n i)").bitcast(I32))
+        gain_sb = kept([P, PACK], F32, "gain_sb")
+        nc.sync.dma_start(out=gain_sb[:], in_=gain.rearrange("(p t) -> p t", t=PACK))
+        wo_raw = load_words(wo_words[0], "wo_raw")
         load_scales(wo_sc_raw, wo_scales)
 
-        def quantize_weight(raw, name):
-            dealt = ring.tile([P, PACK * H], BF16, name=name + "_bf", tag="dealt", align_bytes=64)
-            nc.scalar.copy(
-                out=dealt[:].rearrange("p (t m j) -> p m j t", t=PACK, j=PACK),
-                in_=raw[:].rearrange("p j (m t) -> p m j t", t=PACK),
-            )
-            codes = kept([P, H], U32, name + "_q")
-            scales = kept([P, H], U8, name + "_s")
-            nc.vector.quantize_mx(out=codes[:].bitcast(FP8X4), scales=scales[:], in_=dealt[:])
+        def quantize(values, name):
+            width = values.shape[1] // PACK
+            codes = kept([P, width], U32, name + "_q")
+            scales = kept([P, width], U8, name + "_s")
+            nc.vector.quantize_mx(out=codes[:].bitcast(FP8X4), scales=scales[:], in_=values)
             return codes, scales
+
+        def quantize_w1(b):
+            values = ring.tile([P, passes * P * PACK], BF16, name="w1_bf", align_bytes=64)
+            nc.scalar.copy(
+                out=values[:].rearrange("p (a n i j) -> p a n j i", a=passes, i=LINE, j=PACK),
+                in_=w1_raw[b][:].rearrange("p a j (n i) -> p a n j i", i=LINE),
+            )
+            return quantize(values[:], "w1_%d" % b)
 
         v_sc = kept([P, S], U8, "v_sc")
         nc.vector.tensor_copy(out=v_sc[:], in_=tab_sc[:].indirect(idx[:]))
-        w1_q = [quantize_weight(w1_raw[a], "w1_%d" % a) for a in range(passes)]
         v_w = {}
         for a in range(passes):
             for lo in range(0, S, BANK):
@@ -145,45 +143,51 @@ def tile_list_household_profile_cells_kernel(
                 nc.vector.tensor_copy(out=tile[:], in_=tab_w[a][:].bitcast(U32).indirect(entries(idx, lo, lo + BANK)))
                 v_w[a, lo] = tile
 
-        x = kept([P, PACK, M], F32, "x")
-        starts = [sum(CHUNKS[:i]) for i in range(len(CHUNKS))]
-        x_bf = [kept([P, c, PACK], BF16, "x_bf%d" % i) for i, c in enumerate(CHUNKS)]
-
-        def round_planes(i, t0, t1):
-            lo, c = starts[i], CHUNKS[i]
-            nc.scalar.copy(
-                out=x_bf[i][:, :, t0:t1],
-                in_=x[:, t0:t1, lo : lo + c].rearrange("p t n -> p n t"),
-            )
-
-        for t in range(PACK):
-            cols = slice(t * P, (t + 1) * P)
-            for lo, hi in cuts[t]:
-                h = ring.tile([P, hi - lo], F32, name="h", tag="h", bufs=3, align_bytes=64)
-                for b in range(lo, hi, BANK):
+        for b in range(blocks):
+            w1_q, w1_s = quantize_w1(b)
+            cuts = ((0, BANK), (BANK, S)) if b == 0 else ((0, S),)
+            for lo, hi in cuts:
+                if b == blocks - 1:
+                    h = kept([P, S], F32, "h_last", tag="after_scatter")
+                else:
+                    h = ring.tile([P, hi - lo], F32, name="h", tag="h", bufs=3, align_bytes=64)
+                for first in range(lo, hi, BANK):
                     acc = psum.tile([P, BANK], F32, name="acc_h", tag="y", bufs=4)
                     for a in range(passes):
                         nc.tensor.matmul_mx(
                             out=acc[:],
-                            lhsT=w1_q[a][0][:, cols].bitcast(FP8X4),
-                            lhsT_scale=w1_q[a][1][:, cols],
-                            rhs=v_w[a, b][:].bitcast(FP8X4),
-                            rhs_scale=v_sc[4 * a : P, b : b + BANK],
+                            lhsT=w1_q[:, a * P : (a + 1) * P].bitcast(FP8X4),
+                            lhsT_scale=w1_s[:, a * P : (a + 1) * P],
+                            rhs=v_w[a, first][:].bitcast(FP8X4),
+                            rhs_scale=v_sc[4 * a : P, first : first + BANK],
                             start=(a == 0),
                             stop=(a == passes - 1),
                         )
-                    nc.scalar.copy(out=h[:, b - lo : b - lo + BANK], in_=acc[:])
+                    nc.scalar.copy(out=h[:, first - lo : first - lo + BANK], in_=acc[:])
                 nc.vector.tensor_tensor(
-                    out=page[t][:].indirect(entries(idx2, lo, hi)), in0=h[:], in1=wgs_sb[t, lo][:], op=ALU.mult
+                    out=page[b][:].indirect(entries(idx2, lo, hi)), in0=h[:], in1=wgs_sb[:, lo:hi], op=ALU.mult
                 )
-            step = M if t < PACK - 1 else GATHER
-            for lo in range(0, M, step):
-                nc.vector.tensor_copy(out=x[:, t, lo : lo + step], in_=page[t][:].indirect(entries(idx3, lo, lo + step)))
-            if t == PACK - 2:
-                for i in range(len(CHUNKS)):
-                    round_planes(i, 0, PACK - 1)
 
-        wc_q, wc_s = quantize_weight(wc_raw, "wc")
+        x = []
+
+        def fetch(picked):
+            lo = len(x) * FETCH
+            rows = kept([P, PACK, FETCH], F32, "x%d" % len(x))
+            for b in range(blocks):
+                nc.vector.tensor_copy(out=picked[:, b, :], in_=page[b][:].indirect(entries(idx3, lo, lo + FETCH)))
+                nc.sync.dma_start(out=rows[QUAD * b : QUAD * (b + 1), :, :], in_=picked[:, b, :])
+            x.append(rows)
+
+        picked_first = kept([P, 2, blocks, FETCH], F32, "picked_first", tag="after_scatter")
+        fetch(picked_first[:, 0, :, :])
+        fetch(picked_first[:, 1, :, :])
+
+        wc_bf = kept([P, PACK * H], BF16, "wc_bf")
+        nc.scalar.copy(
+            out=wc_bf[:].rearrange("p (t m j) -> p m j t", t=PACK, j=PACK),
+            in_=wc_raw[:].rearrange("p j (m t) -> p m j t", t=PACK),
+        )
+        wc_q, wc_s = quantize(wc_bf[:], "wc")
         wg_q = kept([P, 2 * H], U8, "wg_q")
         nc.vector.tensor_copy(
             out=wg_q[:].rearrange("p (t m b) -> p m t b", t=PACK, b=2),
@@ -205,17 +209,20 @@ def tile_list_household_profile_cells_kernel(
         y_sc = kept([P, groups, M], U8, "y_sc")
         y_rows = out_0.rearrange("(g p t) m -> g p t m", p=P, t=PACK)
         y_words = out_1.rearrange("g p m t -> p g (m t)").bitcast(I32)
+        starts = [sum(CHUNKS[:i]) for i in range(len(CHUNKS))]
 
-        def product(tag, bufs, count, c, lhs, rhs, rhs_scale):
+        def product(tag, bufs, count, lhs, rhs):
+            codes, scales = rhs
+            c = codes.shape[1]
             per_bank = BANK // c
             banks = []
             for first in range(0, count, per_bank):
                 acc = psum.tile([P, BANK], F32, name="acc_" + tag, tag=tag, bufs=bufs)
                 for s in range(per_bank):
-                    codes, scales = lhs(first + s)
+                    lhs_codes, lhs_scales = lhs(first + s)
                     nc.tensor.matmul_mx(
-                        out=acc[:, s * c : (s + 1) * c], lhsT=codes, lhsT_scale=scales,
-                        rhs=rhs, rhs_scale=rhs_scale, start=True, stop=True,
+                        out=acc[:, s * c : (s + 1) * c], lhsT=lhs_codes, lhsT_scale=lhs_scales,
+                        rhs=codes[:].bitcast(FP8X4), rhs_scale=scales[:], start=True, stop=True,
                     )
                 banks.append(acc)
             return banks
@@ -229,56 +236,88 @@ def tile_list_household_profile_cells_kernel(
         def out_lhs(s):
             return wo_q[:, s * P : (s + 1) * P].bitcast(FP8X4), wo_s[:, s * P : (s + 1) * P]
 
-        for i, c in enumerate(CHUNKS):
-            lo = starts[i]
-            cols = slice(lo, lo + c)
-            round_planes(i, PACK - 1, PACK)
-            x_q = kept([P, c], U32, "x_q%d" % i)
-            x_s = kept([P, c], U8, "x_s%d" % i)
-            nc.vector.quantize_mx(out=x_q[:].bitcast(FP8X4), scales=x_s[:], in_=x_bf[i][:].rearrange("p n t -> p (n t)"))
+        def woven(values):
+            return values.rearrange("p (n i t) -> p n t i", i=LINE, t=PACK)
 
-            cand = ring.tile([P, PACK * c], F32, name="cand", align_bytes=64)
-            for b, acc in enumerate(product("c", 2, PACK, c, cand_lhs, x_q[:].bitcast(FP8X4), x_s[:])):
-                nc.scalar.activation(out=cand[:, b * BANK : (b + 1) * BANK], in_=acc[:], func=ACT.Tanh)
-            gate = ring.tile([P, PACK * c], F32, name="gate", align_bytes=64)
-            for b, acc in enumerate(product("g", 2, PACK, c, gate_lhs, x_q[:].bitcast(FP8X4), x_s[:])):
-                nc.scalar.activation(out=gate[:, b * BANK : (b + 1) * BANK], in_=acc[:], func=ACT.Sigmoid)
+        def by_lines(planes):
+            return planes.rearrange("p t (n i) -> p n t i", i=LINE)
 
+        def x_of(i):
+            lo = starts[i] % FETCH
+            return x[starts[i] // FETCH][:, :, lo : lo + CHUNKS[i]]
+
+        cand, gate, z, y = {}, {}, {}, {}
+
+        def activate(i):
+            c = CHUNKS[i]
+            x_bf = kept([P, PACK * c], BF16, "x_bf%d" % i)
+            nc.scalar.copy(out=woven(x_bf[:]), in_=by_lines(x_of(i)))
+            x_mx = quantize(x_bf[:], "x%d" % i)
+            if i == 0:
+                fetch(kept([P, blocks, FETCH], F32, "picked2", tag="x_bf0")[:])
+            cand[i] = ring.tile([P, PACK * c], F32, name="cand", bufs=3, align_bytes=64)
+            for b, acc in enumerate(product("c", 2, PACK, cand_lhs, x_mx)):
+                nc.scalar.activation(out=cand[i][:, b * BANK : (b + 1) * BANK], in_=acc[:], func=ACT.Tanh)
+            gate[i] = ring.tile([P, PACK * c], F32, name="gate", bufs=3, align_bytes=64)
+            for b, acc in enumerate(product("g", 2, PACK, gate_lhs, x_mx)):
+                nc.scalar.activation(out=gate[i][:, b * BANK : (b + 1) * BANK], in_=acc[:], func=ACT.Sigmoid)
+
+        def interpolate(i):
+            c = CHUNKS[i]
             for t in range(PACK):
-                part = cand[:, t * c : (t + 1) * c]
+                part = cand[i][:, t * c : (t + 1) * c]
                 nc.vector.scalar_tensor_tensor(
-                    out=part, in0=part, scalar=gain_sb[:, t : t + 1], in1=x[:, t, cols], op0=ALU.mult, op1=ALU.subtract
+                    out=part, in0=part, scalar=gain_sb[:, t : t + 1], in1=x_of(i)[:, t, :],
+                    op0=ALU.mult, op1=ALU.subtract,
                 )
-            nc.vector.tensor_tensor(out=cand[:], in0=cand[:], in1=gate[:], op=ALU.mult)
-            z_bf = ring.tile([P, PACK * c], BF16, name="z_bf", align_bytes=64)
+            for half in (slice(0, 2 * c), slice(2 * c, PACK * c)):
+                nc.vector.tensor_tensor(out=cand[i][:, half], in0=cand[i][:, half], in1=gate[i][:, half], op=ALU.mult)
+            z_bf = kept([P, PACK * c], BF16, "z_bf%d" % i)
             nc.vector.tensor_tensor(
-                out=z_bf[:].rearrange("p (n i t) -> p n t i", i=4, t=PACK),
-                in0=cand[:].rearrange("p (t n i) -> p n t i", i=4, t=PACK),
-                in1=x[:, :, cols].rearrange("p t (n i) -> p n t i", i=4),
+                out=woven(z_bf[:]),
+                in0=by_lines(cand[i][:].rearrange("p (t n) -> p t n", t=PACK)),
+                in1=by_lines(x_of(i)),
                 op=ALU.add,
             )
-            z_q = ring.tile([P, c], U32, name="z_q", align_bytes=64)
-            z_s = ring.tile([P, c], U8, name="z_s", align_bytes=64)
-            nc.vector.quantize_mx(out=z_q[:].bitcast(FP8X4), scales=z_s[:], in_=z_bf[:])
+            z[i] = quantize(z_bf[:], "z%d" % i)
+            if i == 0:
+                fetch(kept([P, blocks, FETCH], F32, "picked3", tag="z_bf0")[:])
 
-            y = big([P, groups * PACK * c], "y")
-            for b, acc in enumerate(product("y", 4, groups * PACK, c, out_lhs, z_q[:].bitcast(FP8X4), z_s[:])):
-                nc.scalar.copy(out=y[:, b * BANK : (b + 1) * BANK], in_=acc[:])
+        def project(i):
+            c = CHUNKS[i]
+            y[i] = kept([P, groups, PACK, c], F32, "y%d" % i, tag=("w1_raw0", "wc_raw", "after_scatter")[i % 3])
+            flat = y[i][:].rearrange("p g t n -> p (g t n)")
+            for b, acc in enumerate(product("y", 4, groups * PACK, out_lhs, z[i])):
+                mover = nc.vector.tensor_copy if (i == len(CHUNKS) - 1 and b == 1) else nc.scalar.copy
+                mover(out=flat[:, b * BANK : (b + 1) * BANK], in_=acc[:])
+            for g in range(groups):
+                nc.sync.dma_start(out=y_rows[g][:, :, starts[i] : starts[i] + c], in_=y[i][:, g, :, :])
+
+        def make_planes(i):
+            c = CHUNKS[i]
+            cols = slice(starts[i], starts[i] + c)
             y_q = ring.tile([P, groups, c], I32, name="y_q", bufs=3, align_bytes=64)
             for g in range(groups):
-                y_g = y[:, g * PACK * c : (g + 1) * PACK * c]
-                nc.sync.dma_start(out=y_rows[g][:, :, cols], in_=y_g.rearrange("p (t n) -> p t n", t=PACK))
                 y_bf = ring.tile([P, PACK * c], BF16, name="y_bf", bufs=3, align_bytes=64)
-                rounder = nc.scalar.copy if (g == 1 and i < 2) else nc.vector.tensor_copy
-                rounder(
-                    out=y_bf[:].rearrange("p (n i t) -> p n t i", i=4, t=PACK),
-                    in_=y_g.rearrange("p (t n i) -> p n t i", i=4, t=PACK),
-                )
+                rounder = nc.scalar.copy if (i, g) in ROUND_ON_SCALAR else nc.vector.tensor_copy
+                rounder(out=woven(y_bf[:]), in_=by_lines(y[i][:, g, :, :]))
                 nc.vector.quantize_mx(out=y_q[:, g, :].bitcast(FP8X4), scales=y_sc[:, g, cols], in_=y_bf[:])
             nc.sync.dma_start(out=y_words[:, :, cols], in_=y_q[:])
 
-        for q in range(4):
+        count = len(CHUNKS)
+        activate(0)
+        for step in range(count + 2):
+            if step + 1 < count:
+                activate(step + 1)
+            if 0 <= step - 2:
+                make_planes(step - 2)
+            if 0 <= step - 1 < count:
+                project(step - 1)
+            if step < count:
+                interpolate(step)
+
+        for q in range(P // QUAD):
             nc.sync.dma_start(
                 out=out_2[:, 4 * q : 4 * q + 4, :].rearrange("g r m -> r g m").bitcast(I32),
-                in_=y_sc[32 * q : 32 * q + 4, :, :].bitcast(I32),
+                in_=y_sc[QUAD * q : QUAD * q + 4, :, :].bitcast(I32),
             )

@@ -24,8 +24,8 @@ BANK = 512
 LIST = 16
 LINE = 4
 FETCH = 256
-CHUNKS = (256, 256, 256, 128, 128)
-ROUND_ON_SCALAR = ((0, 0), (0, 1), (1, 0), (1, 1), (2, 0), (2, 1), (4, 0))
+CHUNKS = (256, 256, 256, 256)
+ROUND_ON_SCALAR = ((0, 1), (1, 1))
 
 
 def tile_list_household_profile_cells_kernel(
@@ -92,9 +92,9 @@ def tile_list_household_profile_cells_kernel(
             nc.sync.dma_start(out=tile[:], in_=rows)
             return tile
 
+        nc.sync.dma_start(idx[:], offs)
         tab_w = [load_words(tab_words[0], "tab_w0")]
         load_scales(tab_sc, tab_scales)
-        nc.sync.dma_start(idx[:], offs)
         load_w1(0)
         tab_w.append(load_words(tab_words[1], "tab_w1"))
         page = [load_rows(page0[0:P, :], "page0")]
@@ -137,8 +137,8 @@ def tile_list_household_profile_cells_kernel(
         v_sc = kept([P, S], U8, "v_sc")
         nc.vector.tensor_copy(out=v_sc[:], in_=tab_sc[:].indirect(idx[:]))
         v_w = {}
-        for a in range(passes):
-            for lo in range(0, S, BANK):
+        for lo in range(0, S, BANK):
+            for a in range(passes):
                 tile = kept([P, BANK], U32, "v_w%d_%d" % (a, lo))
                 nc.vector.tensor_copy(out=tile[:], in_=tab_w[a][:].bitcast(U32).indirect(entries(idx, lo, lo + BANK)))
                 v_w[a, lo] = tile
@@ -253,8 +253,8 @@ def tile_list_household_profile_cells_kernel(
             x_bf = kept([P, PACK * c], BF16, "x_bf%d" % i)
             nc.scalar.copy(out=woven(x_bf[:]), in_=by_lines(x_of(i)))
             x_mx = quantize(x_bf[:], "x%d" % i)
-            if i == 0:
-                fetch(kept([P, blocks, FETCH], F32, "picked2", tag="x_bf0")[:])
+            if len(x) < len(CHUNKS):
+                fetch(kept([P, blocks, FETCH], F32, "picked%d" % len(x), tag="x_bf%d" % i)[:])
             cand[i] = ring.tile([P, PACK * c], F32, name="cand", bufs=3, align_bytes=64)
             for b, acc in enumerate(product("c", 2, PACK, cand_lhs, x_mx)):
                 nc.scalar.activation(out=cand[i][:, b * BANK : (b + 1) * BANK], in_=acc[:], func=ACT.Tanh)
@@ -270,8 +270,7 @@ def tile_list_household_profile_cells_kernel(
                     out=part, in0=part, scalar=gain_sb[:, t : t + 1], in1=x_of(i)[:, t, :],
                     op0=ALU.mult, op1=ALU.subtract,
                 )
-            for half in (slice(0, 2 * c), slice(2 * c, PACK * c)):
-                nc.vector.tensor_tensor(out=cand[i][:, half], in0=cand[i][:, half], in1=gate[i][:, half], op=ALU.mult)
+            nc.vector.tensor_tensor(out=cand[i][:], in0=cand[i][:], in1=gate[i][:], op=ALU.mult)
             z_bf = kept([P, PACK * c], BF16, "z_bf%d" % i)
             nc.vector.tensor_tensor(
                 out=woven(z_bf[:]),
@@ -280,16 +279,13 @@ def tile_list_household_profile_cells_kernel(
                 op=ALU.add,
             )
             z[i] = quantize(z_bf[:], "z%d" % i)
-            if i == 0:
-                fetch(kept([P, blocks, FETCH], F32, "picked3", tag="z_bf0")[:])
 
         def project(i):
             c = CHUNKS[i]
             y[i] = kept([P, groups, PACK, c], F32, "y%d" % i, tag=("w1_raw0", "wc_raw", "after_scatter")[i % 3])
             flat = y[i][:].rearrange("p g t n -> p (g t n)")
             for b, acc in enumerate(product("y", 4, groups * PACK, out_lhs, z[i])):
-                mover = nc.vector.tensor_copy if (i == len(CHUNKS) - 1 and b == 1) else nc.scalar.copy
-                mover(out=flat[:, b * BANK : (b + 1) * BANK], in_=acc[:])
+                nc.scalar.copy(out=flat[:, b * BANK : (b + 1) * BANK], in_=acc[:])
             for g in range(groups):
                 nc.sync.dma_start(out=y_rows[g][:, :, starts[i] : starts[i] + c], in_=y[i][:, g, :, :])
 
@@ -309,12 +305,12 @@ def tile_list_household_profile_cells_kernel(
         for step in range(count + 2):
             if step + 1 < count:
                 activate(step + 1)
-            if 0 <= step - 2:
-                make_planes(step - 2)
-            if 0 <= step - 1 < count:
-                project(step - 1)
             if step < count:
                 interpolate(step)
+            if 0 <= step - 1 < count:
+                project(step - 1)
+            if 0 <= step - 2:
+                make_planes(step - 2)
 
         for q in range(P // QUAD):
             nc.sync.dma_start(

@@ -25,7 +25,7 @@ LIST = 16
 LINE = 4
 FETCH = 256
 CHUNKS = (256, 256, 256, 256)
-ROUND_ON_SCALAR = ((0, 1), (1, 1))
+ROUND_ON_SCALAR = ((0, 0), (0, 1), (3, 0))
 
 
 def tile_list_household_profile_cells_kernel(
@@ -57,17 +57,16 @@ def tile_list_household_profile_cells_kernel(
             nc.vector.memset(plane[:].bitcast(I32), 0)
             return plane
 
-        def load_scales(plane, scales):
+        def load_scales(plane, scales, first=0):
             rows = 4 * scales.shape[0]
             for q in range(P // QUAD):
                 nc.sync.dma_start(
-                    out=plane[QUAD * q : QUAD * q + rows, :].bitcast(I32),
+                    out=plane[QUAD * q + first : QUAD * q + first + rows, :].bitcast(I32),
                     in_=scales[:, 4 * q : 4 * q + 4, :].bitcast(I32),
                 )
 
         tab_sc = zeroed_plane(T, "tab_sc")
-        wg_sc_raw = zeroed_plane(H, "wg_sc_raw")
-        wo_sc_raw = zeroed_plane(N, "wo_sc_raw")
+        w_sc_raw = zeroed_plane(KP, "w_sc_raw")
         warm_in = kept([P, 1], F32, "warm_in")
         warm_out = kept([P, 1], F32, "warm_out")
         nc.vector.memset(warm_in[:], 0.0)
@@ -93,14 +92,13 @@ def tile_list_household_profile_cells_kernel(
             return tile
 
         nc.sync.dma_start(idx[:], offs)
-        tab_w = [load_words(tab_words[0], "tab_w0")]
         load_scales(tab_sc, tab_scales)
-        load_w1(0)
-        tab_w.append(load_words(tab_words[1], "tab_w1"))
-        page = [load_rows(page0[0:P, :], "page0")]
         nc.sync.dma_start(idx2[:], offs2)
+        load_w1(0)
+        tab_w = [load_words(tab_words[a], "tab_w%d" % a) for a in range(passes)]
         wgs_sb = kept([P, S], F32, "wgs")
         nc.sync.dma_start(out=wgs_sb[:, 0:BANK], in_=wgs[:, 0:BANK])
+        page = [load_rows(page0[0:P, :], "page0")]
         load_w1(1)
         load_w1(2)
         nc.sync.dma_start(out=wgs_sb[:, BANK:S], in_=wgs[:, BANK:S])
@@ -113,11 +111,11 @@ def tile_list_household_profile_cells_kernel(
         nc.sync.dma_start(out=wc_raw[:], in_=wc.rearrange("(p j) c -> p j c", j=PACK))
         wg_raw = kept([P, 2 * H], U8, "wg_raw")
         nc.sync.dma_start(out=wg_raw[:].bitcast(I32), in_=wg_words[0].bitcast(I32))
-        load_scales(wg_sc_raw, wg_scales)
+        load_scales(w_sc_raw, wg_scales)
         gain_sb = kept([P, PACK], F32, "gain_sb")
         nc.sync.dma_start(out=gain_sb[:], in_=gain.rearrange("(p t) -> p t", t=PACK))
+        load_scales(w_sc_raw, wo_scales[0].rearrange("r (g e) -> g r e", g=groups), first=4)
         wo_raw = load_words(wo_words[0], "wo_raw")
-        load_scales(wo_sc_raw, wo_scales)
 
         def quantize(values, name):
             width = values.shape[1] // PACK
@@ -202,9 +200,8 @@ def tile_list_household_profile_cells_kernel(
             )
             return dealt
 
-        wg_s = deal(wg_sc_raw, U8, "wg_s")
+        w_s = deal(w_sc_raw, U8, "w_s")
         wo_q = deal(wo_raw, I32, "wo_q")
-        wo_s = deal(wo_sc_raw, U8, "wo_s")
 
         y_sc = kept([P, groups, M], U8, "y_sc")
         y_rows = out_0.rearrange("(g p t) m -> g p t m", p=P, t=PACK)
@@ -228,13 +225,14 @@ def tile_list_household_profile_cells_kernel(
             return banks
 
         def gate_lhs(t):
-            return wg_q[:, 2 * t * P : 2 * (t + 1) * P].bitcast(FP4X4), wg_s[:, t * P : (t + 1) * P]
+            return wg_q[:, 2 * t * P : 2 * (t + 1) * P].bitcast(FP4X4), w_s[:, t * P : (t + 1) * P]
 
         def cand_lhs(t):
             return wc_q[:, t * P : (t + 1) * P].bitcast(FP8X4), wc_s[:, t * P : (t + 1) * P]
 
         def out_lhs(s):
-            return wo_q[:, s * P : (s + 1) * P].bitcast(FP8X4), wo_s[:, s * P : (s + 1) * P]
+            g, t = divmod(s, PACK)
+            return wo_q[:, s * P : (s + 1) * P].bitcast(FP8X4), w_s[4 + 4 * g : P, t * P : (t + 1) * P]
 
         def woven(values):
             return values.rearrange("p (n i t) -> p n t i", i=LINE, t=PACK)
@@ -248,33 +246,42 @@ def tile_list_household_profile_cells_kernel(
 
         cand, gate, z, y = {}, {}, {}, {}
 
-        def activate(i):
+        x_mx = {}
+
+        def round_x(i):
             c = CHUNKS[i]
             x_bf = kept([P, PACK * c], BF16, "x_bf%d" % i)
             nc.scalar.copy(out=woven(x_bf[:]), in_=by_lines(x_of(i)))
-            x_mx = quantize(x_bf[:], "x%d" % i)
+            x_mx[i] = quantize(x_bf[:], "x%d" % i)
             if len(x) < len(CHUNKS):
                 fetch(kept([P, blocks, FETCH], F32, "picked%d" % len(x), tag="x_bf%d" % i)[:])
-            cand[i] = ring.tile([P, PACK * c], F32, name="cand", bufs=3, align_bytes=64)
-            for b, acc in enumerate(product("c", 2, PACK, cand_lhs, x_mx)):
+
+        def activate(i):
+            c = CHUNKS[i]
+            wide = 4 if i == 2 else 2
+            both = kept([P, wide * PACK * c], F32, "acts%d" % i, tag=("after_scatter", "page_free", "x_bf1", "w1_raw0")[i])
+            cand[i] = both[:, 0 : PACK * c]
+            gate[i] = both[:, PACK * c : 2 * PACK * c]
+            if i == 2:
+                y[0] = both[:, 2 * PACK * c :]
+            for b, acc in enumerate(product("c", 2, PACK, cand_lhs, x_mx[i])):
                 nc.scalar.activation(out=cand[i][:, b * BANK : (b + 1) * BANK], in_=acc[:], func=ACT.Tanh)
-            gate[i] = ring.tile([P, PACK * c], F32, name="gate", bufs=3, align_bytes=64)
-            for b, acc in enumerate(product("g", 2, PACK, gate_lhs, x_mx)):
+            for b, acc in enumerate(product("g", 2, PACK, gate_lhs, x_mx[i])):
                 nc.scalar.activation(out=gate[i][:, b * BANK : (b + 1) * BANK], in_=acc[:], func=ACT.Sigmoid)
 
         def interpolate(i):
             c = CHUNKS[i]
+            step = kept([P, PACK * c], F32, "step%d" % i, tag=("page3", "x_bf3", "page1", "page2")[i])
             for t in range(PACK):
-                part = cand[i][:, t * c : (t + 1) * c]
                 nc.vector.scalar_tensor_tensor(
-                    out=part, in0=part, scalar=gain_sb[:, t : t + 1], in1=x_of(i)[:, t, :],
-                    op0=ALU.mult, op1=ALU.subtract,
+                    out=step[:, t * c : (t + 1) * c], in0=cand[i][:, t * c : (t + 1) * c],
+                    scalar=gain_sb[:, t : t + 1], in1=x_of(i)[:, t, :], op0=ALU.mult, op1=ALU.subtract,
                 )
-            nc.vector.tensor_tensor(out=cand[i][:], in0=cand[i][:], in1=gate[i][:], op=ALU.mult)
-            z_bf = kept([P, PACK * c], BF16, "z_bf%d" % i)
+            nc.vector.tensor_tensor(out=step[:], in0=step[:], in1=gate[i], op=ALU.mult)
+            z_bf = kept([P, PACK * c], BF16, "z_bf%d" % i, tag="x_bf2" if i == 0 else "")
             nc.vector.tensor_tensor(
                 out=woven(z_bf[:]),
-                in0=by_lines(cand[i][:].rearrange("p (t n) -> p t n", t=PACK)),
+                in0=by_lines(step[:].rearrange("p (t n) -> p t n", t=PACK)),
                 in1=by_lines(x_of(i)),
                 op=ALU.add,
             )
@@ -282,8 +289,10 @@ def tile_list_household_profile_cells_kernel(
 
         def project(i):
             c = CHUNKS[i]
-            y[i] = kept([P, groups, PACK, c], F32, "y%d" % i, tag=("w1_raw0", "wc_raw", "after_scatter")[i % 3])
-            flat = y[i][:].rearrange("p g t n -> p (g t n)")
+            if i > 0:
+                y[i] = kept([P, groups * PACK * c], F32, "y%d" % i, tag=("", "tab_w0", "tab_w1", "wc_raw")[i])[:]
+            flat = y[i]
+            y[i] = flat.rearrange("p (g t n) -> p g t n", g=groups, t=PACK)
             for b, acc in enumerate(product("y", 4, groups * PACK, out_lhs, z[i])):
                 nc.scalar.copy(out=flat[:, b * BANK : (b + 1) * BANK], in_=acc[:])
             for g in range(groups):
@@ -292,25 +301,25 @@ def tile_list_household_profile_cells_kernel(
         def make_planes(i):
             c = CHUNKS[i]
             cols = slice(starts[i], starts[i] + c)
-            y_q = ring.tile([P, groups, c], I32, name="y_q", bufs=3, align_bytes=64)
+            y_q = kept([P, groups, c], I32, "y_q%d" % i)
             for g in range(groups):
-                y_bf = ring.tile([P, PACK * c], BF16, name="y_bf", bufs=3, align_bytes=64)
+                y_bf = ring.tile([P, PACK * c], BF16, name="y_bf", bufs=4, align_bytes=64)
                 rounder = nc.scalar.copy if (i, g) in ROUND_ON_SCALAR else nc.vector.tensor_copy
                 rounder(out=woven(y_bf[:]), in_=by_lines(y[i][:, g, :, :]))
                 nc.vector.quantize_mx(out=y_q[:, g, :].bitcast(FP8X4), scales=y_sc[:, g, cols], in_=y_bf[:])
             nc.sync.dma_start(out=y_words[:, :, cols], in_=y_q[:])
 
         count = len(CHUNKS)
-        activate(0)
-        for step in range(count + 2):
-            if step + 1 < count:
-                activate(step + 1)
-            if step < count:
-                interpolate(step)
-            if 0 <= step - 1 < count:
-                project(step - 1)
-            if 0 <= step - 2:
-                make_planes(step - 2)
+        for i in range(0, count, 2):
+            round_x(i)
+            round_x(i + 1)
+            activate(i)
+            activate(i + 1)
+        for i in range(count):
+            interpolate(i)
+            project(i)
+        for i in range(count):
+            make_planes(i)
 
         for q in range(P // QUAD):
             nc.sync.dma_start(

@@ -93,9 +93,9 @@ def tile_list_household_profile_cells_kernel(
 
         nc.sync.dma_start(idx[:], offs)
         load_scales(tab_sc, tab_scales)
-        nc.sync.dma_start(idx2[:], offs2)
         load_w1(0)
         tab_w = [load_words(tab_words[a], "tab_w%d" % a) for a in range(passes)]
+        nc.sync.dma_start(idx2[:], offs2)
         wgs_sb = kept([P, S], F32, "wgs")
         nc.sync.dma_start(out=wgs_sb[:, 0:BANK], in_=wgs[:, 0:BANK])
         page = [load_rows(page0[0:P, :], "page0")]
@@ -192,8 +192,8 @@ def tile_list_household_profile_cells_kernel(
             in_=wg_raw[:].rearrange("p (m t b) -> p m t b", t=PACK, b=2),
         )
 
-        def deal(raw, dtype, name):
-            dealt = kept([P, raw.shape[1]], dtype, name)
+        def deal(raw, dtype, name, tag=""):
+            dealt = kept([P, raw.shape[1]], dtype, name, tag=tag)
             nc.vector.tensor_copy(
                 out=dealt[:].rearrange("p (g t m) -> p g m t", t=PACK, m=P),
                 in_=raw[:].rearrange("p (g m t) -> p g m t", t=PACK, m=P),
@@ -201,7 +201,6 @@ def tile_list_household_profile_cells_kernel(
             return dealt
 
         w_s = deal(w_sc_raw, U8, "w_s")
-        wo_q = deal(wo_raw, I32, "wo_q")
 
         y_sc = kept([P, groups, M], U8, "y_sc")
         y_rows = out_0.rearrange("(g p t) m -> g p t m", p=P, t=PACK)
@@ -232,7 +231,7 @@ def tile_list_household_profile_cells_kernel(
 
         def out_lhs(s):
             g, t = divmod(s, PACK)
-            return wo_q[:, s * P : (s + 1) * P].bitcast(FP8X4), w_s[4 + 4 * g : P, t * P : (t + 1) * P]
+            return wo_q[0][:, s * P : (s + 1) * P].bitcast(FP8X4), w_s[4 + 4 * g : P, t * P : (t + 1) * P]
 
         def woven(values):
             return values.rearrange("p (n i t) -> p n t i", i=LINE, t=PACK)
@@ -247,6 +246,7 @@ def tile_list_household_profile_cells_kernel(
         cand, gate, z, y = {}, {}, {}, {}
 
         x_mx = {}
+        wo_q = []
 
         def round_x(i):
             c = CHUNKS[i]
@@ -315,6 +315,7 @@ def tile_list_household_profile_cells_kernel(
             round_x(i + 1)
             activate(i)
             activate(i + 1)
+        wo_q.append(deal(wo_raw, I32, "wo_q", tag="page0"))
         for i in range(count):
             interpolate(i)
             project(i)

@@ -25,7 +25,7 @@ LIST = 16
 LINE = 4
 FETCH = 256
 CHUNKS = (256, 256, 256, 256)
-ROUND_ON_SCALAR = ((0, 0), (0, 1), (3, 0))
+ROUND_ON_SCALAR = ((0, 0), (1, 0), (3, 0))
 
 
 def tile_list_household_profile_cells_kernel(

@@ -192,9 +192,9 @@ def tile_list_household_profile_cells_kernel(
             in_=wg_raw[:].rearrange("p (m t b) -> p m t b", t=PACK, b=2),
         )
 
-        def deal(raw, dtype, name, tag=""):
+        def deal(raw, dtype, name, tag="", engine=nc.vector):
             dealt = kept([P, raw.shape[1]], dtype, name, tag=tag)
-            nc.vector.tensor_copy(
+            engine.tensor_copy(
                 out=dealt[:].rearrange("p (g t m) -> p g m t", t=PACK, m=P),
                 in_=raw[:].rearrange("p (g m t) -> p g m t", t=PACK, m=P),
             )
@@ -246,7 +246,7 @@ def tile_list_household_profile_cells_kernel(
         cand, gate, z, y = {}, {}, {}, {}
 
         x_mx = {}
-        wo_q = []
+        wo_q = [deal(wo_raw, I32, "wo_q", tag="wgs", engine=nc.gpsimd)]
 
         def round_x(i):
             c = CHUNKS[i]
@@ -315,7 +315,6 @@ def tile_list_household_profile_cells_kernel(
             round_x(i + 1)
             activate(i)
             activate(i + 1)
-        wo_q.append(deal(wo_raw, I32, "wo_q", tag="page0"))
         for i in range(count):
             interpolate(i)
             project(i)

@@ -25,7 +25,7 @@ LIST = 16
 LINE = 4
 FETCH = 256
 CHUNKS = (256, 256, 256, 256)
-ROUND_ON_SCALAR = ((0, 0), (1, 0), (3, 0))
+ROUND_ON_SCALAR = ((2, 1), (3, 0), (3, 1))
 
 
 def tile_list_household_profile_cells_kernel(
@@ -172,13 +172,17 @@ def tile_list_household_profile_cells_kernel(
             lo = len(x) * FETCH
             rows = kept([P, PACK, FETCH], F32, "x%d" % len(x))
             for b in range(blocks):
-                nc.vector.tensor_copy(out=picked[:, b, :], in_=page[b][:].indirect(entries(idx3, lo, lo + FETCH)))
-                nc.sync.dma_start(out=rows[QUAD * b : QUAD * (b + 1), :, :], in_=picked[:, b, :])
+                nc.vector.tensor_copy(out=picked[b], in_=page[b][:].indirect(entries(idx3, lo, lo + FETCH)))
+                nc.sync.dma_start(out=rows[QUAD * b : QUAD * (b + 1), :, :], in_=picked[b])
             x.append(rows)
 
-        picked_first = kept([P, 2, blocks, FETCH], F32, "picked_first", tag="after_scatter")
-        fetch(picked_first[:, 0, :, :])
-        fetch(picked_first[:, 1, :, :])
+        def parts(tile):
+            return [tile[:, b, :] for b in range(tile.shape[1])]
+
+        picked_first = parts(kept([P, 3 * blocks - 1, FETCH], F32, "picked_first", tag="after_scatter"))
+        fetch(picked_first[:blocks])
+        fetch(picked_first[blocks : 2 * blocks - 1] + [kept([P, FETCH], F32, "picked_last")[:]])
+        fetch(picked_first[2 * blocks - 1 :])
 
         wc_bf = kept([P, PACK * H], BF16, "wc_bf")
         nc.scalar.copy(
@@ -246,6 +250,7 @@ def tile_list_household_profile_cells_kernel(
         cand, gate, z, y = {}, {}, {}, {}
 
         x_mx = {}
+        steps = {}
         wo_q = [deal(wo_raw, I32, "wo_q", tag="wgs", engine=nc.gpsimd)]
 
         def round_x(i):
@@ -253,32 +258,34 @@ def tile_list_household_profile_cells_kernel(
             x_bf = kept([P, PACK * c], BF16, "x_bf%d" % i)
             nc.scalar.copy(out=woven(x_bf[:]), in_=by_lines(x_of(i)))
             x_mx[i] = quantize(x_bf[:], "x%d" % i)
-            if len(x) < len(CHUNKS):
-                fetch(kept([P, blocks, FETCH], F32, "picked%d" % len(x), tag="x_bf%d" % i)[:])
+            if i == 0:
+                fetch(parts(kept([P, blocks, FETCH], F32, "picked3", tag="x_bf0")))
 
         def activate(i):
             c = CHUNKS[i]
-            wide = 4 if i == 2 else 2
-            both = kept([P, wide * PACK * c], F32, "acts%d" % i, tag=("after_scatter", "page_free", "x_bf1", "w1_raw0")[i])
-            cand[i] = both[:, 0 : PACK * c]
-            gate[i] = both[:, PACK * c : 2 * PACK * c]
+            both = kept([P, 4 if i == 2 else 2, PACK * c], F32, "acts%d" % i, tag=("picked_last", "after_scatter", "x_bf0", "w1_raw0")[i])
             if i == 2:
-                y[0] = both[:, 2 * PACK * c :]
-            for b, acc in enumerate(product("c", 2, PACK, cand_lhs, x_mx[i])):
-                nc.scalar.activation(out=cand[i][:, b * BANK : (b + 1) * BANK], in_=acc[:], func=ACT.Tanh)
-            for b, acc in enumerate(product("g", 2, PACK, gate_lhs, x_mx[i])):
-                nc.scalar.activation(out=gate[i][:, b * BANK : (b + 1) * BANK], in_=acc[:], func=ACT.Sigmoid)
+                y[0] = both[:, 2:4, :].rearrange("p g n -> p (g n)")
+            cand[i] = both[:, 0, :]
+            gate[i] = both[:, 1, :]
+            for tag, into, lhs, func in (("c", cand[i], cand_lhs, ACT.Tanh), ("g", gate[i], gate_lhs, ACT.Sigmoid)):
+                for b, acc in enumerate(product(tag, 2, PACK, lhs, x_mx[i])):
+                    nc.scalar.activation(out=into[:, b * BANK : (b + 1) * BANK], in_=acc[:], func=func)
+
+        def subtract(i):
+            c = CHUNKS[i]
+            steps[i] = kept([P, PACK * c], F32, "step%d" % i, tag=("page3", "page0", "page1", "page2")[i])
+            for t in range(PACK):
+                nc.vector.scalar_tensor_tensor(
+                    out=steps[i][:, t * c : (t + 1) * c], in0=cand[i][:, t * c : (t + 1) * c],
+                    scalar=gain_sb[:, t : t + 1], in1=x_of(i)[:, t, :], op0=ALU.mult, op1=ALU.subtract,
+                )
 
         def interpolate(i):
             c = CHUNKS[i]
-            step = kept([P, PACK * c], F32, "step%d" % i, tag=("page3", "x_bf3", "page1", "page2")[i])
-            for t in range(PACK):
-                nc.vector.scalar_tensor_tensor(
-                    out=step[:, t * c : (t + 1) * c], in0=cand[i][:, t * c : (t + 1) * c],
-                    scalar=gain_sb[:, t : t + 1], in1=x_of(i)[:, t, :], op0=ALU.mult, op1=ALU.subtract,
-                )
-            nc.vector.tensor_tensor(out=step[:], in0=step[:], in1=gate[i], op=ALU.mult)
-            z_bf = kept([P, PACK * c], BF16, "z_bf%d" % i, tag="x_bf2" if i == 0 else "")
+            step = steps[i]
+            nc.vector.tensor_tensor(out=step[:], in0=steps[i][:], in1=gate[i], op=ALU.mult)
+            z_bf = kept([P, PACK * c], BF16, "z_bf%d" % i, tag=("x_bf2", "x_bf3", "", "")[i])
             nc.vector.tensor_tensor(
                 out=woven(z_bf[:]),
                 in0=by_lines(step[:].rearrange("p (t n) -> p t n", t=PACK)),
@@ -303,21 +310,28 @@ def tile_list_household_profile_cells_kernel(
             cols = slice(starts[i], starts[i] + c)
             y_q = kept([P, groups, c], I32, "y_q%d" % i)
             for g in range(groups):
-                y_bf = ring.tile([P, PACK * c], BF16, name="y_bf", bufs=4, align_bytes=64)
-                rounder = nc.scalar.copy if (i, g) in ROUND_ON_SCALAR else nc.vector.tensor_copy
-                rounder(out=woven(y_bf[:]), in_=by_lines(y[i][:, g, :, :]))
-                nc.vector.quantize_mx(out=y_q[:, g, :].bitcast(FP8X4), scales=y_sc[:, g, cols], in_=y_bf[:])
+                if (i, g) in ROUND_ON_SCALAR:
+                    y_bf = kept([P, PACK * c], BF16, "y_bf%d_%d" % (i, g))[:]
+                    nc.scalar.copy(out=woven(y_bf), in_=by_lines(y[i][:, g, :, :]))
+                else:
+                    y_bf = late.pop()
+                    nc.vector.tensor_copy(out=woven(y_bf), in_=by_lines(y[i][:, g, :, :]))
+                nc.vector.quantize_mx(out=y_q[:, g, :].bitcast(FP8X4), scales=y_sc[:, g, cols], in_=y_bf)
             nc.sync.dma_start(out=y_words[:, :, cols], in_=y_q[:])
 
         count = len(CHUNKS)
-        for i in range(0, count, 2):
-            round_x(i)
-            round_x(i + 1)
-            activate(i)
-            activate(i + 1)
+        round_x(0)
         for i in range(count):
+            if i + 1 < count:
+                round_x(i + 1)
+            activate(i)
+        for i in range(count):
+            subtract(i)
             interpolate(i)
             project(i)
+        on_vector = groups * count - len(ROUND_ON_SCALAR)
+        late_tile = kept([P, on_vector, PACK * FETCH], BF16, "late", tag="z_bf%d" % (count - 1))
+        late = [late_tile[:, j, :] for j in range(on_vector)]
         for i in range(count):
             make_planes(i)
 

@@ -25,7 +25,7 @@ LIST = 16
 LINE = 4
 FETCH = 256
 CHUNKS = (256, 256, 256, 256)
-ROUND_ON_SCALAR = ((2, 1), (3, 0), (3, 1))
+ROUND_ON_SCALAR = ((3, 0), (3, 1))
 
 
 def tile_list_household_profile_cells_kernel(
@@ -251,6 +251,7 @@ def tile_list_household_profile_cells_kernel(
 
         x_mx = {}
         steps = {}
+        acts = {}
         wo_q = [deal(wo_raw, I32, "wo_q", tag="wgs", engine=nc.gpsimd)]
 
         def round_x(i):
@@ -261,15 +262,19 @@ def tile_list_household_profile_cells_kernel(
             if i == 0:
                 fetch(parts(kept([P, blocks, FETCH], F32, "picked3", tag="x_bf0")))
 
-        def activate(i):
+        def activate(i, which="cg"):
             c = CHUNKS[i]
-            both = kept([P, 4 if i == 2 else 2, PACK * c], F32, "acts%d" % i, tag=("picked_last", "after_scatter", "x_bf0", "w1_raw0")[i])
+            both = acts[i] if i in acts else kept([P, 4 if i == 2 else 2, PACK * c], F32, "acts%d" % i, tag=("picked_last", "after_scatter", "x_bf0", "w1_raw0")[i])
+            acts[i] = both
             if i == 2:
                 y[0] = both[:, 2:4, :].rearrange("p g n -> p (g n)")
             cand[i] = both[:, 0, :]
             gate[i] = both[:, 1, :]
             for tag, into, lhs, func in (("c", cand[i], cand_lhs, ACT.Tanh), ("g", gate[i], gate_lhs, ACT.Sigmoid)):
-                for b, acc in enumerate(product(tag, 2, PACK, lhs, x_mx[i])):
+                if tag not in which:
+                    continue
+                ring_tag, depth = ("y", 4) if (tag, i) == ("g", 3) else (tag, 2)
+                for b, acc in enumerate(product(ring_tag, depth, PACK, lhs, x_mx[i])):
                     nc.scalar.activation(out=into[:, b * BANK : (b + 1) * BANK], in_=acc[:], func=func)
 
         def subtract(i):
@@ -324,14 +329,19 @@ def tile_list_household_profile_cells_kernel(
         for i in range(count):
             if i + 1 < count:
                 round_x(i + 1)
-            activate(i)
+                activate(i)
+        activate(count - 1, "c")
         for i in range(count):
             subtract(i)
             interpolate(i)
             project(i)
+            if i == 0:
+                activate(count - 1, "g")
         on_vector = groups * count - len(ROUND_ON_SCALAR)
-        late_tile = kept([P, on_vector, PACK * FETCH], BF16, "late", tag="z_bf%d" % (count - 1))
-        late = [late_tile[:, j, :] for j in range(on_vector)]
+        late_tile = kept([P, on_vector - groups, PACK * FETCH], BF16, "late", tag="z_bf%d" % (count - 1))
+        late = [late_tile[:, j, :] for j in range(on_vector - groups)]
+        sooner = kept([P, groups, PACK * FETCH], BF16, "sooner", tag="z_bf%d" % (count - 2))
+        late.extend([sooner[:, j, :] for j in range(groups)])
         for i in range(count):
             make_planes(i)
 

@@ -24,6 +24,8 @@ BANK = 512
 LIST = 16
 LINE = 4
 FETCH = 256
+PAIR = 2 * FETCH
+LATE = 14336
 CHUNKS = (256, 256, 256, 256)
 ROUND_ON_SCALAR = ((3, 0), (3, 1))
 
@@ -40,10 +42,14 @@ def tile_list_household_profile_cells_kernel(
     with ExitStack() as ctx:
         keep = ctx.enter_context(tc.tile_pool(name="keep", bufs=1))
         ring = ctx.enter_context(tc.tile_pool(name="ring", bufs=2))
+        table = ctx.enter_context(tc.tile_pool(name="table", bufs=1))
         psum = ctx.enter_context(tc.psum_pool(name="psum", bufs=2))
 
         def kept(shape, dtype, name, tag=""):
             return keep.tile(shape, dtype, name=name, tag=tag or name, align_bytes=64)
+
+        def placed(shape, dtype, name, offset):
+            return table.tile(shape, dtype, name=name, offset=offset, align_bytes=64)
 
         def entries(offsets, lo, hi):
             return offsets[:, lo // LIST : hi // LIST]
@@ -93,8 +99,14 @@ def tile_list_household_profile_cells_kernel(
 
         nc.sync.dma_start(idx[:], offs)
         load_scales(tab_sc, tab_scales)
+        wg_raw = kept([P, 2 * H], U8, "wg_raw")
+        nc.sync.dma_start(out=wg_raw[:].bitcast(I32), in_=wg_words[0].bitcast(I32))
         load_w1(0)
-        tab_w = [load_words(tab_words[a], "tab_w%d" % a) for a in range(passes)]
+        tab_w = []
+        for a in range(passes):
+            tile = placed([P, T], I32, "tab_w%d" % a, 4 * T * a)
+            nc.sync.dma_start(out=tile[:], in_=tab_words[a].rearrange("p c i -> p (c i)").bitcast(I32))
+            tab_w.append(tile)
         nc.sync.dma_start(idx2[:], offs2)
         wgs_sb = kept([P, S], F32, "wgs")
         nc.sync.dma_start(out=wgs_sb[:, 0:BANK], in_=wgs[:, 0:BANK])
@@ -109,17 +121,15 @@ def tile_list_household_profile_cells_kernel(
         nc.sync.dma_start(idx3[:], offs3)
         wc_raw = kept([P, PACK, H], F32, "wc_raw")
         nc.sync.dma_start(out=wc_raw[:], in_=wc.rearrange("(p j) c -> p j c", j=PACK))
-        wg_raw = kept([P, 2 * H], U8, "wg_raw")
-        nc.sync.dma_start(out=wg_raw[:].bitcast(I32), in_=wg_words[0].bitcast(I32))
         load_scales(w_sc_raw, wg_scales)
         gain_sb = kept([P, PACK], F32, "gain_sb")
         nc.sync.dma_start(out=gain_sb[:], in_=gain.rearrange("(p t) -> p t", t=PACK))
         load_scales(w_sc_raw, wo_scales[0].rearrange("r (g e) -> g r e", g=groups), first=4)
         wo_raw = load_words(wo_words[0], "wo_raw")
 
-        def quantize(values, name):
+        def quantize(values, name, tag=""):
             width = values.shape[1] // PACK
-            codes = kept([P, width], U32, name + "_q")
+            codes = kept([P, width], U32, name + "_q", tag=tag)
             scales = kept([P, width], U8, name + "_s")
             nc.vector.quantize_mx(out=codes[:].bitcast(FP8X4), scales=scales[:], in_=values)
             return codes, scales
@@ -135,11 +145,11 @@ def tile_list_household_profile_cells_kernel(
         v_sc = kept([P, S], U8, "v_sc")
         nc.vector.tensor_copy(out=v_sc[:], in_=tab_sc[:].indirect(idx[:]))
         v_w = {}
-        for lo in range(0, S, BANK):
-            for a in range(passes):
-                tile = kept([P, BANK], U32, "v_w%d_%d" % (a, lo))
-                nc.vector.tensor_copy(out=tile[:], in_=tab_w[a][:].bitcast(U32).indirect(entries(idx, lo, lo + BANK)))
-                v_w[a, lo] = tile
+        for a, lo, hi in ((0, 0, BANK), (1, 0, BANK), (0, BANK, S), (1, BANK, S)):
+            tile = kept([P, hi - lo], U32, "v_w%d_%d" % (a, lo))
+            nc.vector.tensor_copy(out=tile[:], in_=tab_w[a][:].bitcast(U32).indirect(entries(idx, lo, hi)))
+            for first in range(lo, hi, BANK):
+                v_w[a, first] = tile[:, first - lo : first - lo + BANK]
 
         for b in range(blocks):
             w1_q, w1_s = quantize_w1(b)
@@ -156,7 +166,7 @@ def tile_list_household_profile_cells_kernel(
                             out=acc[:],
                             lhsT=w1_q[:, a * P : (a + 1) * P].bitcast(FP8X4),
                             lhsT_scale=w1_s[:, a * P : (a + 1) * P],
-                            rhs=v_w[a, first][:].bitcast(FP8X4),
+                            rhs=v_w[a, first].bitcast(FP8X4),
                             rhs_scale=v_sc[4 * a : P, first : first + BANK],
                             start=(a == 0),
                             stop=(a == passes - 1),
@@ -181,7 +191,7 @@ def tile_list_household_profile_cells_kernel(
 
         picked_first = parts(kept([P, 3 * blocks - 1, FETCH], F32, "picked_first", tag="after_scatter"))
         fetch(picked_first[:blocks])
-        fetch(picked_first[blocks : 2 * blocks - 1] + [kept([P, FETCH], F32, "picked_last")[:]])
+        fetch(picked_first[blocks : 2 * blocks - 1] + [placed([P, FETCH], F32, "picked_last", LATE)[:]])
         fetch(picked_first[2 * blocks - 1 :])
 
         wc_bf = kept([P, PACK * H], BF16, "wc_bf")
@@ -204,7 +214,7 @@ def tile_list_household_profile_cells_kernel(
             )
             return dealt
 
-        w_s = deal(w_sc_raw, U8, "w_s")
+        w_s = []
 
         y_sc = kept([P, groups, M], U8, "y_sc")
         y_rows = out_0.rearrange("(g p t) m -> g p t m", p=P, t=PACK)
@@ -228,14 +238,14 @@ def tile_list_household_profile_cells_kernel(
             return banks
 
         def gate_lhs(t):
-            return wg_q[:, 2 * t * P : 2 * (t + 1) * P].bitcast(FP4X4), w_s[:, t * P : (t + 1) * P]
+            return wg_q[:, 2 * t * P : 2 * (t + 1) * P].bitcast(FP4X4), w_s[0][:, t * P : (t + 1) * P]
 
         def cand_lhs(t):
             return wc_q[:, t * P : (t + 1) * P].bitcast(FP8X4), wc_s[:, t * P : (t + 1) * P]
 
         def out_lhs(s):
             g, t = divmod(s, PACK)
-            return wo_q[0][:, s * P : (s + 1) * P].bitcast(FP8X4), w_s[4 + 4 * g : P, t * P : (t + 1) * P]
+            return wo_q[0][:, s * P : (s + 1) * P].bitcast(FP8X4), w_s[0][4 + 4 * g : P, t * P : (t + 1) * P]
 
         def woven(values):
             return values.rearrange("p (n i t) -> p n t i", i=LINE, t=PACK)
@@ -256,30 +266,34 @@ def tile_list_household_profile_cells_kernel(
 
         def round_x(i):
             c = CHUNKS[i]
-            x_bf = kept([P, PACK * c], BF16, "x_bf%d" % i)
+            x_bf = kept([P, PACK * c], BF16, "x_bf%d" % i, tag="x0_q" if i == 2 else "")
             nc.scalar.copy(out=woven(x_bf[:]), in_=by_lines(x_of(i)))
-            x_mx[i] = quantize(x_bf[:], "x%d" % i)
+            x_mx[i] = quantize(x_bf[:], "x%d" % i, tag="page3" if i == 2 else "")
             if i == 0:
-                fetch(parts(kept([P, blocks, FETCH], F32, "picked3", tag="x_bf0")))
+                w_s.append(deal(w_sc_raw, U8, "w_s", tag="x_bf0"))
 
-        def activate(i, which="cg"):
+        def activate(i, which):
             c = CHUNKS[i]
-            both = acts[i] if i in acts else kept([P, 4 if i == 2 else 2, PACK * c], F32, "acts%d" % i, tag=("picked_last", "after_scatter", "x_bf0", "w1_raw0")[i])
-            acts[i] = both
-            if i == 2:
-                y[0] = both[:, 2:4, :].rearrange("p g n -> p (g n)")
-            cand[i] = both[:, 0, :]
-            gate[i] = both[:, 1, :]
-            for tag, into, lhs, func in (("c", cand[i], cand_lhs, ACT.Tanh), ("g", gate[i], gate_lhs, ACT.Sigmoid)):
-                if tag not in which:
-                    continue
-                ring_tag, depth = ("y", 4) if (tag, i) == ("g", 3) else (tag, 2)
-                for b, acc in enumerate(product(ring_tag, depth, PACK, lhs, x_mx[i])):
-                    nc.scalar.activation(out=into[:, b * BANK : (b + 1) * BANK], in_=acc[:], func=func)
+            lhs, func, made = (cand_lhs, ACT.Tanh, cand) if which == "c" else (gate_lhs, ACT.Sigmoid, gate)
+            if (which, i) == ("g", 2):
+                into = placed([P, PACK * c], F32, "gate2", 8 * T)[:]
+            elif (which, i) == ("c", 0):
+                into = placed([P, PACK * c], F32, "cand0", LATE)[:]
+            elif i == 1:
+                if which == "c":
+                    acts[1] = kept([P, 2, PACK * c], F32, "acts1", tag="after_scatter")
+                into = acts[1][:, "cg".index(which), :]
+            else:
+                tag = {("g", 0): "x_bf1", ("c", 2): "w1_raw2", ("c", 3): "w1_raw3", ("g", 3): "w1_raw0"}[which, i]
+                into = kept([P, PACK * c], F32, "%s%d" % (which, i), tag=tag)[:]
+            made[i] = into
+            ring_tag, depth = ("y", 4) if i == 3 else (which, 2)
+            for b, acc in enumerate(product(ring_tag, depth, PACK, lhs, x_mx[i])):
+                nc.scalar.activation(out=into[:, b * BANK : (b + 1) * BANK], in_=acc[:], func=func)
 
         def subtract(i):
             c = CHUNKS[i]
-            steps[i] = kept([P, PACK * c], F32, "step%d" % i, tag=("page3", "page0", "page1", "page2")[i])
+            steps[i] = kept([P, PACK * c], F32, "step%d" % i, tag=("w1_raw1", "page0", "page1", "step_last")[i])
             for t in range(PACK):
                 nc.vector.scalar_tensor_tensor(
                     out=steps[i][:, t * c : (t + 1) * c], in0=cand[i][:, t * c : (t + 1) * c],
@@ -289,8 +303,12 @@ def tile_list_household_profile_cells_kernel(
         def interpolate(i):
             c = CHUNKS[i]
             step = steps[i]
-            nc.vector.tensor_tensor(out=step[:], in0=steps[i][:], in1=gate[i], op=ALU.mult)
-            z_bf = kept([P, PACK * c], BF16, "z_bf%d" % i, tag=("x_bf2", "x_bf3", "", "")[i])
+            if i == 0:
+                nc.gpsimd.tensor_tensor(out=step[:, c:], in0=step[:, c:], in1=gate[i][:, c:], op=ALU.mult)
+                nc.vector.tensor_tensor(out=step[:, :c], in0=step[:, :c], in1=gate[i][:, :c], op=ALU.mult)
+            else:
+                nc.vector.tensor_tensor(out=step[:], in0=steps[i][:], in1=gate[i], op=ALU.mult)
+            z_bf = kept([P, PACK * c], BF16, "z_bf%d" % i, tag=("x0_q", "x_bf3", "", "")[i])
             nc.vector.tensor_tensor(
                 out=woven(z_bf[:]),
                 in0=by_lines(step[:].rearrange("p (t n) -> p t n", t=PACK)),
@@ -301,8 +319,12 @@ def tile_list_household_profile_cells_kernel(
 
         def project(i):
             c = CHUNKS[i]
-            if i > 0:
-                y[i] = kept([P, groups * PACK * c], F32, "y%d" % i, tag=("", "tab_w0", "tab_w1", "wc_raw")[i])[:]
+            if i == 0:
+                y["pair"] = placed([P, 2, groups * PACK * c], F32, "y01", 0)
+            if i < 2:
+                y[i] = y["pair"][:, i, :]
+            else:
+                y[i] = kept([P, groups * PACK * c], F32, "y%d" % i, tag="wc_raw" if i == 2 else "")[:]
             flat = y[i]
             y[i] = flat.rearrange("p (g t n) -> p g t n", g=groups, t=PACK)
             for b, acc in enumerate(product("y", 4, groups * PACK, out_lhs, z[i])):
@@ -326,23 +348,36 @@ def tile_list_household_profile_cells_kernel(
 
         count = len(CHUNKS)
         round_x(0)
+        round_x(1)
+        activate(0, "c")
+        activate(0, "g")
+        subtract(0)
+        fetch(parts(placed([P, blocks, FETCH], F32, "picked3", LATE)))
+        round_x(2)
+        activate(1, "c")
+        activate(1, "g")
+        activate(2, "c")
+        round_x(3)
+        activate(2, "g")
         for i in range(count):
-            if i + 1 < count:
-                round_x(i + 1)
-                activate(i)
-        activate(count - 1, "c")
-        for i in range(count):
-            subtract(i)
+            if i > 0:
+                subtract(i)
             interpolate(i)
             project(i)
             if i == 0:
+                activate(count - 1, "c")
                 activate(count - 1, "g")
-        on_vector = groups * count - len(ROUND_ON_SCALAR)
-        late_tile = kept([P, on_vector - groups, PACK * FETCH], BF16, "late", tag="z_bf%d" % (count - 1))
-        late = [late_tile[:, j, :] for j in range(on_vector - groups)]
-        sooner = kept([P, groups, PACK * FETCH], BF16, "sooner", tag="z_bf%d" % (count - 2))
-        late.extend([sooner[:, j, :] for j in range(groups)])
-        for i in range(count):
+        late_pair = kept([P, groups + 1, PACK * PAIR], BF16, "late", tag="z_bf%d" % (count - 1))
+        both = y["pair"][:].rearrange("p c (g t n i) -> p g c n t i", g=groups, t=PACK, i=LINE)
+        for g in range(groups):
+            nc.vector.tensor_copy(
+                out=late_pair[:, g, :].rearrange("p (c n i t) -> p c n t i", c=2, i=LINE, t=PACK), in_=both[:, g]
+            )
+            y_q = kept([P, PAIR], I32, "y_q01_%d" % g)
+            nc.vector.quantize_mx(out=y_q[:].bitcast(FP8X4), scales=y_sc[:, g, 0:PAIR], in_=late_pair[:, g, :])
+            nc.sync.dma_start(out=y_words[:, g, 0:PAIR], in_=y_q[:])
+        late = [late_pair[:, groups, j * PACK * FETCH : (j + 1) * PACK * FETCH] for j in range(groups)]
+        for i in range(2, count):
             make_planes(i)
 
         for q in range(P // QUAD):

@@ -26,6 +26,7 @@ LINE = 4
 FETCH = 256
 PAIR = 2 * FETCH
 LATE = 14336
+SPARE = 20480
 CHUNKS = (256, 256, 256, 256)
 ROUND_ON_SCALAR = ((3, 0), (3, 1))
 
@@ -99,8 +100,6 @@ def tile_list_household_profile_cells_kernel(
 
         nc.sync.dma_start(idx[:], offs)
         load_scales(tab_sc, tab_scales)
-        wg_raw = kept([P, 2 * H], U8, "wg_raw")
-        nc.sync.dma_start(out=wg_raw[:].bitcast(I32), in_=wg_words[0].bitcast(I32))
         load_w1(0)
         tab_w = []
         for a in range(passes):
@@ -121,6 +120,8 @@ def tile_list_household_profile_cells_kernel(
         nc.sync.dma_start(idx3[:], offs3)
         wc_raw = kept([P, PACK, H], F32, "wc_raw")
         nc.sync.dma_start(out=wc_raw[:], in_=wc.rearrange("(p j) c -> p j c", j=PACK))
+        wg_raw = kept([P, 2 * H], U8, "wg_raw")
+        nc.sync.dma_start(out=wg_raw[:].bitcast(I32), in_=wg_words[0].bitcast(I32))
         load_scales(w_sc_raw, wg_scales)
         gain_sb = kept([P, PACK], F32, "gain_sb")
         nc.sync.dma_start(out=gain_sb[:], in_=gain.rearrange("(p t) -> p t", t=PACK))
@@ -200,14 +201,9 @@ def tile_list_household_profile_cells_kernel(
             in_=wc_raw[:].rearrange("p j (m t) -> p m j t", t=PACK),
         )
         wc_q, wc_s = quantize(wc_bf[:], "wc")
-        wg_q = kept([P, 2 * H], U8, "wg_q")
-        nc.vector.tensor_copy(
-            out=wg_q[:].rearrange("p (t m b) -> p m t b", t=PACK, b=2),
-            in_=wg_raw[:].rearrange("p (m t b) -> p m t b", t=PACK, b=2),
-        )
+        wg_q = []
 
-        def deal(raw, dtype, name, tag="", engine=nc.vector):
-            dealt = kept([P, raw.shape[1]], dtype, name, tag=tag)
+        def deal(raw, dealt, engine):
             engine.tensor_copy(
                 out=dealt[:].rearrange("p (g t m) -> p g m t", t=PACK, m=P),
                 in_=raw[:].rearrange("p (g m t) -> p g m t", t=PACK, m=P),
@@ -238,7 +234,7 @@ def tile_list_household_profile_cells_kernel(
             return banks
 
         def gate_lhs(t):
-            return wg_q[:, 2 * t * P : 2 * (t + 1) * P].bitcast(FP4X4), w_s[0][:, t * P : (t + 1) * P]
+            return wg_q[0][:, 2 * t * P : 2 * (t + 1) * P].bitcast(FP4X4), w_s[0][:, t * P : (t + 1) * P]
 
         def cand_lhs(t):
             return wc_q[:, t * P : (t + 1) * P].bitcast(FP8X4), wc_s[:, t * P : (t + 1) * P]
@@ -262,15 +258,23 @@ def tile_list_household_profile_cells_kernel(
         x_mx = {}
         steps = {}
         acts = {}
-        wo_q = [deal(wo_raw, I32, "wo_q", tag="wgs", engine=nc.gpsimd)]
+        wo_q = [deal(wo_raw, kept([P, N], I32, "wo_q", tag="wgs"), nc.gpsimd)]
 
         def round_x(i):
             c = CHUNKS[i]
-            x_bf = kept([P, PACK * c], BF16, "x_bf%d" % i, tag="x0_q" if i == 2 else "")
+            if i == 0:
+                x_bf = placed([P, PACK * c], BF16, "x_bf0", SPARE)
+            else:
+                x_bf = kept([P, PACK * c], BF16, "x_bf%d" % i, tag="x0_q" if i == 2 else "")
             nc.scalar.copy(out=woven(x_bf[:]), in_=by_lines(x_of(i)))
             x_mx[i] = quantize(x_bf[:], "x%d" % i, tag="page3" if i == 2 else "")
             if i == 0:
-                w_s.append(deal(w_sc_raw, U8, "w_s", tag="x_bf0"))
+                w_s.append(deal(w_sc_raw, placed([P, KP], U8, "w_s", SPARE), nc.vector))
+                wg_q.append(placed([P, 2 * H], U8, "wg_q", SPARE + KP))
+                nc.vector.tensor_copy(
+                    out=wg_q[0][:].rearrange("p (t m b) -> p m t b", t=PACK, b=2),
+                    in_=wg_raw[:].rearrange("p (m t b) -> p m t b", t=PACK, b=2),
+                )
 
         def activate(i, which):
             c = CHUNKS[i]
@@ -288,7 +292,9 @@ def tile_list_household_profile_cells_kernel(
                 into = kept([P, PACK * c], F32, "%s%d" % (which, i), tag=tag)[:]
             made[i] = into
             ring_tag, depth = ("y", 4) if i == 3 else (which, 2)
-            for b, acc in enumerate(product(ring_tag, depth, PACK, lhs, x_mx[i])):
+            turn = 2 if (which, i) == ("g", 0) else 0
+            for made_as, acc in enumerate(product(ring_tag, depth, PACK, lambda t: lhs((t + turn) % PACK), x_mx[i])):
+                b = (made_as + turn // 2) % 2
                 nc.scalar.activation(out=into[:, b * BANK : (b + 1) * BANK], in_=acc[:], func=func)
 
         def subtract(i):
@@ -304,7 +310,8 @@ def tile_list_household_profile_cells_kernel(
             c = CHUNKS[i]
             step = steps[i]
             if i == 0:
-                nc.gpsimd.tensor_tensor(out=step[:, c:], in0=step[:, c:], in1=gate[i][:, c:], op=ALU.mult)
+                for lo, hi in ((2 * c, 4 * c), (c, 2 * c)):
+                    nc.gpsimd.tensor_tensor(out=step[:, lo:hi], in0=step[:, lo:hi], in1=gate[i][:, lo:hi], op=ALU.mult)
                 nc.vector.tensor_tensor(out=step[:, :c], in0=step[:, :c], in1=gate[i][:, :c], op=ALU.mult)
             else:
                 nc.vector.tensor_tensor(out=step[:], in0=steps[i][:], in1=gate[i], op=ALU.mult)
@@ -329,8 +336,11 @@ def tile_list_household_profile_cells_kernel(
             y[i] = flat.rearrange("p (g t n) -> p g t n", g=groups, t=PACK)
             for b, acc in enumerate(product("y", 4, groups * PACK, out_lhs, z[i])):
                 nc.scalar.copy(out=flat[:, b * BANK : (b + 1) * BANK], in_=acc[:])
+            pieces = 2 if i == count - 1 else 1
             for g in range(groups):
-                nc.sync.dma_start(out=y_rows[g][:, :, starts[i] : starts[i] + c], in_=y[i][:, g, :, :])
+                for lo in range(0, PACK, PACK // pieces):
+                    ts = slice(lo, lo + PACK // pieces)
+                    nc.sync.dma_start(out=y_rows[g][:, ts, starts[i] : starts[i] + c], in_=y[i][:, g, ts, :])
 
         def make_planes(i):
             c = CHUNKS[i]
@@ -344,7 +354,10 @@ def tile_list_household_profile_cells_kernel(
                     y_bf = late.pop()
                     nc.vector.tensor_copy(out=woven(y_bf), in_=by_lines(y[i][:, g, :, :]))
                 nc.vector.quantize_mx(out=y_q[:, g, :].bitcast(FP8X4), scales=y_sc[:, g, cols], in_=y_bf)
-            nc.sync.dma_start(out=y_words[:, :, cols], in_=y_q[:])
+                if i == count - 1:
+                    nc.sync.dma_start(out=y_words[:, g, cols], in_=y_q[:, g, :])
+            if i < count - 1:
+                nc.sync.dma_start(out=y_words[:, :, cols], in_=y_q[:])
 
         count = len(CHUNKS)
         round_x(0)

@@ -28,7 +28,7 @@ PAIR = 2 * FETCH
 LATE = 14336
 SPARE = 20480
 CHUNKS = (256, 256, 256, 256)
-ROUND_ON_SCALAR = ((3, 0), (3, 1))
+ROUND_ON_SCALAR = ((2, 1), (3, 0), (3, 1))
 
 
 def tile_list_household_profile_cells_kernel(

@@ -23,11 +23,9 @@ QUAD = 32
 BANK = 512
 LIST = 16
 LINE = 4
-FETCH = 256
-PAIR = 2 * FETCH
-LATE = 14336
-SPARE = 20480
-CHUNKS = (256, 256, 256, 256)
+C = 256
+CHUNKS = M // C
+KB = 1024
 ROUND_ON_SCALAR = ((2, 1), (3, 0), (3, 1))
 
 
@@ -42,15 +40,14 @@ def tile_list_household_profile_cells_kernel(
 
     with ExitStack() as ctx:
         keep = ctx.enter_context(tc.tile_pool(name="keep", bufs=1))
-        ring = ctx.enter_context(tc.tile_pool(name="ring", bufs=2))
-        table = ctx.enter_context(tc.tile_pool(name="table", bufs=1))
+        arena = ctx.enter_context(tc.tile_pool(name="arena", bufs=1))
         psum = ctx.enter_context(tc.psum_pool(name="psum", bufs=2))
 
-        def kept(shape, dtype, name, tag=""):
-            return keep.tile(shape, dtype, name=name, tag=tag or name, align_bytes=64)
+        def kept(shape, dtype, name):
+            return keep.tile(shape, dtype, name=name, align_bytes=64)
 
         def placed(shape, dtype, name, offset):
-            return table.tile(shape, dtype, name=name, offset=offset, align_bytes=64)
+            return arena.tile(shape, dtype, name=name, offset=offset, align_bytes=64)
 
         def entries(offsets, lo, hi):
             return offsets[:, lo // LIST : hi // LIST]
@@ -79,64 +76,63 @@ def tile_list_household_profile_cells_kernel(
         nc.vector.memset(warm_in[:], 0.0)
         nc.scalar.activation(out=warm_out[:], in_=warm_in[:], func=ACT.Sigmoid)
 
+        AT_TAB, AT_W1, AT_V, AT_H, AT_WC, AT_WO, AT_WG, AT_W1BF = 0, 16 * KB, 32 * KB, 40 * KB, 56 * KB, 64 * KB, 68 * KB, 70 * KB
+        AT_WCBF, AT_WGS, AT_FREE = 78 * KB, 82 * KB, 86 * KB
+
         w1_raw = []
 
         def load_w1(b):
-            raw = kept([P, passes, PACK, P], F32, "w1_raw%d" % b)
+            raw = placed([P, passes, PACK, P], F32, "w1_raw%d" % b, AT_W1 + 4 * KB * b)
             for a in range(passes):
                 rows = w1[a * KP : (a + 1) * KP, b * P : (b + 1) * P]
                 nc.sync.dma_start(out=raw[:, a, :, :], in_=rows.rearrange("(p j) c -> p j c", j=PACK))
             w1_raw.append(raw)
 
-        def load_words(words, name):
-            tile = kept([P, words.shape[1]], I32, name)
+        def load_words(words, name, offset):
+            tile = placed([P, words.shape[1]], I32, name, offset)
             nc.sync.dma_start(out=tile[:], in_=words.rearrange("p c i -> p (c i)").bitcast(I32))
             return tile
 
-        def load_rows(rows, name):
-            tile = kept([P, rows.shape[1]], F32, name)
-            nc.sync.dma_start(out=tile[:], in_=rows)
+        def load_page(b):
+            tile = kept([P, T2], F32, "page%d" % b)
+            nc.sync.dma_start(out=tile[:], in_=page0[b * P : (b + 1) * P, :])
             return tile
 
         nc.sync.dma_start(idx[:], offs)
         load_scales(tab_sc, tab_scales)
         load_w1(0)
-        tab_w = []
-        for a in range(passes):
-            tile = placed([P, T], I32, "tab_w%d" % a, 4 * T * a)
-            nc.sync.dma_start(out=tile[:], in_=tab_words[a].rearrange("p c i -> p (c i)").bitcast(I32))
-            tab_w.append(tile)
+        tab_w = [load_words(tab_words[a], "tab_w%d" % a, AT_TAB + 4 * T * a) for a in range(passes)]
         nc.sync.dma_start(idx2[:], offs2)
-        wgs_sb = kept([P, S], F32, "wgs")
+        wgs_sb = placed([P, S], F32, "wgs", AT_WGS)
         nc.sync.dma_start(out=wgs_sb[:, 0:BANK], in_=wgs[:, 0:BANK])
-        page = [load_rows(page0[0:P, :], "page0")]
+        page = [load_page(0)]
         load_w1(1)
         load_w1(2)
         nc.sync.dma_start(out=wgs_sb[:, BANK:S], in_=wgs[:, BANK:S])
-        page.append(load_rows(page0[P : 2 * P, :], "page1"))
+        page.append(load_page(1))
         load_w1(3)
-        for b in range(2, blocks):
-            page.append(load_rows(page0[b * P : (b + 1) * P, :], "page%d" % b))
+        page.append(load_page(2))
+        page.append(load_page(3))
         nc.sync.dma_start(idx3[:], offs3)
-        wc_raw = kept([P, PACK, H], F32, "wc_raw")
+        wc_raw = placed([P, PACK, H], F32, "wc_raw", AT_WC)
         nc.sync.dma_start(out=wc_raw[:], in_=wc.rearrange("(p j) c -> p j c", j=PACK))
-        wg_raw = kept([P, 2 * H], U8, "wg_raw")
+        wg_raw = placed([P, H], U16, "wg_raw", AT_WG)
         nc.sync.dma_start(out=wg_raw[:].bitcast(I32), in_=wg_words[0].bitcast(I32))
         load_scales(w_sc_raw, wg_scales)
         gain_sb = kept([P, PACK], F32, "gain_sb")
         nc.sync.dma_start(out=gain_sb[:], in_=gain.rearrange("(p t) -> p t", t=PACK))
         load_scales(w_sc_raw, wo_scales[0].rearrange("r (g e) -> g r e", g=groups), first=4)
-        wo_raw = load_words(wo_words[0], "wo_raw")
+        wo_raw = load_words(wo_words[0], "wo_raw", AT_WO)
 
-        def quantize(values, name, tag=""):
+        def quantize(values, name, at=None):
             width = values.shape[1] // PACK
-            codes = kept([P, width], U32, name + "_q", tag=tag)
+            codes = kept([P, width], U32, name + "_q") if at is None else placed([P, width], U32, name + "_q", at)
             scales = kept([P, width], U8, name + "_s")
             nc.vector.quantize_mx(out=codes[:].bitcast(FP8X4), scales=scales[:], in_=values)
             return codes, scales
 
         def quantize_w1(b):
-            values = ring.tile([P, passes * P * PACK], BF16, name="w1_bf", align_bytes=64)
+            values = placed([P, passes * P * PACK], BF16, "w1_bf%d" % b, AT_W1BF + 2 * KB * (b % 2))
             nc.scalar.copy(
                 out=values[:].rearrange("p (a n i j) -> p a n j i", a=passes, i=LINE, j=PACK),
                 in_=w1_raw[b][:].rearrange("p a j (n i) -> p a n j i", i=LINE),
@@ -146,20 +142,19 @@ def tile_list_household_profile_cells_kernel(
         v_sc = kept([P, S], U8, "v_sc")
         nc.vector.tensor_copy(out=v_sc[:], in_=tab_sc[:].indirect(idx[:]))
         v_w = {}
-        for a, lo, hi in ((0, 0, BANK), (1, 0, BANK), (0, BANK, S), (1, BANK, S)):
-            tile = kept([P, hi - lo], U32, "v_w%d_%d" % (a, lo))
-            nc.vector.tensor_copy(out=tile[:], in_=tab_w[a][:].bitcast(U32).indirect(entries(idx, lo, hi)))
-            for first in range(lo, hi, BANK):
-                v_w[a, first] = tile[:, first - lo : first - lo + BANK]
+        for lo in range(0, S, BANK):
+            for a in range(passes):
+                v_w[a, lo] = placed([P, BANK], U32, "v_w%d_%d" % (a, lo), AT_V + 4 * (passes * lo + BANK * a))
+                nc.vector.tensor_copy(out=v_w[a, lo][:], in_=tab_w[a][:].bitcast(U32).indirect(entries(idx, lo, lo + BANK)))
 
+        h_count = []
         for b in range(blocks):
             w1_q, w1_s = quantize_w1(b)
             cuts = ((0, BANK), (BANK, S)) if b == 0 else ((0, S),)
             for lo, hi in cuts:
-                if b == blocks - 1:
-                    h = kept([P, S], F32, "h_last", tag="after_scatter")
-                else:
-                    h = ring.tile([P, hi - lo], F32, name="h", tag="h", bufs=3, align_bytes=64)
+                slot = 3 if b == blocks - 1 else len(h_count) % 3
+                h = placed([P, hi - lo], F32, "h%d" % len(h_count), AT_H + 4 * KB * slot)
+                h_count.append(h)
                 for first in range(lo, hi, BANK):
                     acc = psum.tile([P, BANK], F32, name="acc_h", tag="y", bufs=4)
                     for a in range(passes):
@@ -167,7 +162,7 @@ def tile_list_household_profile_cells_kernel(
                             out=acc[:],
                             lhsT=w1_q[:, a * P : (a + 1) * P].bitcast(FP8X4),
                             lhsT_scale=w1_s[:, a * P : (a + 1) * P],
-                            rhs=v_w[a, first].bitcast(FP8X4),
+                            rhs=v_w[a, first][:].bitcast(FP8X4),
                             rhs_scale=v_sc[4 * a : P, first : first + BANK],
                             start=(a == 0),
                             stop=(a == passes - 1),
@@ -177,71 +172,83 @@ def tile_list_household_profile_cells_kernel(
                     out=page[b][:].indirect(entries(idx2, lo, hi)), in0=h[:], in1=wgs_sb[:, lo:hi], op=ALU.mult
                 )
 
-        x = []
-
-        def fetch(picked):
-            lo = len(x) * FETCH
-            rows = kept([P, PACK, FETCH], F32, "x%d" % len(x))
-            for b in range(blocks):
-                nc.vector.tensor_copy(out=picked[b], in_=page[b][:].indirect(entries(idx3, lo, lo + FETCH)))
-                nc.sync.dma_start(out=rows[QUAD * b : QUAD * (b + 1), :, :], in_=picked[b])
-            x.append(rows)
-
-        def parts(tile):
-            return [tile[:, b, :] for b in range(tile.shape[1])]
-
-        picked_first = parts(kept([P, 3 * blocks - 1, FETCH], F32, "picked_first", tag="after_scatter"))
-        fetch(picked_first[:blocks])
-        fetch(picked_first[blocks : 2 * blocks - 1] + [placed([P, FETCH], F32, "picked_last", LATE)[:]])
-        fetch(picked_first[2 * blocks - 1 :])
-
-        wc_bf = kept([P, PACK * H], BF16, "wc_bf")
+        wc_bf = placed([P, PACK * H], BF16, "wc_bf", AT_WCBF)
         nc.scalar.copy(
             out=wc_bf[:].rearrange("p (t m j) -> p m j t", t=PACK, j=PACK),
             in_=wc_raw[:].rearrange("p j (m t) -> p m j t", t=PACK),
         )
-        wc_q, wc_s = quantize(wc_bf[:], "wc")
-        wg_q = []
 
-        def deal(raw, dealt, engine):
-            engine.tensor_copy(
-                out=dealt[:].rearrange("p (g t m) -> p g m t", t=PACK, m=P),
-                in_=raw[:].rearrange("p (g m t) -> p g m t", t=PACK, m=P),
+        def deal(raw, dealt, copy):
+            copy(
+                out=dealt.rearrange("p (g t m) -> p g t m", t=PACK, m=P),
+                in_=raw.rearrange("p (g m t) -> p g t m", t=PACK, m=P),
             )
-            return dealt
 
-        w_s = []
+        wg_q = kept([P, H], U16, "wg_q")
+        deal(wg_raw[:], wg_q[:], nc.scalar.copy)
+        wo_q = kept([P, N], U32, "wo_q")
+        deal(wo_raw[:].bitcast(U32), wo_q[:], nc.scalar.copy)
+        w_s = placed([P, KP], U8, "w_s", AT_WGS)
+        deal(w_sc_raw[:], w_s[:], nc.gpsimd.tensor_copy)
+
+        AT_X = AT_FREE
+        AT_PICK = AT_X + 16 * KB
+        AT_XBF0 = AT_PICK + 8 * KB
+        AT_GATE2 = AT_XBF0 + 4 * KB
+        AT_XQ0 = AT_GATE2 + 2 * KB
+        AT_PICK3 = AT_XQ0 + KB
+        AT_CAND0 = AT_XQ0 + 2 * KB
+        AT_Y0 = AT_PICK3 + KB
+        AT_STEP = AT_Y0 + 8 * KB
+        AT_GATE = AT_STEP + 16 * KB
+        AT_YBF = AT_GATE + 8 * KB
+        pick_at = (AT_PICK, AT_PICK + 4 * KB, AT_XBF0, AT_PICK3)
+        xbf_at = (AT_XBF0, AT_XQ0, AT_W1BF + 4 * KB, AT_W1BF + 6 * KB)
+        cand_at = ((AT_V, AT_CAND0), (AT_H, AT_H + 2 * KB), (AT_H + 4 * KB, AT_H + 6 * KB), (AT_H + 8 * KB, AT_H + 10 * KB))
+        y_at = (AT_Y0, AT_TAB + 8 * KB, AT_W1, AT_W1 + 8 * KB)
+        zbf_at = (xbf_at[2], xbf_at[3], AT_V + 4 * KB, AT_V + 6 * KB)
+        gate_at = (AT_GATE, pick_at[2], AT_GATE2, AT_GATE + 4 * KB)
+        ybf_at = (zbf_at[2], AT_STEP + 12 * KB, AT_STEP + 14 * KB)
+
+        x = []
+
+        def fetch():
+            i = len(x)
+            picked = placed([P, blocks, C], F32, "picked%d" % i, pick_at[i])
+            rows = placed([P, PACK, C], F32, "x%d" % i, AT_X + 4 * KB * i)
+            for b in range(blocks):
+                nc.vector.tensor_copy(out=picked[:, b, :], in_=page[b][:].indirect(entries(idx3, i * C, (i + 1) * C)))
+                nc.sync.dma_start(out=rows[QUAD * b : QUAD * (b + 1), :, :], in_=picked[:, b, :])
+            x.append(rows)
 
         y_sc = kept([P, groups, M], U8, "y_sc")
         y_rows = out_0.rearrange("(g p t) m -> g p t m", p=P, t=PACK)
         y_words = out_1.rearrange("g p m t -> p g (m t)").bitcast(I32)
-        starts = [sum(CHUNKS[:i]) for i in range(len(CHUNKS))]
 
-        def product(tag, bufs, count, lhs, rhs):
+        def product(tag, bufs, slices, lhs, rhs):
             codes, scales = rhs
-            c = codes.shape[1]
-            per_bank = BANK // c
+            per_bank = BANK // C
             banks = []
-            for first in range(0, count, per_bank):
+            for first in range(0, len(slices), per_bank):
                 acc = psum.tile([P, BANK], F32, name="acc_" + tag, tag=tag, bufs=bufs)
                 for s in range(per_bank):
-                    lhs_codes, lhs_scales = lhs(first + s)
+                    lhs_codes, lhs_scales = lhs(slices[first + s])
                     nc.tensor.matmul_mx(
-                        out=acc[:, s * c : (s + 1) * c], lhsT=lhs_codes, lhsT_scale=lhs_scales,
+                        out=acc[:, s * C : (s + 1) * C], lhsT=lhs_codes, lhsT_scale=lhs_scales,
                         rhs=codes[:].bitcast(FP8X4), rhs_scale=scales[:], start=True, stop=True,
                     )
                 banks.append(acc)
             return banks
 
         def gate_lhs(t):
-            return wg_q[0][:, 2 * t * P : 2 * (t + 1) * P].bitcast(FP4X4), w_s[0][:, t * P : (t + 1) * P]
+            return wg_q[:, t * P : (t + 1) * P].bitcast(FP4X4), w_s[:, t * P : (t + 1) * P]
 
         def cand_lhs(t):
             return wc_q[:, t * P : (t + 1) * P].bitcast(FP8X4), wc_s[:, t * P : (t + 1) * P]
 
         def out_lhs(s):
             g, t = divmod(s, PACK)
-            return wo_q[0][:, s * P : (s + 1) * P].bitcast(FP8X4), w_s[0][4 + 4 * g : P, t * P : (t + 1) * P]
+            return wo_q[:, s * P : (s + 1) * P].bitcast(FP8X4), w_s[4 + 4 * g : P, t * P : (t + 1) * P]
 
         def woven(values):
             return values.rearrange("p (n i t) -> p n t i", i=LINE, t=PACK)
@@ -249,149 +256,129 @@ def tile_list_household_profile_cells_kernel(
         def by_lines(planes):
             return planes.rearrange("p t (n i) -> p n t i", i=LINE)
 
-        def x_of(i):
-            lo = starts[i] % FETCH
-            return x[starts[i] // FETCH][:, :, lo : lo + CHUNKS[i]]
-
-        cand, gate, z, y = {}, {}, {}, {}
-
-        x_mx = {}
-        steps = {}
-        acts = {}
-        wo_q = [deal(wo_raw, kept([P, N], I32, "wo_q", tag="wgs"), nc.gpsimd)]
+        cand, gate, step, x_mx, z_in, z, y, y_in, y_q, x_in = {}, {}, {}, {}, {}, {}, {}, {}, {}, {}
 
         def round_x(i):
-            c = CHUNKS[i]
-            if i == 0:
-                x_bf = placed([P, PACK * c], BF16, "x_bf0", SPARE)
-            else:
-                x_bf = kept([P, PACK * c], BF16, "x_bf%d" % i, tag="x0_q" if i == 2 else "")
-            nc.scalar.copy(out=woven(x_bf[:]), in_=by_lines(x_of(i)))
-            x_mx[i] = quantize(x_bf[:], "x%d" % i, tag="page3" if i == 2 else "")
-            if i == 0:
-                w_s.append(deal(w_sc_raw, placed([P, KP], U8, "w_s", SPARE), nc.vector))
-                wg_q.append(placed([P, 2 * H], U8, "wg_q", SPARE + KP))
-                nc.vector.tensor_copy(
-                    out=wg_q[0][:].rearrange("p (t m b) -> p m t b", t=PACK, b=2),
-                    in_=wg_raw[:].rearrange("p (m t b) -> p m t b", t=PACK, b=2),
-                )
+            x_bf = placed([P, PACK * C], BF16, "x_bf%d" % i, xbf_at[i])
+            nc.scalar.copy(out=woven(x_bf[:]), in_=by_lines(x[i][:]))
+            x_in[i] = x_bf
 
-        def activate(i, which):
-            c = CHUNKS[i]
-            lhs, func, made = (cand_lhs, ACT.Tanh, cand) if which == "c" else (gate_lhs, ACT.Sigmoid, gate)
-            if (which, i) == ("g", 2):
-                into = placed([P, PACK * c], F32, "gate2", 8 * T)[:]
-            elif (which, i) == ("c", 0):
-                into = placed([P, PACK * c], F32, "cand0", LATE)[:]
-            elif i == 1:
-                if which == "c":
-                    acts[1] = kept([P, 2, PACK * c], F32, "acts1", tag="after_scatter")
-                into = acts[1][:, "cg".index(which), :]
-            else:
-                tag = {("g", 0): "x_bf1", ("c", 2): "w1_raw2", ("c", 3): "w1_raw3", ("g", 3): "w1_raw0"}[which, i]
-                into = kept([P, PACK * c], F32, "%s%d" % (which, i), tag=tag)[:]
-            made[i] = into
-            ring_tag, depth = ("y", 4) if i == 3 else (which, 2)
-            turn = 2 if (which, i) == ("g", 0) else 0
-            for made_as, acc in enumerate(product(ring_tag, depth, PACK, lambda t: lhs((t + turn) % PACK), x_mx[i])):
-                b = (made_as + turn // 2) % 2
-                nc.scalar.activation(out=into[:, b * BANK : (b + 1) * BANK], in_=acc[:], func=func)
+        def quantize_x(i):
+            x_mx[i] = quantize(x_in[i][:], "x%d" % i, at=AT_XQ0 if i == 0 else None)
 
-        def subtract(i):
-            c = CHUNKS[i]
-            steps[i] = kept([P, PACK * c], F32, "step%d" % i, tag=("w1_raw1", "page0", "page1", "step_last")[i])
-            for t in range(PACK):
+        def candidate(i):
+            cand[i] = []
+            tag, depth = ("y", 4) if i == CHUNKS - 1 else ("c", 2)
+            for b, acc in enumerate(product(tag, depth, range(PACK), cand_lhs, x_mx[i])):
+                half = placed([P, BANK], F32, "cand%d_%d" % (i, b), cand_at[i][b])
+                nc.scalar.activation(out=half[:], in_=acc[:], func=ACT.Tanh)
+                cand[i].append(half)
+
+        def gating(i):
+            gate[i] = placed([P, PACK * C], F32, "gate%d" % i, gate_at[i])
+            tag, depth = ("y", 4) if i == CHUNKS - 1 else ("g", 2)
+            for b, acc in enumerate(product(tag, depth, range(PACK), gate_lhs, x_mx[i])):
+                nc.scalar.activation(out=gate[i][:, b * BANK : (b + 1) * BANK], in_=acc[:], func=ACT.Sigmoid)
+
+        def subtract(i, slices):
+            if i not in step:
+                step[i] = placed([P, PACK * C], F32, "step%d" % i, AT_STEP + 4 * KB * i)
+            for t in slices:
                 nc.vector.scalar_tensor_tensor(
-                    out=steps[i][:, t * c : (t + 1) * c], in0=cand[i][:, t * c : (t + 1) * c],
-                    scalar=gain_sb[:, t : t + 1], in1=x_of(i)[:, t, :], op0=ALU.mult, op1=ALU.subtract,
+                    out=step[i][:, t * C : (t + 1) * C], in0=cand[i][t // 2][:, (t % 2) * C : (t % 2 + 1) * C],
+                    scalar=gain_sb[:, t : t + 1], in1=x[i][:, t, :], op0=ALU.mult, op1=ALU.subtract,
                 )
+
+        def gate_step(i, engine, lo, hi):
+            engine.tensor_tensor(out=step[i][:, lo:hi], in0=step[i][:, lo:hi], in1=gate[i][:, lo:hi], op=ALU.mult)
 
         def interpolate(i):
-            c = CHUNKS[i]
-            step = steps[i]
-            if i == 0:
-                for lo, hi in ((2 * c, 4 * c), (c, 2 * c)):
-                    nc.gpsimd.tensor_tensor(out=step[:, lo:hi], in0=step[:, lo:hi], in1=gate[i][:, lo:hi], op=ALU.mult)
-                nc.vector.tensor_tensor(out=step[:, :c], in0=step[:, :c], in1=gate[i][:, :c], op=ALU.mult)
-            else:
-                nc.vector.tensor_tensor(out=step[:], in0=steps[i][:], in1=gate[i], op=ALU.mult)
-            z_bf = kept([P, PACK * c], BF16, "z_bf%d" % i, tag=("x0_q", "x_bf3", "", "")[i])
+            z_bf = placed([P, PACK * C], BF16, "z_bf%d" % i, zbf_at[i])
             nc.vector.tensor_tensor(
                 out=woven(z_bf[:]),
-                in0=by_lines(step[:].rearrange("p (t n) -> p t n", t=PACK)),
-                in1=by_lines(x_of(i)),
+                in0=by_lines(step[i][:].rearrange("p (t n) -> p t n", t=PACK)),
+                in1=by_lines(x[i][:]),
                 op=ALU.add,
             )
-            z[i] = quantize(z_bf[:], "z%d" % i)
+            z_in[i] = z_bf
 
         def project(i):
-            c = CHUNKS[i]
-            if i == 0:
-                y["pair"] = placed([P, 2, groups * PACK * c], F32, "y01", 0)
-            if i < 2:
-                y[i] = y["pair"][:, i, :]
-            else:
-                y[i] = kept([P, groups * PACK * c], F32, "y%d" % i, tag="wc_raw" if i == 2 else "")[:]
-            flat = y[i]
-            y[i] = flat.rearrange("p (g t n) -> p g t n", g=groups, t=PACK)
-            for b, acc in enumerate(product("y", 4, groups * PACK, out_lhs, z[i])):
+            z[i] = quantize(z_in[i][:], "z%d" % i)
+            flat = placed([P, groups * PACK * C], F32, "y%d" % i, y_at[i])
+            y[i] = flat[:].rearrange("p (g t n) -> p g t n", g=groups, t=PACK)
+            for b, acc in enumerate(product("y", 4, range(groups * PACK), out_lhs, z[i])):
                 nc.scalar.copy(out=flat[:, b * BANK : (b + 1) * BANK], in_=acc[:])
-            pieces = 2 if i == count - 1 else 1
+            pieces = 2 if i == CHUNKS - 1 else 1
             for g in range(groups):
                 for lo in range(0, PACK, PACK // pieces):
                     ts = slice(lo, lo + PACK // pieces)
-                    nc.sync.dma_start(out=y_rows[g][:, ts, starts[i] : starts[i] + c], in_=y[i][:, g, ts, :])
+                    nc.sync.dma_start(out=y_rows[g][:, ts, i * C : (i + 1) * C], in_=y[i][:, g, ts, :])
 
-        def make_planes(i):
-            c = CHUNKS[i]
-            cols = slice(starts[i], starts[i] + c)
-            y_q = kept([P, groups, c], I32, "y_q%d" % i)
-            for g in range(groups):
-                if (i, g) in ROUND_ON_SCALAR:
-                    y_bf = kept([P, PACK * c], BF16, "y_bf%d_%d" % (i, g))[:]
-                    nc.scalar.copy(out=woven(y_bf), in_=by_lines(y[i][:, g, :, :]))
-                else:
-                    y_bf = late.pop()
-                    nc.vector.tensor_copy(out=woven(y_bf), in_=by_lines(y[i][:, g, :, :]))
-                nc.vector.quantize_mx(out=y_q[:, g, :].bitcast(FP8X4), scales=y_sc[:, g, cols], in_=y_bf)
-                if i == count - 1:
-                    nc.sync.dma_start(out=y_words[:, g, cols], in_=y_q[:, g, :])
-            if i < count - 1:
-                nc.sync.dma_start(out=y_words[:, :, cols], in_=y_q[:])
+        def round_y(i, g):
+            if (i, g) in ROUND_ON_SCALAR:
+                y_in[i, g] = placed([P, PACK * C], BF16, "y_bf%d_%d" % (i, g), AT_YBF + 2 * KB * (2 * i + g - 5))
+                nc.scalar.copy(out=woven(y_in[i, g][:]), in_=by_lines(y[i][:, g, :, :]))
+            else:
+                y_in[i, g] = placed([P, PACK * C], BF16, "y_bf%d_%d" % (i, g), ybf_at[(groups * i + g) % 3])
+                nc.vector.tensor_copy(out=woven(y_in[i, g][:]), in_=by_lines(y[i][:, g, :, :]))
 
-        count = len(CHUNKS)
+        def quantize_y(i, g):
+            cols = slice(i * C, (i + 1) * C)
+            if g == 0:
+                y_q[i] = kept([P, groups, C], I32, "y_q%d" % i)
+            nc.vector.quantize_mx(out=y_q[i][:, g, :].bitcast(FP8X4), scales=y_sc[:, g, cols], in_=y_in[i, g][:])
+            if i == CHUNKS - 1:
+                nc.sync.dma_start(out=y_words[:, g, cols], in_=y_q[i][:, g, :])
+            elif g == groups - 1:
+                nc.sync.dma_start(out=y_words[:, :, cols], in_=y_q[i][:])
+
+        fetch()
+        fetch()
+        wc_q, wc_s = quantize(wc_bf[:], "wc")
         round_x(0)
+        quantize_x(0)
+        fetch()
+        candidate(0)
         round_x(1)
-        activate(0, "c")
-        activate(0, "g")
-        subtract(0)
-        fetch(parts(placed([P, blocks, FETCH], F32, "picked3", LATE)))
+        gating(0)
+        subtract(0, (2, 3))
+        quantize_x(1)
+        subtract(0, (0, 1))
+        fetch()
+        gate_step(0, nc.gpsimd, C, PACK * C)
+        candidate(1)
         round_x(2)
-        activate(1, "c")
-        activate(1, "g")
-        activate(2, "c")
+        quantize_x(2)
+        gating(1)
+        gate_step(0, nc.vector, 0, C)
+        subtract(1, (0, 1))
+        interpolate(0)
+        subtract(1, (2, 3))
+        candidate(2)
         round_x(3)
-        activate(2, "g")
-        for i in range(count):
-            if i > 0:
-                subtract(i)
+        gating(2)
+        project(0)
+        quantize_x(3)
+        candidate(3)
+        gating(3)
+        for i in range(1, CHUNKS - 1):
+            gate_step(i, nc.vector, 0, PACK * C)
+            subtract(i + 1, (0, 1))
             interpolate(i)
+            subtract(i + 1, (2, 3))
             project(i)
-            if i == 0:
-                activate(count - 1, "c")
-                activate(count - 1, "g")
-        late_pair = kept([P, groups + 1, PACK * PAIR], BF16, "late", tag="z_bf%d" % (count - 1))
-        both = y["pair"][:].rearrange("p c (g t n i) -> p g c n t i", g=groups, t=PACK, i=LINE)
-        for g in range(groups):
-            nc.vector.tensor_copy(
-                out=late_pair[:, g, :].rearrange("p (c n i t) -> p c n t i", c=2, i=LINE, t=PACK), in_=both[:, g]
-            )
-            y_q = kept([P, PAIR], I32, "y_q01_%d" % g)
-            nc.vector.quantize_mx(out=y_q[:].bitcast(FP8X4), scales=y_sc[:, g, 0:PAIR], in_=late_pair[:, g, :])
-            nc.sync.dma_start(out=y_words[:, g, 0:PAIR], in_=y_q[:])
-        late = [late_pair[:, groups, j * PACK * FETCH : (j + 1) * PACK * FETCH] for j in range(groups)]
-        for i in range(2, count):
-            make_planes(i)
+        last = CHUNKS - 1
+        gate_step(last, nc.vector, 0, PACK * C)
+        round_y(0, 0)
+        interpolate(last)
+        quantize_y(0, 0)
+        project(last)
+        planes = [(i, g) for i in range(CHUNKS) for g in range(groups)][1:]
+        round_y(*planes[0])
+        for done, ahead in zip(planes, planes[1:]):
+            round_y(*ahead)
+            quantize_y(*done)
+        quantize_y(*planes[-1])
 
         for q in range(P // QUAD):
             nc.sync.dma_start(

@@ -26,7 +26,7 @@ LINE = 4
 C = 256
 CHUNKS = M // C
 KB = 1024
-ROUND_ON_SCALAR = ((2, 1), (3, 0), (3, 1))
+ROUND_ON_SCALAR = ((2, 0), (3, 0), (3, 1))
 
 
 def tile_list_household_profile_cells_kernel(
@@ -113,16 +113,16 @@ def tile_list_household_profile_cells_kernel(
         load_w1(3)
         page.append(load_page(2))
         page.append(load_page(3))
-        nc.sync.dma_start(idx3[:], offs3)
-        wc_raw = placed([P, PACK, H], F32, "wc_raw", AT_WC)
-        nc.sync.dma_start(out=wc_raw[:], in_=wc.rearrange("(p j) c -> p j c", j=PACK))
+        wo_raw = load_words(wo_words[0], "wo_raw", AT_WO)
         wg_raw = placed([P, H], U16, "wg_raw", AT_WG)
         nc.sync.dma_start(out=wg_raw[:].bitcast(I32), in_=wg_words[0].bitcast(I32))
         load_scales(w_sc_raw, wg_scales)
+        load_scales(w_sc_raw, wo_scales[0].rearrange("r (g e) -> g r e", g=groups), first=4)
         gain_sb = kept([P, PACK], F32, "gain_sb")
         nc.sync.dma_start(out=gain_sb[:], in_=gain.rearrange("(p t) -> p t", t=PACK))
-        load_scales(w_sc_raw, wo_scales[0].rearrange("r (g e) -> g r e", g=groups), first=4)
-        wo_raw = load_words(wo_words[0], "wo_raw", AT_WO)
+        wc_raw = placed([P, PACK, H], F32, "wc_raw", AT_WC)
+        nc.sync.dma_start(out=wc_raw[:], in_=wc.rearrange("(p j) c -> p j c", j=PACK))
+        nc.sync.dma_start(idx3[:], offs3)
 
         def quantize(values, name, at=None):
             width = values.shape[1] // PACK
@@ -193,33 +193,38 @@ def tile_list_household_profile_cells_kernel(
 
         AT_X = AT_FREE
         AT_PICK = AT_X + 16 * KB
-        AT_XBF0 = AT_PICK + 8 * KB
-        AT_GATE2 = AT_XBF0 + 4 * KB
-        AT_XQ0 = AT_GATE2 + 2 * KB
-        AT_PICK3 = AT_XQ0 + KB
-        AT_CAND0 = AT_XQ0 + 2 * KB
-        AT_Y0 = AT_PICK3 + KB
-        AT_STEP = AT_Y0 + 8 * KB
-        AT_GATE = AT_STEP + 16 * KB
-        AT_YBF = AT_GATE + 8 * KB
-        pick_at = (AT_PICK, AT_PICK + 4 * KB, AT_XBF0, AT_PICK3)
-        xbf_at = (AT_XBF0, AT_XQ0, AT_W1BF + 4 * KB, AT_W1BF + 6 * KB)
-        cand_at = ((AT_V, AT_CAND0), (AT_H, AT_H + 2 * KB), (AT_H + 4 * KB, AT_H + 6 * KB), (AT_H + 8 * KB, AT_H + 10 * KB))
-        y_at = (AT_Y0, AT_TAB + 8 * KB, AT_W1, AT_W1 + 8 * KB)
-        zbf_at = (xbf_at[2], xbf_at[3], AT_V + 4 * KB, AT_V + 6 * KB)
-        gate_at = (AT_GATE, pick_at[2], AT_GATE2, AT_GATE + 4 * KB)
-        ybf_at = (zbf_at[2], AT_STEP + 12 * KB, AT_STEP + 14 * KB)
+        LANE_A = AT_PICK + 9 * KB
+        LANE_B = LANE_A + 4 * KB
+        LANE_C = LANE_B + KB
+        LANE_D = LANE_C + 16 * KB
+        LANE_E = LANE_D + 2 * KB
+        LANE_F = LANE_E + 2 * KB
+        LANE_G = LANE_F + 4 * KB
+        LANE_H = LANE_G + 4 * KB
+        AT_STEP = LANE_H + 4 * KB
+        pick_at = (((0, 4, AT_PICK),), ((0, 4, AT_PICK + 4 * KB),), ((0, 1, AT_PICK + 8 * KB), (1, 4, LANE_A)), ((0, 4, LANE_C),))
+        xbf_at = (LANE_A, LANE_B, LANE_E, LANE_D)
+        xq_at = (LANE_B, None, LANE_D, None)
+        cand_at = ((AT_V, LANE_C + KB), (AT_H, AT_H + 2 * KB), (AT_H + 4 * KB, AT_H + 6 * KB), (AT_H + 8 * KB, AT_H + 10 * KB))
+        y_at = (LANE_C, None, AT_W1, AT_W1 + 8 * KB)
+        zbf_at = (LANE_E, LANE_D, LANE_G, AT_V + 2 * KB)
+        gate_at = (LANE_F, LANE_A, AT_WC, AT_WC + 4 * KB)
+        step_at = (AT_STEP, LANE_F, AT_STEP + 4 * KB, LANE_H)
+        ybf_at = {
+            (0, 0): LANE_G, (0, 1): LANE_H,
+            (2, 0): AT_TAB + 8 * KB, (2, 1): LANE_G, (3, 0): AT_TAB + 12 * KB, (3, 1): AT_TAB + 10 * KB,
+        }
 
-        x = []
+        x, picked = {}, {}
 
-        def fetch():
-            i = len(x)
-            picked = placed([P, blocks, C], F32, "picked%d" % i, pick_at[i])
-            rows = placed([P, PACK, C], F32, "x%d" % i, AT_X + 4 * KB * i)
-            for b in range(blocks):
-                nc.vector.tensor_copy(out=picked[:, b, :], in_=page[b][:].indirect(entries(idx3, i * C, (i + 1) * C)))
-                nc.sync.dma_start(out=rows[QUAD * b : QUAD * (b + 1), :, :], in_=picked[:, b, :])
-            x.append(rows)
+        def fetch(i, part):
+            lo, hi, at = pick_at[i][part]
+            picked[i] = placed([P, hi - lo, C], F32, "picked%d_%d" % (i, part), at)
+            if lo == 0:
+                x[i] = placed([P, PACK, C], F32, "x%d" % i, AT_X + 4 * KB * i)
+            for b in range(lo, hi):
+                nc.vector.tensor_copy(out=picked[i][:, b - lo, :], in_=page[b][:].indirect(entries(idx3, i * C, (i + 1) * C)))
+                nc.sync.dma_start(out=x[i][QUAD * b : QUAD * (b + 1), :, :], in_=picked[i][:, b - lo, :])
 
         y_sc = kept([P, groups, M], U8, "y_sc")
         y_rows = out_0.rearrange("(g p t) m -> g p t m", p=P, t=PACK)
@@ -264,15 +269,15 @@ def tile_list_household_profile_cells_kernel(
             x_in[i] = x_bf
 
         def quantize_x(i):
-            x_mx[i] = quantize(x_in[i][:], "x%d" % i, at=AT_XQ0 if i == 0 else None)
+            x_mx[i] = quantize(x_in[i][:], "x%d" % i, at=xq_at[i])
 
-        def candidate(i):
-            cand[i] = []
+        def candidate(i, halves=(0, 1)):
+            cand[i] = {}
             tag, depth = ("y", 4) if i == CHUNKS - 1 else ("c", 2)
-            for b, acc in enumerate(product(tag, depth, range(PACK), cand_lhs, x_mx[i])):
-                half = placed([P, BANK], F32, "cand%d_%d" % (i, b), cand_at[i][b])
-                nc.scalar.activation(out=half[:], in_=acc[:], func=ACT.Tanh)
-                cand[i].append(half)
+            slices = [2 * b + s for b in halves for s in range(2)]
+            for b, acc in zip(halves, product(tag, depth, slices, cand_lhs, x_mx[i])):
+                cand[i][b] = placed([P, BANK], F32, "cand%d_%d" % (i, b), cand_at[i][b])
+                nc.scalar.activation(out=cand[i][b][:], in_=acc[:], func=ACT.Tanh)
 
         def gating(i):
             gate[i] = placed([P, PACK * C], F32, "gate%d" % i, gate_at[i])
@@ -282,7 +287,7 @@ def tile_list_household_profile_cells_kernel(
 
         def subtract(i, slices):
             if i not in step:
-                step[i] = placed([P, PACK * C], F32, "step%d" % i, AT_STEP + 4 * KB * i)
+                step[i] = placed([P, PACK * C], F32, "step%d" % i, step_at[i])
             for t in slices:
                 nc.vector.scalar_tensor_tensor(
                     out=step[i][:, t * C : (t + 1) * C], in0=cand[i][t // 2][:, (t % 2) * C : (t % 2 + 1) * C],
@@ -302,83 +307,105 @@ def tile_list_household_profile_cells_kernel(
             )
             z_in[i] = z_bf
 
-        def project(i):
+        def quantize_z(i):
             z[i] = quantize(z_in[i][:], "z%d" % i)
-            flat = placed([P, groups * PACK * C], F32, "y%d" % i, y_at[i])
-            y[i] = flat[:].rearrange("p (g t n) -> p g t n", g=groups, t=PACK)
-            for b, acc in enumerate(product("y", 4, range(groups * PACK), out_lhs, z[i])):
-                nc.scalar.copy(out=flat[:, b * BANK : (b + 1) * BANK], in_=acc[:])
+            if i == 0:
+                y["pair"] = placed([P, 2, groups, PACK, C], F32, "y01", y_at[0])
+            y[i] = y["pair"][:, i] if i < 2 else placed([P, groups, PACK, C], F32, "y%d" % i, y_at[i])[:]
+
+        def project(i, g):
+            for b, acc in enumerate(product("y", 4, range(g * PACK, (g + 1) * PACK), out_lhs, z[i])):
+                nc.scalar.copy(out=y[i][:, g, 2 * b : 2 * b + 2, :].rearrange("p t n -> p (t n)"), in_=acc[:])
             pieces = 2 if i == CHUNKS - 1 else 1
-            for g in range(groups):
-                for lo in range(0, PACK, PACK // pieces):
-                    ts = slice(lo, lo + PACK // pieces)
-                    nc.sync.dma_start(out=y_rows[g][:, ts, i * C : (i + 1) * C], in_=y[i][:, g, ts, :])
+            for lo in range(0, PACK, PACK // pieces):
+                ts = slice(lo, lo + PACK // pieces)
+                nc.sync.dma_start(out=y_rows[g][:, ts, i * C : (i + 1) * C], in_=y[i][:, g, ts, :])
 
         def round_y(i, g):
-            if (i, g) in ROUND_ON_SCALAR:
-                y_in[i, g] = placed([P, PACK * C], BF16, "y_bf%d_%d" % (i, g), AT_YBF + 2 * KB * (2 * i + g - 5))
-                nc.scalar.copy(out=woven(y_in[i, g][:]), in_=by_lines(y[i][:, g, :, :]))
+            if i == 0:
+                y_in[i, g] = placed([P, 2 * PACK * C], BF16, "y_bf01_%d" % g, ybf_at[i, g])
+                nc.vector.tensor_copy(
+                    out=y_in[i, g][:].rearrange("p (c n i t) -> p c n t i", c=2, i=LINE, t=PACK),
+                    in_=y["pair"][:, :, g].rearrange("p c t (n i) -> p c n t i", i=LINE),
+                )
             else:
-                y_in[i, g] = placed([P, PACK * C], BF16, "y_bf%d_%d" % (i, g), ybf_at[(groups * i + g) % 3])
-                nc.vector.tensor_copy(out=woven(y_in[i, g][:]), in_=by_lines(y[i][:, g, :, :]))
+                y_in[i, g] = placed([P, PACK * C], BF16, "y_bf%d_%d" % (i, g), ybf_at[i, g])
+                copy = nc.scalar.copy if (i, g) in ROUND_ON_SCALAR else nc.vector.tensor_copy
+                copy(out=woven(y_in[i, g][:]), in_=by_lines(y[i][:, g, :, :]))
 
         def quantize_y(i, g):
-            cols = slice(i * C, (i + 1) * C)
-            if g == 0:
-                y_q[i] = kept([P, groups, C], I32, "y_q%d" % i)
-            nc.vector.quantize_mx(out=y_q[i][:, g, :].bitcast(FP8X4), scales=y_sc[:, g, cols], in_=y_in[i, g][:])
-            if i == CHUNKS - 1:
-                nc.sync.dma_start(out=y_words[:, g, cols], in_=y_q[i][:, g, :])
-            elif g == groups - 1:
-                nc.sync.dma_start(out=y_words[:, :, cols], in_=y_q[i][:])
+            width = y_in[i, g].shape[1] // PACK
+            cols = slice(i * C, i * C + width)
+            codes = kept([P, width], I32, "y_q%d_%d" % (i, g))
+            nc.vector.quantize_mx(out=codes[:].bitcast(FP8X4), scales=y_sc[:, g, cols], in_=y_in[i, g][:])
+            nc.sync.dma_start(out=y_words[:, g, cols], in_=codes[:])
 
-        fetch()
-        fetch()
+        def gate_halves(i):
+            gate_step(i, nc.vector, 0, 2 * C)
+            gate_step(i, nc.vector, 2 * C, PACK * C)
+
+        def project_all(i):
+            for g in range(groups):
+                project(i, g)
+
+        fetch(0, 0)
+        fetch(1, 0)
         wc_q, wc_s = quantize(wc_bf[:], "wc")
+        fetch(2, 0)
         round_x(0)
         quantize_x(0)
-        fetch()
+        fetch(2, 1)
         candidate(0)
         round_x(1)
         gating(0)
         subtract(0, (2, 3))
         quantize_x(1)
         subtract(0, (0, 1))
-        fetch()
-        gate_step(0, nc.gpsimd, C, PACK * C)
+        fetch(3, 0)
+        gate_step(0, nc.gpsimd, 0, PACK * C)
         candidate(1)
         round_x(2)
-        quantize_x(2)
         gating(1)
-        gate_step(0, nc.vector, 0, C)
-        subtract(1, (0, 1))
+        quantize_x(2)
         interpolate(0)
+        subtract(1, (0, 1))
+        quantize_z(0)
         subtract(1, (2, 3))
         candidate(2)
-        round_x(3)
         gating(2)
-        project(0)
+        round_x(3)
+        project_all(0)
+        gate_halves(1)
+        subtract(2, (0, 1))
         quantize_x(3)
         candidate(3)
         gating(3)
-        for i in range(1, CHUNKS - 1):
-            gate_step(i, nc.vector, 0, PACK * C)
-            subtract(i + 1, (0, 1))
-            interpolate(i)
-            subtract(i + 1, (2, 3))
-            project(i)
-        last = CHUNKS - 1
-        gate_step(last, nc.vector, 0, PACK * C)
+        interpolate(1)
+        subtract(2, (2, 3))
+        quantize_z(1)
+        project_all(1)
+        gate_step(2, nc.vector, 0, PACK * C)
+        subtract(3, (0, 1))
+        interpolate(2)
+        subtract(3, (2, 3))
+        quantize_z(2)
+        project_all(2)
+        round_y(2, 0)
+        gate_step(3, nc.vector, 0, PACK * C)
         round_y(0, 0)
-        interpolate(last)
+        interpolate(3)
         quantize_y(0, 0)
-        project(last)
-        planes = [(i, g) for i in range(CHUNKS) for g in range(groups)][1:]
-        round_y(*planes[0])
-        for done, ahead in zip(planes, planes[1:]):
-            round_y(*ahead)
-            quantize_y(*done)
-        quantize_y(*planes[-1])
+        quantize_z(3)
+        project_all(3)
+        round_y(0, 1)
+        round_y(2, 1)
+        quantize_y(0, 1)
+        quantize_y(2, 0)
+        quantize_y(2, 1)
+        round_y(3, 0)
+        round_y(3, 1)
+        quantize_y(3, 0)
+        quantize_y(3, 1)
 
         for q in range(P // QUAD):
             nc.sync.dma_start(

@@ -194,7 +194,8 @@ def tile_list_household_profile_cells_kernel(
         AT_X = AT_FREE
         AT_PICK = AT_X + 16 * KB
         LANE_A = AT_PICK + 9 * KB
-        LANE_B = LANE_A + 4 * KB
+        LANE_P = LANE_A + 4 * KB
+        LANE_B = LANE_P + 3 * KB
         LANE_C = LANE_B + KB
         LANE_D = LANE_C + 16 * KB
         LANE_E = LANE_D + 2 * KB
@@ -208,14 +209,14 @@ def tile_list_household_profile_cells_kernel(
         cand_at = ((AT_V, LANE_C + KB), (AT_H, AT_H + 2 * KB), (AT_H + 4 * KB, AT_H + 6 * KB), (AT_H + 8 * KB, AT_H + 10 * KB))
         y_at = (LANE_C, None, AT_W1, AT_W1 + 8 * KB)
         zbf_at = (LANE_E, LANE_D, LANE_G, AT_V + 2 * KB)
-        gate_at = (LANE_F, LANE_A, AT_WC, AT_WC + 4 * KB)
-        step_at = (AT_STEP, LANE_F, AT_STEP + 4 * KB, LANE_H)
+        gate_at = (AT_PICK + 4 * KB, LANE_A, AT_WC, AT_WC + 4 * KB)
+        step_at = (AT_STEP, gate_at[0], AT_STEP + 4 * KB, LANE_H)
         ybf_at = {
             (0, 0): LANE_G, (0, 1): LANE_H,
             (2, 0): AT_TAB + 8 * KB, (2, 1): LANE_G, (3, 0): AT_TAB + 12 * KB, (3, 1): AT_TAB + 10 * KB,
         }
 
-        x, picked = {}, {}
+        x, picked, gated = {}, {}, {}
 
         def fetch(i, part):
             lo, hi, at = pick_at[i][part]
@@ -279,10 +280,11 @@ def tile_list_household_profile_cells_kernel(
                 cand[i][b] = placed([P, BANK], F32, "cand%d_%d" % (i, b), cand_at[i][b])
                 nc.scalar.activation(out=cand[i][b][:], in_=acc[:], func=ACT.Tanh)
 
-        def gating(i):
+        def gating(i, halves=(0, 1)):
             gate[i] = placed([P, PACK * C], F32, "gate%d" % i, gate_at[i])
             tag, depth = ("y", 4) if i == CHUNKS - 1 else ("g", 2)
-            for b, acc in enumerate(product(tag, depth, range(PACK), gate_lhs, x_mx[i])):
+            slices = [2 * b + s for b in halves for s in range(2)]
+            for b, acc in zip(halves, product(tag, depth, slices, gate_lhs, x_mx[i])):
                 nc.scalar.activation(out=gate[i][:, b * BANK : (b + 1) * BANK], in_=acc[:], func=ACT.Sigmoid)
 
         def subtract(i, slices):
@@ -295,13 +297,15 @@ def tile_list_household_profile_cells_kernel(
                 )
 
         def gate_step(i, engine, lo, hi):
-            engine.tensor_tensor(out=step[i][:, lo:hi], in0=step[i][:, lo:hi], in1=gate[i][:, lo:hi], op=ALU.mult)
+            if i not in gated:
+                gated[i] = placed([P, PACK * C], F32, "gated0", LANE_P) if i == 0 else step[i]
+            engine.tensor_tensor(out=gated[i][:, lo:hi], in0=step[i][:, lo:hi], in1=gate[i][:, lo:hi], op=ALU.mult)
 
         def interpolate(i):
             z_bf = placed([P, PACK * C], BF16, "z_bf%d" % i, zbf_at[i])
             nc.vector.tensor_tensor(
                 out=woven(z_bf[:]),
-                in0=by_lines(step[i][:].rearrange("p (t n) -> p t n", t=PACK)),
+                in0=by_lines(gated[i][:].rearrange("p (t n) -> p t n", t=PACK)),
                 in1=by_lines(x[i][:]),
                 op=ALU.add,
             )
@@ -357,15 +361,17 @@ def tile_list_household_profile_cells_kernel(
         fetch(2, 1)
         candidate(0)
         round_x(1)
-        gating(0)
+        gating(0, (1, 0))
         subtract(0, (2, 3))
         quantize_x(1)
         subtract(0, (0, 1))
         fetch(3, 0)
-        gate_step(0, nc.gpsimd, 0, PACK * C)
+        gate_step(0, nc.gpsimd, 2 * C, PACK * C)
+        gate_step(0, nc.gpsimd, C, 2 * C)
         candidate(1)
         round_x(2)
         gating(1)
+        gate_step(0, nc.vector, 0, C)
         quantize_x(2)
         interpolate(0)
         subtract(1, (0, 1))

@@ -113,16 +113,16 @@ def tile_list_household_profile_cells_kernel(
         load_w1(3)
         page.append(load_page(2))
         page.append(load_page(3))
-        wo_raw = load_words(wo_words[0], "wo_raw", AT_WO)
+        nc.sync.dma_start(idx3[:], offs3)
+        wc_raw = placed([P, PACK, H], F32, "wc_raw", AT_WC)
+        nc.sync.dma_start(out=wc_raw[:], in_=wc.rearrange("(p j) c -> p j c", j=PACK))
         wg_raw = placed([P, H], U16, "wg_raw", AT_WG)
         nc.sync.dma_start(out=wg_raw[:].bitcast(I32), in_=wg_words[0].bitcast(I32))
         load_scales(w_sc_raw, wg_scales)
-        load_scales(w_sc_raw, wo_scales[0].rearrange("r (g e) -> g r e", g=groups), first=4)
         gain_sb = kept([P, PACK], F32, "gain_sb")
         nc.sync.dma_start(out=gain_sb[:], in_=gain.rearrange("(p t) -> p t", t=PACK))
-        wc_raw = placed([P, PACK, H], F32, "wc_raw", AT_WC)
-        nc.sync.dma_start(out=wc_raw[:], in_=wc.rearrange("(p j) c -> p j c", j=PACK))
-        nc.sync.dma_start(idx3[:], offs3)
+        load_scales(w_sc_raw, wo_scales[0].rearrange("r (g e) -> g r e", g=groups), first=4)
+        wo_raw = load_words(wo_words[0], "wo_raw", AT_WO)
 
         def quantize(values, name, at=None):
             width = values.shape[1] // PACK
@@ -203,7 +203,7 @@ def tile_list_household_profile_cells_kernel(
         LANE_G = LANE_F + 4 * KB
         LANE_H = LANE_G + 4 * KB
         AT_STEP = LANE_H + 4 * KB
-        pick_at = (((0, 4, AT_PICK),), ((0, 4, AT_PICK + 4 * KB),), ((0, 1, AT_PICK + 8 * KB), (1, 4, LANE_A)), ((0, 4, LANE_C),))
+        pick_at = (((0, 4, AT_PICK),), ((0, 4, AT_PICK + 4 * KB),), ((0, 4, LANE_A),), ((0, 4, LANE_C),))
         xbf_at = (LANE_A, LANE_B, LANE_E, LANE_D)
         xq_at = (LANE_B, None, LANE_D, None)
         cand_at = ((AT_V, LANE_C + KB), (AT_H, AT_H + 2 * KB), (AT_H + 4 * KB, AT_H + 6 * KB), (AT_H + 8 * KB, AT_H + 10 * KB))
@@ -212,7 +212,7 @@ def tile_list_household_profile_cells_kernel(
         gate_at = (AT_PICK + 4 * KB, LANE_A, AT_WC, AT_WC + 4 * KB)
         step_at = (AT_STEP, gate_at[0], AT_STEP + 4 * KB, LANE_H)
         ybf_at = {
-            (0, 0): LANE_G, (0, 1): LANE_H,
+            (0, 0): gate_at[3], (0, 1): LANE_H,
             (2, 0): AT_TAB + 8 * KB, (2, 1): LANE_G, (3, 0): AT_TAB + 12 * KB, (3, 1): AT_TAB + 10 * KB,
         }
 
@@ -348,6 +348,25 @@ def tile_list_household_profile_cells_kernel(
             gate_step(i, nc.vector, 0, 2 * C)
             gate_step(i, nc.vector, 2 * C, PACK * C)
 
+        def finish_in_halves(i):
+            halves = [slice(lo, lo + C // 2) for lo in (0, C // 2)]
+            planes = step[i][:].rearrange("p (t n) -> p t n", t=PACK)
+            gates = gate[i][:].rearrange("p (t n) -> p t n", t=PACK)
+            z_bf = placed([P, PACK * C], BF16, "z_bf%d" % i, zbf_at[i])
+            z[i] = kept([P, C], U32, "z%d_q" % i), kept([P, C], U8, "z%d_s" % i)
+            y[i] = placed([P, groups, PACK, C], F32, "y%d" % i, y_at[i])[:]
+            for n in halves:
+                nc.vector.tensor_tensor(out=planes[:, :, n], in0=planes[:, :, n], in1=gates[:, :, n], op=ALU.mult)
+            for n in halves:
+                nc.vector.tensor_tensor(
+                    out=woven(z_bf[:, PACK * n.start : PACK * n.stop]),
+                    in0=by_lines(planes[:, :, n]), in1=by_lines(x[i][:, :, n]), op=ALU.add,
+                )
+            for n in halves:
+                nc.vector.quantize_mx(
+                    out=z[i][0][:, n].bitcast(FP8X4), scales=z[i][1][:, n], in_=z_bf[:, PACK * n.start : PACK * n.stop]
+                )
+
         def project_all(i):
             for g in range(groups):
                 project(i, g)
@@ -355,10 +374,9 @@ def tile_list_household_profile_cells_kernel(
         fetch(0, 0)
         fetch(1, 0)
         wc_q, wc_s = quantize(wc_bf[:], "wc")
-        fetch(2, 0)
         round_x(0)
         quantize_x(0)
-        fetch(2, 1)
+        fetch(2, 0)
         candidate(0)
         round_x(1)
         gating(0, (1, 0))
@@ -397,15 +415,13 @@ def tile_list_household_profile_cells_kernel(
         quantize_z(2)
         project_all(2)
         round_y(2, 0)
-        gate_step(3, nc.vector, 0, PACK * C)
-        round_y(0, 0)
-        interpolate(3)
-        quantize_y(0, 0)
-        quantize_z(3)
+        finish_in_halves(3)
         project_all(3)
+        round_y(0, 0)
         round_y(0, 1)
-        round_y(2, 1)
+        quantize_y(0, 0)
         quantize_y(0, 1)
+        round_y(2, 1)
         quantize_y(2, 0)
         quantize_y(2, 1)
         round_y(3, 0)

@@ -26,7 +26,7 @@ LINE = 4
 C = 256
 CHUNKS = M // C
 KB = 1024
-ROUND_ON_SCALAR = ((2, 0), (3, 0), (3, 1))
+ROUND_ON_SCALAR = ((2, 1), (3, 0), (3, 1))
 
 
 def tile_list_household_profile_cells_kernel(
@@ -197,8 +197,9 @@ def tile_list_household_profile_cells_kernel(
         LANE_P = LANE_A + 4 * KB
         LANE_B = LANE_P + 3 * KB
         LANE_C = LANE_B + KB
-        LANE_D = LANE_C + 16 * KB
-        LANE_E = LANE_D + 2 * KB
+        LANE_Z = LANE_C + 8 * KB
+        LANE_D = LANE_Z + KB
+        LANE_E = LANE_D + 3 * KB
         LANE_F = LANE_E + 2 * KB
         LANE_G = LANE_F + 4 * KB
         LANE_H = LANE_G + 4 * KB
@@ -206,17 +207,17 @@ def tile_list_household_profile_cells_kernel(
         pick_at = (((0, 4, AT_PICK),), ((0, 4, AT_PICK + 4 * KB),), ((0, 4, LANE_A),), ((0, 4, LANE_C),))
         xbf_at = (LANE_A, LANE_B, LANE_E, LANE_D)
         xq_at = (LANE_B, None, LANE_D, None)
-        cand_at = ((AT_V, LANE_C + KB), (AT_H, AT_H + 2 * KB), (AT_H + 4 * KB, AT_H + 6 * KB), (AT_H + 8 * KB, AT_H + 10 * KB))
-        y_at = (LANE_C, None, AT_W1, AT_W1 + 8 * KB)
-        zbf_at = (LANE_E, LANE_D, LANE_G, AT_V + 2 * KB)
+        cand_at = ((LANE_C + KB, AT_V), (AT_H, AT_H + 2 * KB), (AT_H + 4 * KB, AT_H + 6 * KB), (AT_H + 8 * KB, AT_H + 10 * KB))
+        y_at = (LANE_C, AT_TAB, AT_W1, AT_W1 + 8 * KB)
+        zbf_at = (LANE_E, LANE_Z, LANE_G, AT_V + 2 * KB)
         gate_at = (AT_PICK + 4 * KB, LANE_A, AT_WC, AT_WC + 4 * KB)
         step_at = (AT_STEP, gate_at[0], AT_STEP + 4 * KB, LANE_H)
         ybf_at = {
-            (0, 0): gate_at[3], (0, 1): LANE_H,
-            (2, 0): AT_TAB + 8 * KB, (2, 1): LANE_G, (3, 0): AT_TAB + 12 * KB, (3, 1): AT_TAB + 10 * KB,
+            (0, 0): LANE_G, (0, 1): LANE_H, (1, 0): LANE_H + 2 * KB, (1, 1): LANE_G,
+            (2, 0): LANE_H, (2, 1): AT_TAB + 8 * KB, (3, 0): AT_TAB + 12 * KB, (3, 1): AT_TAB + 10 * KB,
         }
 
-        x, picked, gated = {}, {}, {}
+        x, picked, gated, upper = {}, {}, {}, {}
 
         def fetch(i, part):
             lo, hi, at = pick_at[i][part]
@@ -290,16 +291,18 @@ def tile_list_household_profile_cells_kernel(
         def subtract(i, slices):
             if i not in step:
                 step[i] = placed([P, PACK * C], F32, "step%d" % i, step_at[i])
+            if (i, slices[0]) == (2, 2):
+                upper[i] = placed([P, 2 * C], F32, "upper2", LANE_D + KB)
             for t in slices:
                 nc.vector.scalar_tensor_tensor(
-                    out=step[i][:, t * C : (t + 1) * C], in0=cand[i][t // 2][:, (t % 2) * C : (t % 2 + 1) * C],
+                    out=upper[i][:, (t - 2) * C : (t - 1) * C] if i in upper else step[i][:, t * C : (t + 1) * C], in0=cand[i][t // 2][:, (t % 2) * C : (t % 2 + 1) * C],
                     scalar=gain_sb[:, t : t + 1], in1=x[i][:, t, :], op0=ALU.mult, op1=ALU.subtract,
                 )
 
         def gate_step(i, engine, lo, hi):
             if i not in gated:
                 gated[i] = placed([P, PACK * C], F32, "gated0", LANE_P) if i == 0 else step[i]
-            engine.tensor_tensor(out=gated[i][:, lo:hi], in0=step[i][:, lo:hi], in1=gate[i][:, lo:hi], op=ALU.mult)
+            engine.tensor_tensor(out=gated[i][:, lo:hi], in0=upper[i][:] if i in upper and lo > 0 else step[i][:, lo:hi], in1=gate[i][:, lo:hi], op=ALU.mult)
 
         def interpolate(i):
             z_bf = placed([P, PACK * C], BF16, "z_bf%d" % i, zbf_at[i])
@@ -313,9 +316,7 @@ def tile_list_household_profile_cells_kernel(
 
         def quantize_z(i):
             z[i] = quantize(z_in[i][:], "z%d" % i)
-            if i == 0:
-                y["pair"] = placed([P, 2, groups, PACK, C], F32, "y01", y_at[0])
-            y[i] = y["pair"][:, i] if i < 2 else placed([P, groups, PACK, C], F32, "y%d" % i, y_at[i])[:]
+            y[i] = placed([P, groups, PACK, C], F32, "y%d" % i, y_at[i])[:]
 
         def project(i, g):
             for b, acc in enumerate(product("y", 4, range(g * PACK, (g + 1) * PACK), out_lhs, z[i])):
@@ -326,46 +327,24 @@ def tile_list_household_profile_cells_kernel(
                 nc.sync.dma_start(out=y_rows[g][:, ts, i * C : (i + 1) * C], in_=y[i][:, g, ts, :])
 
         def round_y(i, g):
-            if i == 0:
-                y_in[i, g] = placed([P, 2 * PACK * C], BF16, "y_bf01_%d" % g, ybf_at[i, g])
-                nc.vector.tensor_copy(
-                    out=y_in[i, g][:].rearrange("p (c n i t) -> p c n t i", c=2, i=LINE, t=PACK),
-                    in_=y["pair"][:, :, g].rearrange("p c t (n i) -> p c n t i", i=LINE),
-                )
-            else:
-                y_in[i, g] = placed([P, PACK * C], BF16, "y_bf%d_%d" % (i, g), ybf_at[i, g])
-                copy = nc.scalar.copy if (i, g) in ROUND_ON_SCALAR else nc.vector.tensor_copy
-                copy(out=woven(y_in[i, g][:]), in_=by_lines(y[i][:, g, :, :]))
+            y_in[i, g] = placed([P, PACK * C], BF16, "y_bf%d_%d" % (i, g), ybf_at[i, g])
+            copy = nc.scalar.copy if (i, g) in ROUND_ON_SCALAR else nc.vector.tensor_copy
+            copy(out=woven(y_in[i, g][:]), in_=by_lines(y[i][:, g, :, :]))
 
         def quantize_y(i, g):
-            width = y_in[i, g].shape[1] // PACK
-            cols = slice(i * C, i * C + width)
-            codes = kept([P, width], I32, "y_q%d_%d" % (i, g))
-            nc.vector.quantize_mx(out=codes[:].bitcast(FP8X4), scales=y_sc[:, g, cols], in_=y_in[i, g][:])
-            nc.sync.dma_start(out=y_words[:, g, cols], in_=codes[:])
+            cols = slice(i * C, (i + 1) * C)
+            if g == 0:
+                y_q[i] = kept([P, groups, C], I32, "y_q%d" % i)
+            codes = y_q[i][:, g, :]
+            nc.vector.quantize_mx(out=codes.bitcast(FP8X4), scales=y_sc[:, g, cols], in_=y_in[i, g][:])
+            if i == CHUNKS - 1:
+                nc.sync.dma_start(out=y_words[:, g, cols], in_=codes)
+            elif g == groups - 1:
+                nc.sync.dma_start(out=y_words[:, :, cols], in_=y_q[i][:])
 
         def gate_halves(i):
             gate_step(i, nc.vector, 0, 2 * C)
             gate_step(i, nc.vector, 2 * C, PACK * C)
-
-        def finish_in_halves(i):
-            halves = [slice(lo, lo + C // 2) for lo in (0, C // 2)]
-            planes = step[i][:].rearrange("p (t n) -> p t n", t=PACK)
-            gates = gate[i][:].rearrange("p (t n) -> p t n", t=PACK)
-            z_bf = placed([P, PACK * C], BF16, "z_bf%d" % i, zbf_at[i])
-            z[i] = kept([P, C], U32, "z%d_q" % i), kept([P, C], U8, "z%d_s" % i)
-            y[i] = placed([P, groups, PACK, C], F32, "y%d" % i, y_at[i])[:]
-            for n in halves:
-                nc.vector.tensor_tensor(out=planes[:, :, n], in0=planes[:, :, n], in1=gates[:, :, n], op=ALU.mult)
-            for n in halves:
-                nc.vector.tensor_tensor(
-                    out=woven(z_bf[:, PACK * n.start : PACK * n.stop]),
-                    in0=by_lines(planes[:, :, n]), in1=by_lines(x[i][:, :, n]), op=ALU.add,
-                )
-            for n in halves:
-                nc.vector.quantize_mx(
-                    out=z[i][0][:, n].bitcast(FP8X4), scales=z[i][1][:, n], in_=z_bf[:, PACK * n.start : PACK * n.stop]
-                )
 
         def project_all(i):
             for g in range(groups):
@@ -377,12 +356,12 @@ def tile_list_household_profile_cells_kernel(
         round_x(0)
         quantize_x(0)
         fetch(2, 0)
-        candidate(0)
+        candidate(0, (1, 0))
         round_x(1)
         gating(0, (1, 0))
-        subtract(0, (2, 3))
-        quantize_x(1)
         subtract(0, (0, 1))
+        quantize_x(1)
+        subtract(0, (2, 3))
         fetch(3, 0)
         gate_step(0, nc.gpsimd, 2 * C, PACK * C)
         gate_step(0, nc.gpsimd, C, 2 * C)
@@ -408,26 +387,25 @@ def tile_list_household_profile_cells_kernel(
         subtract(2, (2, 3))
         quantize_z(1)
         project_all(1)
-        gate_step(2, nc.vector, 0, PACK * C)
+        gate_halves(2)
         subtract(3, (0, 1))
         interpolate(2)
         subtract(3, (2, 3))
         quantize_z(2)
         project_all(2)
-        round_y(2, 0)
-        finish_in_halves(3)
-        project_all(3)
+        last = CHUNKS - 1
+        gate_step(last, nc.vector, 0, PACK * C)
         round_y(0, 0)
-        round_y(0, 1)
+        interpolate(last)
         quantize_y(0, 0)
-        quantize_y(0, 1)
-        round_y(2, 1)
-        quantize_y(2, 0)
-        quantize_y(2, 1)
-        round_y(3, 0)
-        round_y(3, 1)
-        quantize_y(3, 0)
-        quantize_y(3, 1)
+        quantize_z(last)
+        project_all(last)
+        planes = [(i, g) for i in range(CHUNKS) for g in range(groups)][1:]
+        round_y(*planes[0])
+        for done, ahead in zip(planes, planes[1:]):
+            round_y(*ahead)
+            quantize_y(*done)
+        quantize_y(*planes[-1])
 
         for q in range(P // QUAD):
             nc.sync.dma_start(

@@ -26,7 +26,8 @@ LINE = 4
 C = 256
 CHUNKS = M // C
 KB = 1024
-ROUND_ON_SCALAR = ((2, 1), (3, 0), (3, 1))
+SHARED = (3, 0)
+ROUND_ON_SCALAR = ((2, 1), (3, 1))
 
 
 def tile_list_household_profile_cells_kernel(
@@ -199,19 +200,19 @@ def tile_list_household_profile_cells_kernel(
         LANE_C = LANE_B + KB
         LANE_Z = LANE_C + 8 * KB
         LANE_D = LANE_Z + KB
-        LANE_E = LANE_D + 3 * KB
-        LANE_F = LANE_E + 2 * KB
+        LANE_E = LANE_D + 4 * KB
+        LANE_F = LANE_E + 3 * KB
         LANE_G = LANE_F + 4 * KB
         LANE_H = LANE_G + 4 * KB
         AT_STEP = LANE_H + 4 * KB
-        pick_at = (((0, 4, AT_PICK),), ((0, 4, AT_PICK + 4 * KB),), ((0, 4, LANE_A),), ((0, 4, LANE_C),))
+        pick_at = (((0, 4, AT_PICK),), ((0, 4, AT_PICK + 4 * KB),), ((0, 1, AT_PICK + 8 * KB), (1, 4, LANE_A)), ((0, 4, LANE_C),))
         xbf_at = (LANE_A, LANE_B, LANE_E, LANE_D)
-        xq_at = (LANE_B, None, LANE_D, None)
+        xq_at = (None, None, LANE_D, None)
         cand_at = ((LANE_C + KB, AT_V), (AT_H, AT_H + 2 * KB), (AT_H + 4 * KB, AT_H + 6 * KB), (AT_H + 8 * KB, AT_H + 10 * KB))
         y_at = (LANE_C, AT_TAB, AT_W1, AT_W1 + 8 * KB)
-        zbf_at = (LANE_E, LANE_Z, LANE_G, AT_V + 2 * KB)
-        gate_at = (AT_PICK + 4 * KB, LANE_A, AT_WC, AT_WC + 4 * KB)
-        step_at = (AT_STEP, gate_at[0], AT_STEP + 4 * KB, LANE_H)
+        zbf_at = (LANE_E - KB, LANE_Z, LANE_G, AT_V + 2 * KB)
+        gate_at = (LANE_F, LANE_A, AT_WC, AT_WC + 4 * KB)
+        step_at = (AT_PICK + 4 * KB, gate_at[0], AT_STEP + 4 * KB, LANE_H)
         ybf_at = {
             (0, 0): LANE_G, (0, 1): LANE_H, (1, 0): LANE_H + 2 * KB, (1, 1): LANE_G,
             (2, 0): LANE_H, (2, 1): AT_TAB + 8 * KB, (3, 0): AT_TAB + 12 * KB, (3, 1): AT_TAB + 10 * KB,
@@ -267,7 +268,8 @@ def tile_list_household_profile_cells_kernel(
 
         def round_x(i):
             x_bf = placed([P, PACK * C], BF16, "x_bf%d" % i, xbf_at[i])
-            nc.scalar.copy(out=woven(x_bf[:]), in_=by_lines(x[i][:]))
+            copy = nc.vector.tensor_copy if i == 1 else nc.scalar.copy
+            copy(out=woven(x_bf[:]), in_=by_lines(x[i][:]))
             x_in[i] = x_bf
 
         def quantize_x(i):
@@ -291,8 +293,8 @@ def tile_list_household_profile_cells_kernel(
         def subtract(i, slices):
             if i not in step:
                 step[i] = placed([P, PACK * C], F32, "step%d" % i, step_at[i])
-            if (i, slices[0]) == (2, 2):
-                upper[i] = placed([P, 2 * C], F32, "upper2", LANE_D + KB)
+            if i in (1, 2) and slices[0] == 2:
+                upper[i] = placed([P, 2 * C], F32, "upper%d" % i, xbf_at[i + 1] + KB)
             for t in slices:
                 nc.vector.scalar_tensor_tensor(
                     out=upper[i][:, (t - 2) * C : (t - 1) * C] if i in upper else step[i][:, t * C : (t + 1) * C], in0=cand[i][t // 2][:, (t % 2) * C : (t % 2 + 1) * C],
@@ -328,8 +330,15 @@ def tile_list_household_profile_cells_kernel(
 
         def round_y(i, g):
             y_in[i, g] = placed([P, PACK * C], BF16, "y_bf%d_%d" % (i, g), ybf_at[i, g])
-            copy = nc.scalar.copy if (i, g) in ROUND_ON_SCALAR else nc.vector.tensor_copy
-            copy(out=woven(y_in[i, g][:]), in_=by_lines(y[i][:, g, :, :]))
+            if (i, g) == SHARED:
+                for copy, lo in ((nc.vector.tensor_copy, 0), (nc.scalar.copy, C // 2)):
+                    copy(
+                        out=woven(y_in[i, g][:, PACK * lo : PACK * (lo + C // 2)]),
+                        in_=by_lines(y[i][:, g, :, lo : lo + C // 2]),
+                    )
+            else:
+                copy = nc.scalar.copy if (i, g) in ROUND_ON_SCALAR else nc.vector.tensor_copy
+                copy(out=woven(y_in[i, g][:]), in_=by_lines(y[i][:, g, :, :]))
 
         def quantize_y(i, g):
             cols = slice(i * C, (i + 1) * C)
@@ -353,9 +362,10 @@ def tile_list_household_profile_cells_kernel(
         fetch(0, 0)
         fetch(1, 0)
         wc_q, wc_s = quantize(wc_bf[:], "wc")
+        fetch(2, 0)
         round_x(0)
         quantize_x(0)
-        fetch(2, 0)
+        fetch(2, 1)
         candidate(0, (1, 0))
         round_x(1)
         gating(0, (1, 0))
@@ -369,11 +379,11 @@ def tile_list_household_profile_cells_kernel(
         round_x(2)
         gating(1)
         gate_step(0, nc.vector, 0, C)
+        subtract(1, (0, 1))
         quantize_x(2)
         interpolate(0)
-        subtract(1, (0, 1))
-        quantize_z(0)
         subtract(1, (2, 3))
+        quantize_z(0)
         candidate(2)
         gating(2)
         round_x(3)

@@ -27,7 +27,7 @@ C = 256
 CHUNKS = M // C
 KB = 1024
 SHARED = (3, 0)
-ROUND_ON_SCALAR = ((2, 1), (3, 1))
+ROUND_ON_SCALAR = ((0, 0), (2, 1), (3, 1))
 
 
 def tile_list_household_profile_cells_kernel(
@@ -198,24 +198,24 @@ def tile_list_household_profile_cells_kernel(
         LANE_P = LANE_A + 4 * KB
         LANE_B = LANE_P + 3 * KB
         LANE_C = LANE_B + KB
-        LANE_Z = LANE_C + 8 * KB
+        LANE_Z = LANE_C + 12 * KB
         LANE_D = LANE_Z + KB
         LANE_E = LANE_D + 4 * KB
         LANE_F = LANE_E + 3 * KB
         LANE_G = LANE_F + 4 * KB
-        LANE_H = LANE_G + 4 * KB
+        LANE_H = LANE_G + 5 * KB
         AT_STEP = LANE_H + 4 * KB
         pick_at = (((0, 4, AT_PICK),), ((0, 4, AT_PICK + 4 * KB),), ((0, 1, AT_PICK + 8 * KB), (1, 4, LANE_A)), ((0, 4, LANE_C),))
         xbf_at = (LANE_A, LANE_B, LANE_E, LANE_D)
-        xq_at = (None, None, LANE_D, None)
+        xq_at = (None, None, None, AT_TAB + 14 * KB)
         cand_at = ((LANE_C + KB, AT_V), (AT_H, AT_H + 2 * KB), (AT_H + 4 * KB, AT_H + 6 * KB), (AT_H + 8 * KB, AT_H + 10 * KB))
-        y_at = (LANE_C, AT_TAB, AT_W1, AT_W1 + 8 * KB)
+        y_at = (LANE_C + 4 * KB, AT_TAB, AT_W1, AT_W1 + 8 * KB)
         zbf_at = (LANE_E - KB, LANE_Z, LANE_G, AT_V + 2 * KB)
         gate_at = (LANE_F, LANE_A, AT_WC, AT_WC + 4 * KB)
-        step_at = (AT_PICK + 4 * KB, gate_at[0], AT_STEP + 4 * KB, LANE_H)
+        step_at = (AT_PICK + 4 * KB, gate_at[0], LANE_C, LANE_H)
         ybf_at = {
-            (0, 0): LANE_G, (0, 1): LANE_H, (1, 0): LANE_H + 2 * KB, (1, 1): LANE_G,
-            (2, 0): LANE_H, (2, 1): AT_TAB + 8 * KB, (3, 0): AT_TAB + 12 * KB, (3, 1): AT_TAB + 10 * KB,
+            (0, 0): xq_at[3], (0, 1): zbf_at[3], (1, 0): zbf_at[3] + 2 * KB, (1, 1): zbf_at[3],
+            (2, 0): zbf_at[3] + 2 * KB, (2, 1): AT_TAB + 8 * KB, (3, 0): zbf_at[3], (3, 1): AT_TAB + 10 * KB,
         }
 
         x, picked, gated, upper = {}, {}, {}, {}
@@ -268,7 +268,7 @@ def tile_list_household_profile_cells_kernel(
 
         def round_x(i):
             x_bf = placed([P, PACK * C], BF16, "x_bf%d" % i, xbf_at[i])
-            copy = nc.vector.tensor_copy if i == 1 else nc.scalar.copy
+            copy = nc.vector.tensor_copy if i in (1, 3) else nc.scalar.copy
             copy(out=woven(x_bf[:]), in_=by_lines(x[i][:]))
             x_in[i] = x_bf
 
@@ -343,7 +343,7 @@ def tile_list_household_profile_cells_kernel(
         def quantize_y(i, g):
             cols = slice(i * C, (i + 1) * C)
             if g == 0:
-                y_q[i] = kept([P, groups, C], I32, "y_q%d" % i)
+                y_q[i] = placed([P, groups, C], I32, "y_q0", LANE_G + 2 * KB - 64) if i == 0 else kept([P, groups, C], I32, "y_q%d" % i)
             codes = y_q[i][:, g, :]
             nc.vector.quantize_mx(out=codes.bitcast(FP8X4), scales=y_sc[:, g, cols], in_=y_in[i, g][:])
             if i == CHUNKS - 1:
@@ -354,6 +354,20 @@ def tile_list_household_profile_cells_kernel(
         def gate_halves(i):
             gate_step(i, nc.vector, 0, 2 * C)
             gate_step(i, nc.vector, 2 * C, PACK * C)
+
+        def finish_in_halves(i):
+            halves = [slice(lo, lo + C // 2) for lo in (0, C // 2)]
+            planes = step[i][:].rearrange("p (t n) -> p t n", t=PACK)
+            z_bf = [placed([P, PACK * C // 2], BF16, "z_bf%d_%d" % (i, h), zbf_at[i] + 2 * KB * h) for h in range(2)]
+            z[i] = kept([P, C], U32, "z%d_q" % i), kept([P, C], U8, "z%d_s" % i)
+            y[i] = placed([P, groups, PACK, C], F32, "y%d" % i, y_at[i])[:]
+            for n, rounded in zip(halves, z_bf):
+                nc.vector.tensor_tensor(
+                    out=woven(rounded[:]),
+                    in0=by_lines(planes[:, :, n]), in1=by_lines(x[i][:, :, n]), op=ALU.add,
+                )
+            for n, rounded in zip(halves, z_bf):
+                nc.vector.quantize_mx(out=z[i][0][:, n].bitcast(FP8X4), scales=z[i][1][:, n], in_=rounded[:])
 
         def project_all(i):
             for g in range(groups):
@@ -386,9 +400,9 @@ def tile_list_household_profile_cells_kernel(
         quantize_z(0)
         candidate(2)
         gating(2)
-        round_x(3)
         project_all(0)
         gate_halves(1)
+        round_x(3)
         subtract(2, (0, 1))
         quantize_x(3)
         candidate(3)
@@ -397,6 +411,7 @@ def tile_list_household_profile_cells_kernel(
         subtract(2, (2, 3))
         quantize_z(1)
         project_all(1)
+        round_y(0, 0)
         gate_halves(2)
         subtract(3, (0, 1))
         interpolate(2)
@@ -405,17 +420,20 @@ def tile_list_household_profile_cells_kernel(
         project_all(2)
         last = CHUNKS - 1
         gate_step(last, nc.vector, 0, PACK * C)
-        round_y(0, 0)
-        interpolate(last)
         quantize_y(0, 0)
-        quantize_z(last)
+        finish_in_halves(last)
         project_all(last)
-        planes = [(i, g) for i in range(CHUNKS) for g in range(groups)][1:]
-        round_y(*planes[0])
-        for done, ahead in zip(planes, planes[1:]):
-            round_y(*ahead)
-            quantize_y(*done)
-        quantize_y(*planes[-1])
+        for pair in (((0, 1), (1, 0)), ((1, 1), (2, 0))):
+            for plane in pair:
+                round_y(*plane)
+            for plane in pair:
+                quantize_y(*plane)
+        round_y(2, 1)
+        round_y(3, 0)
+        round_y(3, 1)
+        quantize_y(2, 1)
+        quantize_y(3, 0)
+        quantize_y(3, 1)
 
         for q in range(P // QUAD):
             nc.sync.dma_start(

@@ -198,7 +198,7 @@ def tile_list_household_profile_cells_kernel(
         LANE_P = LANE_A + 4 * KB
         LANE_B = LANE_P + 3 * KB
         LANE_C = LANE_B + KB
-        LANE_Z = LANE_C + 12 * KB
+        LANE_Z = LANE_C + 14 * KB
         LANE_D = LANE_Z + KB
         LANE_E = LANE_D + 4 * KB
         LANE_F = LANE_E + 3 * KB
@@ -209,10 +209,10 @@ def tile_list_household_profile_cells_kernel(
         xbf_at = (LANE_A, LANE_B, LANE_E, LANE_D)
         xq_at = (None, None, None, AT_TAB + 14 * KB)
         cand_at = ((LANE_C + KB, AT_V), (AT_H, AT_H + 2 * KB), (AT_H + 4 * KB, AT_H + 6 * KB), (AT_H + 8 * KB, AT_H + 10 * KB))
-        y_at = (LANE_C + 4 * KB, AT_TAB, AT_W1, AT_W1 + 8 * KB)
-        zbf_at = (LANE_E - KB, LANE_Z, LANE_G, AT_V + 2 * KB)
+        y_at = (LANE_C + 6 * KB, AT_TAB, AT_W1, AT_W1 + 8 * KB)
+        zbf_at = (LANE_E - KB, LANE_C, LANE_G, AT_V + 2 * KB)
         gate_at = (LANE_F, LANE_A, AT_WC, AT_WC + 4 * KB)
-        step_at = (AT_PICK + 4 * KB, gate_at[0], LANE_C, LANE_H)
+        step_at = (AT_PICK + 4 * KB, gate_at[0], LANE_C + 2 * KB, LANE_H)
         ybf_at = {
             (0, 0): xq_at[3], (0, 1): zbf_at[3], (1, 0): zbf_at[3] + 2 * KB, (1, 1): zbf_at[3],
             (2, 0): zbf_at[3] + 2 * KB, (2, 1): AT_TAB + 8 * KB, (3, 0): zbf_at[3], (3, 1): AT_TAB + 10 * KB,
@@ -388,11 +388,11 @@ def tile_list_household_profile_cells_kernel(
         subtract(0, (2, 3))
         fetch(3, 0)
         gate_step(0, nc.gpsimd, 2 * C, PACK * C)
-        gate_step(0, nc.gpsimd, C, 2 * C)
+        gate_step(0, nc.gpsimd, C // 2, 2 * C)
         candidate(1)
         round_x(2)
         gating(1)
-        gate_step(0, nc.vector, 0, C)
+        gate_step(0, nc.vector, 0, C // 2)
         subtract(1, (0, 1))
         quantize_x(2)
         interpolate(0)

@@ -26,7 +26,6 @@ LINE = 4
 C = 256
 CHUNKS = M // C
 KB = 1024
-SHARED = (3, 0)
 ROUND_ON_SCALAR = ((0, 0), (2, 1), (3, 1))
 
 
@@ -214,8 +213,8 @@ def tile_list_household_profile_cells_kernel(
         gate_at = (LANE_F, LANE_A, AT_WC, AT_WC + 4 * KB)
         step_at = (AT_PICK + 4 * KB, gate_at[0], LANE_C + 2 * KB, LANE_H)
         ybf_at = {
-            (0, 0): xq_at[3], (0, 1): zbf_at[3], (1, 0): zbf_at[3] + 2 * KB, (1, 1): zbf_at[3],
-            (2, 0): zbf_at[3] + 2 * KB, (2, 1): AT_TAB + 8 * KB, (3, 0): zbf_at[3], (3, 1): AT_TAB + 10 * KB,
+            (0, 0): xq_at[3], (0, 1): LANE_H, (1, 0): LANE_H + 2 * KB, (1, 1): AT_X + 12 * KB,
+            (2, 0): AT_X + 14 * KB, (2, 1): AT_TAB + 8 * KB, (3, 0): zbf_at[3], (3, 1): AT_TAB + 10 * KB,
         }
 
         x, picked, gated, upper = {}, {}, {}, {}
@@ -293,7 +292,7 @@ def tile_list_household_profile_cells_kernel(
         def subtract(i, slices):
             if i not in step:
                 step[i] = placed([P, PACK * C], F32, "step%d" % i, step_at[i])
-            if i in (1, 2) and slices[0] == 2:
+            if i == 1 and slices[0] == 2:
                 upper[i] = placed([P, 2 * C], F32, "upper%d" % i, xbf_at[i + 1] + KB)
             for t in slices:
                 nc.vector.scalar_tensor_tensor(
@@ -330,20 +329,13 @@ def tile_list_household_profile_cells_kernel(
 
         def round_y(i, g):
             y_in[i, g] = placed([P, PACK * C], BF16, "y_bf%d_%d" % (i, g), ybf_at[i, g])
-            if (i, g) == SHARED:
-                for copy, lo in ((nc.vector.tensor_copy, 0), (nc.scalar.copy, C // 2)):
-                    copy(
-                        out=woven(y_in[i, g][:, PACK * lo : PACK * (lo + C // 2)]),
-                        in_=by_lines(y[i][:, g, :, lo : lo + C // 2]),
-                    )
-            else:
-                copy = nc.scalar.copy if (i, g) in ROUND_ON_SCALAR else nc.vector.tensor_copy
-                copy(out=woven(y_in[i, g][:]), in_=by_lines(y[i][:, g, :, :]))
+            copy = nc.scalar.copy if (i, g) in ROUND_ON_SCALAR else nc.vector.tensor_copy
+            copy(out=woven(y_in[i, g][:]), in_=by_lines(y[i][:, g, :, :]))
 
         def quantize_y(i, g):
             cols = slice(i * C, (i + 1) * C)
             if g == 0:
-                y_q[i] = placed([P, groups, C], I32, "y_q0", LANE_G + 2 * KB - 64) if i == 0 else kept([P, groups, C], I32, "y_q%d" % i)
+                y_q[i] = placed([P, groups, C], I32, "y_q0", gate_at[3]) if i == 0 else kept([P, groups, C], I32, "y_q%d" % i)
             codes = y_q[i][:, g, :]
             nc.vector.quantize_mx(out=codes.bitcast(FP8X4), scales=y_sc[:, g, cols], in_=y_in[i, g][:])
             if i == CHUNKS - 1:
@@ -358,16 +350,15 @@ def tile_list_household_profile_cells_kernel(
         def finish_in_halves(i):
             halves = [slice(lo, lo + C // 2) for lo in (0, C // 2)]
             planes = step[i][:].rearrange("p (t n) -> p t n", t=PACK)
-            z_bf = [placed([P, PACK * C // 2], BF16, "z_bf%d_%d" % (i, h), zbf_at[i] + 2 * KB * h) for h in range(2)]
-            z[i] = kept([P, C], U32, "z%d_q" % i), kept([P, C], U8, "z%d_s" % i)
-            y[i] = placed([P, groups, PACK, C], F32, "y%d" % i, y_at[i])[:]
-            for n, rounded in zip(halves, z_bf):
+            gates = gate[i][:].rearrange("p (t n) -> p t n", t=PACK)
+            z_in[i] = placed([P, PACK * C], BF16, "z_bf%d" % i, zbf_at[i])
+            for n in halves:
+                nc.vector.tensor_tensor(out=planes[:, :, n], in0=planes[:, :, n], in1=gates[:, :, n], op=ALU.mult)
+            for n in halves:
                 nc.vector.tensor_tensor(
-                    out=woven(rounded[:]),
+                    out=woven(z_in[i][:, PACK * n.start : PACK * n.stop]),
                     in0=by_lines(planes[:, :, n]), in1=by_lines(x[i][:, :, n]), op=ALU.add,
                 )
-            for n, rounded in zip(halves, z_bf):
-                nc.vector.quantize_mx(out=z[i][0][:, n].bitcast(FP8X4), scales=z[i][1][:, n], in_=rounded[:])
 
         def project_all(i):
             for g in range(groups):
@@ -382,17 +373,17 @@ def tile_list_household_profile_cells_kernel(
         fetch(2, 1)
         candidate(0, (1, 0))
         round_x(1)
-        gating(0, (1, 0))
+        gating(0)
         subtract(0, (0, 1))
         quantize_x(1)
-        subtract(0, (2, 3))
+        subtract(0, (2,))
+        gate_step(0, nc.vector, 0, C // 2)
+        subtract(0, (3,))
         fetch(3, 0)
-        gate_step(0, nc.gpsimd, 2 * C, PACK * C)
-        gate_step(0, nc.gpsimd, C // 2, 2 * C)
+        gate_step(0, nc.gpsimd, C // 2, PACK * C)
         candidate(1)
         round_x(2)
         gating(1)
-        gate_step(0, nc.vector, 0, C // 2)
         subtract(1, (0, 1))
         quantize_x(2)
         interpolate(0)
@@ -412,30 +403,28 @@ def tile_list_household_profile_cells_kernel(
         quantize_z(1)
         project_all(1)
         round_y(0, 0)
-        gate_halves(2)
+        gate_step(2, nc.vector, 0, PACK * C)
         subtract(3, (0, 1))
         interpolate(2)
         subtract(3, (2, 3))
         quantize_z(2)
         project_all(2)
         last = CHUNKS - 1
-        gate_step(last, nc.vector, 0, PACK * C)
-        quantize_y(0, 0)
         finish_in_halves(last)
+        quantize_y(0, 0)
+        quantize_z(last)
         project_all(last)
-        for pair in (((0, 1), (1, 0)), ((1, 1), (2, 0))):
-            for plane in pair:
-                round_y(*plane)
-            for plane in pair:
-                quantize_y(*plane)
         round_y(2, 1)
-        round_y(3, 0)
+        planes = [(0, 1), (1, 0), (1, 1), (2, 0), (3, 0)]
+        round_y(*planes[0])
+        for done, ahead in zip(planes, planes[1:]):
+            round_y(*ahead)
+            quantize_y(*done)
         round_y(3, 1)
-        quantize_y(2, 1)
-        quantize_y(3, 0)
-        quantize_y(3, 1)
+        for plane in ((2, 1), (3, 0), (3, 1)):
+            quantize_y(*plane)
 
-        for q in range(P // QUAD):
+        for q in (0, 2, 1, 3):
             nc.sync.dma_start(
                 out=out_2[:, 4 * q : 4 * q + 4, :].rearrange("g r m -> r g m").bitcast(I32),
                 in_=y_sc[QUAD * q : QUAD * q + 4, :, :].bitcast(I32),

@@ -322,7 +322,7 @@ def tile_list_household_profile_cells_kernel(
         def project(i, g):
             for b, acc in enumerate(product("y", 4, range(g * PACK, (g + 1) * PACK), out_lhs, z[i])):
                 nc.scalar.copy(out=y[i][:, g, 2 * b : 2 * b + 2, :].rearrange("p t n -> p (t n)"), in_=acc[:])
-            pieces = 2 if i == CHUNKS - 1 else 1
+            pieces = 1 if i == 0 else 2
             for lo in range(0, PACK, PACK // pieces):
                 ts = slice(lo, lo + PACK // pieces)
                 nc.sync.dma_start(out=y_rows[g][:, ts, i * C : (i + 1) * C], in_=y[i][:, g, ts, :])

@@ -122,7 +122,13 @@ def tile_list_household_profile_cells_kernel(
         gain_sb = kept([P, PACK], F32, "gain_sb")
         nc.sync.dma_start(out=gain_sb[:], in_=gain.rearrange("(p t) -> p t", t=PACK))
         load_scales(w_sc_raw, wo_scales[0].rearrange("r (g e) -> g r e", g=groups), first=4)
-        wo_raw = load_words(wo_words[0], "wo_raw", AT_WO)
+        AT_X = AT_FREE
+        AT_PICK = AT_X + 16 * KB
+        LANE_A = AT_PICK + 9 * KB
+        AT_LATE = 166 * KB
+        wo_raw = [
+            load_words(wo_words[0][:, g * KP : (g + 1) * KP, :], "wo_raw%d" % g, at) for g, at in enumerate((LANE_A, AT_LATE))
+        ]
 
         def quantize(values, name, at=None):
             width = values.shape[1] // PACK
@@ -186,14 +192,20 @@ def tile_list_household_profile_cells_kernel(
 
         wg_q = kept([P, H], U16, "wg_q")
         deal(wg_raw[:], wg_q[:], nc.scalar.copy)
-        wo_q = kept([P, N], U32, "wo_q")
-        deal(wo_raw[:].bitcast(U32), wo_q[:], nc.scalar.copy)
+        wo_q = {}
+
+        def deal_wo(g, half, at=None):
+            name = "wo_q%d%d" % (g, half)
+            lo, hi = ((0, PACK - 1), (PACK - 1, PACK))[half]
+            wo_q[g, half] = kept([P, hi - lo, P], U32, name) if at is None else placed([P, hi - lo, P], U32, name, at)
+            columns = wo_raw[g][:].bitcast(U32).rearrange("p (m t) -> p t m", t=PACK)
+            nc.scalar.copy(out=wo_q[g, half][:], in_=columns[:, lo:hi, :])
+
+        for g in range(groups):
+            deal_wo(g, 0)
         w_s = placed([P, KP], U8, "w_s", AT_WGS)
         deal(w_sc_raw[:], w_s[:], nc.gpsimd.tensor_copy)
 
-        AT_X = AT_FREE
-        AT_PICK = AT_X + 16 * KB
-        LANE_A = AT_PICK + 9 * KB
         LANE_P = LANE_A + 4 * KB
         LANE_B = LANE_P + 3 * KB
         LANE_C = LANE_B + KB
@@ -204,12 +216,12 @@ def tile_list_household_profile_cells_kernel(
         LANE_G = LANE_F + 4 * KB
         LANE_H = LANE_G + 5 * KB
         AT_STEP = LANE_H + 4 * KB
-        pick_at = (((0, 4, AT_PICK),), ((0, 4, AT_PICK + 4 * KB),), ((0, 1, AT_PICK + 8 * KB), (1, 4, LANE_A)), ((0, 4, LANE_C),))
-        xbf_at = (LANE_A, LANE_B, LANE_E, LANE_D)
+        pick_at = (((0, 4, AT_PICK),), ((0, 4, AT_PICK + 4 * KB),), ((0, 1, AT_LATE + 3 * KB), (1, 4, LANE_A - 64)), ((0, 4, LANE_C),))
+        xbf_at = (AT_LATE + 4 * KB, LANE_B, LANE_E, LANE_D)
         xq_at = (None, None, None, AT_TAB + 14 * KB)
         cand_at = ((LANE_C + KB, AT_V), (AT_H, AT_H + 2 * KB), (AT_H + 4 * KB, AT_H + 6 * KB), (AT_H + 8 * KB, AT_H + 10 * KB))
         y_at = (LANE_C + 6 * KB, AT_TAB, AT_W1, AT_W1 + 8 * KB)
-        zbf_at = (LANE_E - KB, LANE_C, LANE_G, AT_V + 2 * KB)
+        zbf_at = (AT_LATE + KB, LANE_C, LANE_G, AT_V + 2 * KB)
         gate_at = (LANE_F, LANE_A, AT_WC, AT_WC + 4 * KB)
         step_at = (AT_PICK + 4 * KB, gate_at[0], LANE_C + 2 * KB, LANE_H)
         ybf_at = {
@@ -255,7 +267,7 @@ def tile_list_household_profile_cells_kernel(
 
         def out_lhs(s):
             g, t = divmod(s, PACK)
-            return wo_q[:, s * P : (s + 1) * P].bitcast(FP8X4), w_s[4 + 4 * g : P, t * P : (t + 1) * P]
+            return wo_q[g, t // (PACK - 1)][:, t % (PACK - 1), :].bitcast(FP8X4), w_s[4 + 4 * g : P, t * P : (t + 1) * P]
 
         def woven(values):
             return values.rearrange("p (n i t) -> p n t i", i=LINE, t=PACK)
@@ -369,6 +381,7 @@ def tile_list_household_profile_cells_kernel(
         wc_q, wc_s = quantize(wc_bf[:], "wc")
         fetch(2, 0)
         round_x(0)
+        deal_wo(0, 1, AT_PICK)
         quantize_x(0)
         fetch(2, 1)
         candidate(0, (1, 0))
@@ -383,6 +396,7 @@ def tile_list_household_profile_cells_kernel(
         gate_step(0, nc.gpsimd, C // 2, PACK * C)
         candidate(1)
         round_x(2)
+        deal_wo(1, 1, LANE_A - KB // 2)
         gating(1)
         subtract(1, (0, 1))
         quantize_x(2)

from contextlib import ExitStack

import concourse.mybir as mybir

K, H, N, T, S, T2, M = 1024, 512, 1024, 2048, 1024, 2048, 1024
FLOPS = 2 * (K * H * S + 2 * H * H * M + H * N * M)

F32 = mybir.dt.float32
BF16 = mybir.dt.bfloat16
I32 = mybir.dt.int32
U32 = mybir.dt.uint32
U16 = mybir.dt.uint16
U8 = mybir.dt.uint8
FP8X4 = mybir.dt.float8_e4m3fn_x4
FP4X4 = mybir.dt.float4_e2m1fn_x4
ALU = mybir.AluOpType
ACT = mybir.ActivationFunctionType

P = 128
PACK = 4
KP = P * PACK
QUAD = 32
BANK = 512
LIST = 16
LINE = 4
C = 256
CHUNKS = M // C
KB = 1024
ROUND_ON_SCALAR = ((0, 0), (2, 1), (3, 1))


def tile_list_household_profile_cells_kernel(
    tc, tab_words, tab_scales, offs, w1, page0, wgs, offs2, offs3,
    wg_words, wg_scales, wc, gain, wo_words, wo_scales, out_0, out_1, out_2,
):
    nc = tc.nc
    passes = K // KP
    groups = N // KP
    blocks = H // P

    with ExitStack() as ctx:
        keep = ctx.enter_context(tc.tile_pool(name="keep", bufs=1))
        arena = ctx.enter_context(tc.tile_pool(name="arena", bufs=1))
        psum = ctx.enter_context(tc.psum_pool(name="psum", bufs=2))

        def kept(shape, dtype, name):
            return keep.tile(shape, dtype, name=name, align_bytes=64)

        def placed(shape, dtype, name, offset):
            return arena.tile(shape, dtype, name=name, offset=offset, align_bytes=64)

        def entries(offsets, lo, hi):
            return offsets[:, lo // LIST : hi // LIST]

        idx = keep.tile([P, S // LIST], U16, name="idx")
        idx2 = keep.tile([P, S // LIST], U16, name="idx2")
        idx3 = keep.tile([P, M // LIST], U16, name="idx3")

        def zeroed_plane(width, name):
            plane = kept([P, width], U8, name)
            nc.vector.memset(plane[:].bitcast(I32), 0)
            return plane

        def load_scales(plane, scales, first=0):
            rows = 4 * scales.shape[0]
            for q in range(P // QUAD):
                nc.sync.dma_start(
                    out=plane[QUAD * q + first : QUAD * q + first + rows, :].bitcast(I32),
                    in_=scales[:, 4 * q : 4 * q + 4, :].bitcast(I32),
                )

        tab_sc = zeroed_plane(T, "tab_sc")
        w_sc_raw = zeroed_plane(KP, "w_sc_raw")
        warm_in = kept([P, 1], F32, "warm_in")
        warm_out = kept([P, 1], F32, "warm_out")
        nc.vector.memset(warm_in[:], 0.0)
        nc.scalar.activation(out=warm_out[:], in_=warm_in[:], func=ACT.Sigmoid)

        AT_TAB, AT_W1, AT_V, AT_H, AT_WC, AT_WO, AT_WG, AT_W1BF = 0, 16 * KB, 32 * KB, 40 * KB, 56 * KB, 64 * KB, 68 * KB, 70 * KB
        AT_WCBF, AT_WGS, AT_FREE = 78 * KB, 82 * KB, 86 * KB

        w1_raw = []

        def load_w1(b):
            raw = placed([P, passes, PACK, P], F32, "w1_raw%d" % b, AT_W1 + 4 * KB * b)
            for a in range(passes):
                rows = w1[a * KP : (a + 1) * KP, b * P : (b + 1) * P]
                nc.sync.dma_start(out=raw[:, a, :, :], in_=rows.rearrange("(p j) c -> p j c", j=PACK))
            w1_raw.append(raw)

        def load_words(words, name, offset):
            tile = placed([P, words.shape[1]], I32, name, offset)
            nc.sync.dma_start(out=tile[:], in_=words.rearrange("p c i -> p (c i)").bitcast(I32))
            return tile

        def load_page(b):
            tile = kept([P, T2], F32, "page%d" % b)
            nc.sync.dma_start(out=tile[:], in_=page0[b * P : (b + 1) * P, :])
            return tile

        nc.sync.dma_start(idx[:], offs)
        load_scales(tab_sc, tab_scales)
        load_w1(0)
        tab_w = [load_words(tab_words[a], "tab_w%d" % a, AT_TAB + 4 * T * a) for a in range(passes)]
        nc.sync.dma_start(idx2[:], offs2)
        wgs_sb = placed([P, S], F32, "wgs", AT_WGS)
        nc.sync.dma_start(out=wgs_sb[:, 0:BANK], in_=wgs[:, 0:BANK])
        page = [load_page(0)]
        load_w1(1)
        load_w1(2)
        nc.sync.dma_start(out=wgs_sb[:, BANK:S], in_=wgs[:, BANK:S])
        page.append(load_page(1))
        load_w1(3)
        page.append(load_page(2))
        page.append(load_page(3))
        nc.sync.dma_start(idx3[:], offs3)
        wc_raw = placed([P, PACK, H], F32, "wc_raw", AT_WC)
        nc.sync.dma_start(out=wc_raw[:], in_=wc.rearrange("(p j) c -> p j c", j=PACK))
        wg_raw = placed([P, H], U16, "wg_raw", AT_WG)
        nc.sync.dma_start(out=wg_raw[:].bitcast(I32), in_=wg_words[0].bitcast(I32))
        load_scales(w_sc_raw, wg_scales)
        gain_sb = kept([P, PACK], F32, "gain_sb")
        nc.sync.dma_start(out=gain_sb[:], in_=gain.rearrange("(p t) -> p t", t=PACK))
        load_scales(w_sc_raw, wo_scales[0].rearrange("r (g e) -> g r e", g=groups), first=4)
        AT_X = AT_FREE
        AT_PICK = AT_X + 16 * KB
        LANE_A = AT_PICK + 9 * KB
        AT_LATE = 166 * KB
        wo_raw = [
            load_words(wo_words[0][:, g * KP : (g + 1) * KP, :], "wo_raw%d" % g, at) for g, at in enumerate((LANE_A, AT_LATE))
        ]

        def quantize(values, name, at=None):
            width = values.shape[1] // PACK
            codes = kept([P, width], U32, name + "_q") if at is None else placed([P, width], U32, name + "_q", at)
            scales = kept([P, width], U8, name + "_s")
            nc.vector.quantize_mx(out=codes[:].bitcast(FP8X4), scales=scales[:], in_=values)
            return codes, scales

        def quantize_w1(b):
            values = placed([P, passes * P * PACK], BF16, "w1_bf%d" % b, AT_W1BF + 2 * KB * (b % 2))
            nc.scalar.copy(
                out=values[:].rearrange("p (a n i j) -> p a n j i", a=passes, i=LINE, j=PACK),
                in_=w1_raw[b][:].rearrange("p a j (n i) -> p a n j i", i=LINE),
            )
            return quantize(values[:], "w1_%d" % b)

        v_sc = kept([P, S], U8, "v_sc")
        nc.vector.tensor_copy(out=v_sc[:], in_=tab_sc[:].indirect(idx[:]))
        v_w = {}
        for lo in range(0, S, BANK):
            for a in range(passes):
                v_w[a, lo] = placed([P, BANK], U32, "v_w%d_%d" % (a, lo), AT_V + 4 * (passes * lo + BANK * a))
                nc.vector.tensor_copy(out=v_w[a, lo][:], in_=tab_w[a][:].bitcast(U32).indirect(entries(idx, lo, lo + BANK)))

        h_count = []
        for b in range(blocks):
            w1_q, w1_s = quantize_w1(b)
            cuts = ((0, BANK), (BANK, S)) if b == 0 else ((0, S),)
            for lo, hi in cuts:
                slot = 3 if b == blocks - 1 else len(h_count) % 3
                h = placed([P, hi - lo], F32, "h%d" % len(h_count), AT_H + 4 * KB * slot)
                h_count.append(h)
                for first in range(lo, hi, BANK):
                    acc = psum.tile([P, BANK], F32, name="acc_h", tag="y", bufs=4)
                    for a in range(passes):
                        nc.tensor.matmul_mx(
                            out=acc[:],
                            lhsT=w1_q[:, a * P : (a + 1) * P].bitcast(FP8X4),
                            lhsT_scale=w1_s[:, a * P : (a + 1) * P],
                            rhs=v_w[a, first][:].bitcast(FP8X4),
                            rhs_scale=v_sc[4 * a : P, first : first + BANK],
                            start=(a == 0),
                            stop=(a == passes - 1),
                        )
                    nc.scalar.copy(out=h[:, first - lo : first - lo + BANK], in_=acc[:])
                nc.vector.tensor_tensor(
                    out=page[b][:].indirect(entries(idx2, lo, hi)), in0=h[:], in1=wgs_sb[:, lo:hi], op=ALU.mult
                )

        wc_bf = placed([P, PACK * H], BF16, "wc_bf", AT_WCBF)
        nc.scalar.copy(
            out=wc_bf[:].rearrange("p (t m j) -> p m j t", t=PACK, j=PACK),
            in_=wc_raw[:].rearrange("p j (m t) -> p m j t", t=PACK),
        )

        def deal(raw, dealt, copy):
            copy(
                out=dealt.rearrange("p (g t m) -> p g t m", t=PACK, m=P),
                in_=raw.rearrange("p (g m t) -> p g t m", t=PACK, m=P),
            )

        wg_q = kept([P, H], U16, "wg_q")
        deal(wg_raw[:], wg_q[:], nc.scalar.copy)
        wo_q = {}

        def deal_wo(g, half, at=None):
            name = "wo_q%d%d" % (g, half)
            lo, hi = ((0, PACK - 1), (PACK - 1, PACK))[half]
            wo_q[g, half] = kept([P, hi - lo, P], U32, name) if at is None else placed([P, hi - lo, P], U32, name, at)
            columns = wo_raw[g][:].bitcast(U32).rearrange("p (m t) -> p t m", t=PACK)
            nc.scalar.copy(out=wo_q[g, half][:], in_=columns[:, lo:hi, :])

        for g in range(groups):
            deal_wo(g, 0)
        w_s = placed([P, KP], U8, "w_s", AT_WGS)
        deal(w_sc_raw[:], w_s[:], nc.gpsimd.tensor_copy)

        LANE_P = LANE_A + 4 * KB
        LANE_B = LANE_P + 3 * KB
        LANE_C = LANE_B + KB
        LANE_Z = LANE_C + 14 * KB
        LANE_D = LANE_Z + KB
        LANE_E = LANE_D + 4 * KB
        LANE_F = LANE_E + 3 * KB
        LANE_G = LANE_F + 4 * KB
        LANE_H = LANE_G + 5 * KB
        AT_STEP = LANE_H + 4 * KB
        pick_at = (((0, 4, AT_PICK),), ((0, 4, AT_PICK + 4 * KB),), ((0, 1, AT_LATE + 3 * KB), (1, 4, LANE_A - 64)), ((0, 4, LANE_C),))
        xbf_at = (AT_LATE + 4 * KB, LANE_B, LANE_E, LANE_D)
        xq_at = (None, None, None, AT_TAB + 14 * KB)
        cand_at = ((LANE_C + KB, AT_V), (AT_H, AT_H + 2 * KB), (AT_H + 4 * KB, AT_H + 6 * KB), (AT_H + 8 * KB, AT_H + 10 * KB))
        y_at = (LANE_C + 6 * KB, AT_TAB, AT_W1, AT_W1 + 8 * KB)
        zbf_at = (AT_LATE + KB, LANE_C, LANE_G, AT_V + 2 * KB)
        gate_at = (LANE_F, LANE_A, AT_WC, AT_WC + 4 * KB)
        step_at = (AT_PICK + 4 * KB, gate_at[0], LANE_C + 2 * KB, LANE_H)
        ybf_at = {
            (0, 0): xq_at[3], (0, 1): LANE_H, (1, 0): LANE_H + 2 * KB, (1, 1): AT_X + 12 * KB,
            (2, 0): AT_X + 14 * KB, (2, 1): AT_TAB + 8 * KB, (3, 0): zbf_at[3], (3, 1): AT_TAB + 10 * KB,
        }

        x, picked, gated, upper = {}, {}, {}, {}

        def fetch(i, part):
            lo, hi, at = pick_at[i][part]
            picked[i] = placed([P, hi - lo, C], F32, "picked%d_%d" % (i, part), at)
            if lo == 0:
                x[i] = placed([P, PACK, C], F32, "x%d" % i, AT_X + 4 * KB * i)
            for b in range(lo, hi):
                nc.vector.tensor_copy(out=picked[i][:, b - lo, :], in_=page[b][:].indirect(entries(idx3, i * C, (i + 1) * C)))
                nc.sync.dma_start(out=x[i][QUAD * b : QUAD * (b + 1), :, :], in_=picked[i][:, b - lo, :])

        y_sc = kept([P, groups, M], U8, "y_sc")
        y_rows = out_0.rearrange("(g p t) m -> g p t m", p=P, t=PACK)
        y_words = out_1.rearrange("g p m t -> p g (m t)").bitcast(I32)

        def product(tag, bufs, slices, lhs, rhs):
            codes, scales = rhs
            per_bank = BANK // C
            banks = []
            for first in range(0, len(slices), per_bank):
                acc = psum.tile([P, BANK], F32, name="acc_" + tag, tag=tag, bufs=bufs)
                for s in range(per_bank):
                    lhs_codes, lhs_scales = lhs(slices[first + s])
                    nc.tensor.matmul_mx(
                        out=acc[:, s * C : (s + 1) * C], lhsT=lhs_codes, lhsT_scale=lhs_scales,
                        rhs=codes[:].bitcast(FP8X4), rhs_scale=scales[:], start=True, stop=True,
                    )
                banks.append(acc)
            return banks

        def gate_lhs(t):
            return wg_q[:, t * P : (t + 1) * P].bitcast(FP4X4), w_s[:, t * P : (t + 1) * P]

        def cand_lhs(t):
            return wc_q[:, t * P : (t + 1) * P].bitcast(FP8X4), wc_s[:, t * P : (t + 1) * P]

        def out_lhs(s):
            g, t = divmod(s, PACK)
            return wo_q[g, t // (PACK - 1)][:, t % (PACK - 1), :].bitcast(FP8X4), w_s[4 + 4 * g : P, t * P : (t + 1) * P]

        def woven(values):
            return values.rearrange("p (n i t) -> p n t i", i=LINE, t=PACK)

        def by_lines(planes):
            return planes.rearrange("p t (n i) -> p n t i", i=LINE)

        cand, gate, step, x_mx, z_in, z, y, y_in, y_q, x_in = {}, {}, {}, {}, {}, {}, {}, {}, {}, {}

        def round_x(i):
            x_bf = placed([P, PACK * C], BF16, "x_bf%d" % i, xbf_at[i])
            copy = nc.vector.tensor_copy if i in (1, 3) else nc.scalar.copy
            copy(out=woven(x_bf[:]), in_=by_lines(x[i][:]))
            x_in[i] = x_bf

        def quantize_x(i):
            x_mx[i] = quantize(x_in[i][:], "x%d" % i, at=xq_at[i])

        def candidate(i, halves=(0, 1)):
            cand[i] = {}
            tag, depth = ("y", 4) if i == CHUNKS - 1 else ("c", 2)
            slices = [2 * b + s for b in halves for s in range(2)]
            for b, acc in zip(halves, product(tag, depth, slices, cand_lhs, x_mx[i])):
                cand[i][b] = placed([P, BANK], F32, "cand%d_%d" % (i, b), cand_at[i][b])
                nc.scalar.activation(out=cand[i][b][:], in_=acc[:], func=ACT.Tanh)

        def gating(i, halves=(0, 1)):
            gate[i] = placed([P, PACK * C], F32, "gate%d" % i, gate_at[i])
            tag, depth = ("y", 4) if i == CHUNKS - 1 else ("g", 2)
            slices = [2 * b + s for b in halves for s in range(2)]
            for b, acc in zip(halves, product(tag, depth, slices, gate_lhs, x_mx[i])):
                nc.scalar.activation(out=gate[i][:, b * BANK : (b + 1) * BANK], in_=acc[:], func=ACT.Sigmoid)

        def subtract(i, slices):
            if i not in step:
                step[i] = placed([P, PACK * C], F32, "step%d" % i, step_at[i])
            if i == 1 and slices[0] == 2:
                upper[i] = placed([P, 2 * C], F32, "upper%d" % i, xbf_at[i + 1] + KB)
            for t in slices:
                nc.vector.scalar_tensor_tensor(
                    out=upper[i][:, (t - 2) * C : (t - 1) * C] if i in upper else step[i][:, t * C : (t + 1) * C], in0=cand[i][t // 2][:, (t % 2) * C : (t % 2 + 1) * C],
                    scalar=gain_sb[:, t : t + 1], in1=x[i][:, t, :], op0=ALU.mult, op1=ALU.subtract,
                )

        def gate_step(i, engine, lo, hi):
            if i not in gated:
                gated[i] = placed([P, PACK * C], F32, "gated0", LANE_P) if i == 0 else step[i]
            engine.tensor_tensor(out=gated[i][:, lo:hi], in0=upper[i][:] if i in upper and lo > 0 else step[i][:, lo:hi], in1=gate[i][:, lo:hi], op=ALU.mult)

        def interpolate(i):
            z_bf = placed([P, PACK * C], BF16, "z_bf%d" % i, zbf_at[i])
            nc.vector.tensor_tensor(
                out=woven(z_bf[:]),
                in0=by_lines(gated[i][:].rearrange("p (t n) -> p t n", t=PACK)),
                in1=by_lines(x[i][:]),
                op=ALU.add,
            )
            z_in[i] = z_bf

        def quantize_z(i):
            z[i] = quantize(z_in[i][:], "z%d" % i)
            y[i] = placed([P, groups, PACK, C], F32, "y%d" % i, y_at[i])[:]

        def project(i, g):
            for b, acc in enumerate(product("y", 4, range(g * PACK, (g + 1) * PACK), out_lhs, z[i])):
                nc.scalar.copy(out=y[i][:, g, 2 * b : 2 * b + 2, :].rearrange("p t n -> p (t n)"), in_=acc[:])
            pieces = 1 if i == 0 else 2
            for lo in range(0, PACK, PACK // pieces):
                ts = slice(lo, lo + PACK // pieces)
                nc.sync.dma_start(out=y_rows[g][:, ts, i * C : (i + 1) * C], in_=y[i][:, g, ts, :])

        def round_y(i, g):
            y_in[i, g] = placed([P, PACK * C], BF16, "y_bf%d_%d" % (i, g), ybf_at[i, g])
            copy = nc.scalar.copy if (i, g) in ROUND_ON_SCALAR else nc.vector.tensor_copy
            copy(out=woven(y_in[i, g][:]), in_=by_lines(y[i][:, g, :, :]))

        def quantize_y(i, g):
            cols = slice(i * C, (i + 1) * C)
            if g == 0:
                y_q[i] = placed([P, groups, C], I32, "y_q0", gate_at[3]) if i == 0 else kept([P, groups, C], I32, "y_q%d" % i)
            codes = y_q[i][:, g, :]
            nc.vector.quantize_mx(out=codes.bitcast(FP8X4), scales=y_sc[:, g, cols], in_=y_in[i, g][:])
            if i == CHUNKS - 1:
                nc.sync.dma_start(out=y_words[:, g, cols], in_=codes)
            elif g == groups - 1:
                nc.sync.dma_start(out=y_words[:, :, cols], in_=y_q[i][:])

        def gate_halves(i):
            gate_step(i, nc.vector, 0, 2 * C)
            gate_step(i, nc.vector, 2 * C, PACK * C)

        def finish_in_halves(i):
            halves = [slice(lo, lo + C // 2) for lo in (0, C // 2)]
            planes = step[i][:].rearrange("p (t n) -> p t n", t=PACK)
            gates = gate[i][:].rearrange("p (t n) -> p t n", t=PACK)
            z_in[i] = placed([P, PACK * C], BF16, "z_bf%d" % i, zbf_at[i])
            for n in halves:
                nc.vector.tensor_tensor(out=planes[:, :, n], in0=planes[:, :, n], in1=gates[:, :, n], op=ALU.mult)
            for n in halves:
                nc.vector.tensor_tensor(
                    out=woven(z_in[i][:, PACK * n.start : PACK * n.stop]),
                    in0=by_lines(planes[:, :, n]), in1=by_lines(x[i][:, :, n]), op=ALU.add,
                )

        def project_all(i):
            for g in range(groups):
                project(i, g)

        fetch(0, 0)
        fetch(1, 0)
        wc_q, wc_s = quantize(wc_bf[:], "wc")
        fetch(2, 0)
        round_x(0)
        deal_wo(0, 1, AT_PICK)
        quantize_x(0)
        fetch(2, 1)
        candidate(0, (1, 0))
        round_x(1)
        gating(0)
        subtract(0, (0, 1))
        quantize_x(1)
        subtract(0, (2,))
        gate_step(0, nc.vector, 0, C // 2)
        subtract(0, (3,))
        fetch(3, 0)
        gate_step(0, nc.gpsimd, C // 2, PACK * C)
        candidate(1)
        round_x(2)
        deal_wo(1, 1, LANE_A - KB // 2)
        gating(1)
        subtract(1, (0, 1))
        quantize_x(2)
        interpolate(0)
        subtract(1, (2, 3))
        quantize_z(0)
        candidate(2)
        gating(2)
        project_all(0)
        gate_halves(1)
        round_x(3)
        subtract(2, (0, 1))
        quantize_x(3)
        candidate(3)
        gating(3)
        interpolate(1)
        subtract(2, (2, 3))
        quantize_z(1)
        project_all(1)
        round_y(0, 0)
        gate_step(2, nc.vector, 0, PACK * C)
        subtract(3, (0, 1))
        interpolate(2)
        subtract(3, (2, 3))
        quantize_z(2)
        project_all(2)
        last = CHUNKS - 1
        finish_in_halves(last)
        quantize_y(0, 0)
        quantize_z(last)
        project_all(last)
        round_y(2, 1)
        planes = [(0, 1), (1, 0), (1, 1), (2, 0), (3, 0)]
        round_y(*planes[0])
        for done, ahead in zip(planes, planes[1:]):
            round_y(*ahead)
            quantize_y(*done)
        round_y(3, 1)
        for plane in ((2, 1), (3, 0), (3, 1)):
            quantize_y(*plane)

        for q in (0, 2, 1, 3):
            nc.sync.dma_start(
                out=out_2[:, 4 * q : 4 * q + 4, :].rearrange("g r m -> r g m").bitcast(I32),
                in_=y_sc[QUAD * q : QUAD * q + 4, :, :].bitcast(I32),
            )
